import numpy as np, ml_dtypes
CORES = [35,38,43,46]
N = 4
BF = ml_dtypes.bfloat16
S, L, RO, WEAR = 4096, 256, 3, 8
def near(rng, home, h):
    q = S // 16
    return np.take_along_axis(np.broadcast_to(home, (N, 8, S)), h * q + rng.integers(0, q, h.shape), 2)
def parts(rng):
    home = np.argsort(rng.random((8, S)), axis=1); hab = np.zeros((8, S), np.int64)
    np.put_along_axis(hab, home, np.broadcast_to(np.arange(S) // (S // 16), (8, S)), 1)
    base = rng.integers(0, 256, (N, 8, 16, 16))
    x = np.clip(np.take_along_axis(base, hab[None, :, None, :], 3) + rng.integers(-60, 61, (N, 8, 16, S)), 0, 255)
    lab = np.argsort(rng.random((N, 8, L)), axis=2); inv = np.argsort(lab, axis=2)
    h = np.broadcast_to((lab % 16)[:, :, None, :], (N, 8, 16, L)).reshape(N, 8, 16 * L)
    m = np.where(rng.random(h.shape) < 0.75, near(rng, home, h), rng.integers(0, S, h.shape)).reshape(N, 8, 16, L)
    h = np.broadcast_to(hab[None, :, None, :], (N, 8, 16, S)).reshape(N, 8, 16 * S)
    nb = np.where(rng.random(h.shape) < 0.6, near(rng, home, h), rng.integers(0, S, h.shape)).reshape(N, 8, 16, S)
    v = hab[None] + 16 * rng.integers(0, L // 16, (N, 8, S))
    own = np.where(rng.random((N, 8, S)) < 0.6, np.take_along_axis(inv, v, 2), rng.integers(0, L, (N, 8, S)))
    return x, nb, m, own, rng.integers(600, 1100, (N, 8))
def pack(x, nb, m, own, th):
    return {"x0": x.reshape(N, 128, S).astype(np.float32).astype(BF), "nb": nb.reshape(N, 128, S).astype(np.int32), "m0": m.reshape(N, 128, L).astype(np.int32),
            "own0": own.reshape(N, 8, S).astype(np.int32), "th": th.reshape(N, 8, 1).astype(np.int32)}
def setup_inputs(rng):
    return pack(*parts(rng))
def setup_inputs_ties(rng):
    x, nb, m, own, th = parts(rng); step = rng.choice(np.array([1, 5, 40]), (N, 8, 1, 1))
    lo = ((256 - 3 * step) * rng.random((N, 8, 1, 1)) * (rng.random((N, 8, 1, 1)) < 0.7)).astype(np.int64)
    x = lo + step * rng.integers(0, 4, x.shape)
    pool = rng.integers(0, S, (N, 8, 3, L)); few = np.take_along_axis(pool, rng.integers(0, 3, m.shape), 2)
    m = np.where(rng.random((N, 8, 1, L)) < 0.7, few, rng.integers(0, S, m.shape))
    th = step[:, :, 0, 0] * rng.integers(14, 19, (N, 8))
    z = int(rng.integers(0, 8)); o = rng.permutation(S); cold, warm = o[:S // 2], o[S // 2:]; h = rng.integers(140, 250, N)
    is_cold = np.zeros(S, bool); is_cold[cold] = True
    x[:, z] = np.where(is_cold, 0, h[:, None, None]) + rng.integers(0, 2, (N, 16, S))
    three = cold[rng.integers(0, S // 2, (N, 3, L))]; m[:, z] = np.take_along_axis(three, rng.integers(0, 3, (N, 16, L)), 1)
    nb[:, z] = warm[rng.integers(0, S - S // 2, (N, 16, S))]; th[:, z] = 16 * h + rng.integers(3, 9, N)
    return pack(x, nb, m, own, th)
def setup_inputs_corners(rng):
    x, nb, m, own, th = parts(rng); K = S // L; ev = (K + 1) // 2; od = K // 2
    q = int(rng.integers(0, N)); p = (q - 1) % N; u = (q - 2) % N; la = np.arange(L); st = np.arange(S)
    turn = [rng.permutation(8) for r in range(N)]; turn[u] = turn[p]
    for r in range(N):
        for i, g in enumerate(turn[r]):
            if i == 0: own[r, g] = int(rng.choice(np.array([0, L - 1, L // 2])))
            if i == 1:
                own[r, g] = rng.permutation(L)[st % L]; m[r, g] = la + L * rng.integers(0, K, (16, L))
            if i == 2: m[r, g] = rng.choice(np.array([0, S - 1, int(rng.integers(0, S))]), (1, L))
            if i == 3: nb[r, g] = st[None, :]
            if i == 4: nb[r, g] = (S - 1) * rng.integers(0, 2, (1, S))
            if i == 5:
                th[r, g] = 0; x[r, g] = rng.integers(0, WEAR + 2, (16, S))
            if i == 6:
                th[r, g] = 4080; own[r, g] = (L - 1) * rng.integers(0, 2, S); m[r, g] = (S - 1) * rng.integers(0, 2, (16, L))
            if i == 7: x[r, g] = int(rng.choice(np.array([0, 7, 255])))
    x[q] = np.where((st // L) % 2 == 0, rng.integers(0, 9, (8, 16, S)), 255 - rng.integers(0, 9, (8, 16, S)))
    x[q] = np.where(st // L == 1, rng.integers(18, 21, (8, 16, S)), x[q])
    nb[q] = rng.integers(0, L, (8, 16, S)) + 2 * L * rng.integers(0, ev, (8, 16, S)); th[q] = 200
    own[q] = np.argsort(rng.random((8, L)), axis=1)[:, st % L]
    m[q] = la + L * (2 * rng.integers(1, od, (8, 16, L)) + 1); m[p] = la + 2 * L * rng.integers(0, ev, (8, 16, L))
    m[u, int(turn[u][0])] = L + la
    return pack(x, nb, m, own, th)
def setup_inputs_ends(rng):
    home = 1 + np.argsort(rng.random((8, S - 3)), axis=1)[:, :L]; homes = np.broadcast_to(home, (N, 8, L))
    c = rng.choice(np.array([0, 1, 8, 15, 16]), (N, 8)); c[0, 0] = 0; c[0, 1] = 16; c[N - 1] = rng.choice(np.array([1, 8, 15]), 8)
    x = 255 * rng.integers(0, 2, (N, 8, 16, S))
    x[..., 0] = 255 * (np.argsort(rng.random((N, 8, 16)), axis=2) < c[:, :, None]); x[..., S - 1] = 255 - x[..., 0]; x[..., S - 2] = 255
    np.put_along_axis(x, np.broadcast_to(home[None, :, None, :], (N, 8, 16, L)), 0, 3)
    nb = (S - 1) * rng.integers(0, 2, (N, 8, 16, S))
    nb = np.where(rng.random(nb.shape) < 0.15, np.take_along_axis(homes, rng.integers(0, L, (N, 8, 16 * S)), 2).reshape(nb.shape), nb)
    side = rng.integers(0, 2, (N, 8, S)); nb[:, :, 15] = (S - 1) * side; nb[:, :, 0] = (S - 1) * (1 - side)
    sig = np.argsort(rng.random((N, 8, L)), axis=2); own = (L - 1) * rng.integers(0, 2, (N, 8, S)); np.put_along_axis(own, homes, sig, 2)
    mix = (S - 1) * rng.integers(0, 2, (N, 8, 16, L)); kind = rng.choice(np.array([0, 1, 2, 3, 3, 3]), (N, 8, 1, L)); kind[N - 2] = 3; kind[N - 1] = rng.integers(0, 2, (8, 1, L))
    place = np.argsort(rng.random((N, 8, 16, L)), axis=2); place[:, :, :, L - 1] = np.array([2, 3, 4, 5, 6, 7, 8, 9, 10, 11, 12, 13, 14, 15, 0, 1])
    two = rng.random((N, 8, 1, L)) < 0.5; two[..., L - 1] = True
    far = np.where((place == 1) | ((place == 2) & two), S - 2, mix)
    keep = np.where((place == 0) | ((place == 3) & two), home[None, :, None, :], far)
    m = np.where(kind == 0, 0, np.where(kind == 1, S - 1, np.where(kind == 2, mix, keep)))
    th = 4080 * rng.integers(0, 2, (N, 8)); th[:, 2] = 0; th[:, 7] = 4080
    i = int(rng.integers(0, 7)); th[N - 1] = 4080; th[N - 1, i] = 0
    g = (i + 1 + int(rng.integers(0, 6))) % 7; a = int(rng.integers(0, L)); nb[N - 1, g, :, home[g, a]] = m[N - 1, g, 0, sig[N - 1, g, a]]
    return pack(x, nb, m, own, th)
def setup_inputs_spread(rng):
    x, nb, m, own, th = parts(rng)
    x = np.minimum(np.exp2(8 * rng.random((N, 8, 1, S))) * rng.random((N, 8, 16, S)) * 1.25, 255.0).astype(np.int64) * (rng.random((N, 8, 1, S)) > 0.0625)
    m = np.minimum((S * rng.random((N, 8, 16, L)) ** (1 + 3 * rng.random((N, 8, 1, L)))).astype(np.int64), S - 1)
    m = np.where(rng.random((N, 8, 1, L)) < 0.5, m, S - 1 - m)
    u = np.minimum((S * rng.random((N, 4, 16, S)) ** 2).astype(np.int64), S - 1); nb[:, 1::2] = u
    own = np.minimum((L * rng.random((N, 8, S)) ** 2).astype(np.int64), L - 1)
    return pack(x, nb, m, own, np.exp2(8 + 3 * rng.random((N, 8))).astype(np.int64))
def check_inputs(d):
    bad = []
    for k, lo, hi in (("x0", 0, 255), ("nb", 0, S - 1), ("m0", 0, S - 1), ("own0", 0, L - 1), ("th", 0, 4080)):
        try:
            v = np.asarray(d[k]).astype(np.float32).astype(np.float64)
            if not np.all((v >= lo) & (v <= hi)): bad.append("range of " + k)
            elif not np.all(v == np.floor(v)): bad.append("whole numbers of " + k)
        except Exception:
            bad.append("form of " + k)
    return bad
def centre(x, m):
    v = np.take_along_axis(x, m.reshape(8, 1, 16 * L), 2).reshape(8, 16, 16, L)
    c = (np.max(v, axis=2) + np.min(v, axis=2)) >> 1
    d = np.add.reduce(np.abs(v - c[:, :, None, :]), axis=1)
    return c, np.argmin(d, axis=1), np.argmax(d, axis=1)
def reference(x0, nb, m0, own0, th):
    X = x0.astype(np.float32).astype(np.int32).reshape(N, 8, 16, S); nbs = nb.astype(np.int64).reshape(N, 8, 16, S)
    M = m0.astype(np.int64).reshape(N, 8, 16, L); O = own0.astype(np.int64).reshape(N, 8, S); T = th.astype(np.int64).reshape(N, 8)
    wins = np.zeros(N, np.int64); lane = np.broadcast_to(np.arange(L), (8, L)); grp = np.broadcast_to(np.arange(8)[:, None], (8, L))
    for t in range(RO):
        res, back = [], []; now = np.zeros(N, np.int64)
        for q in range(N):
            p = (q - 1 - t % (N - 1)) % N
            ci, ki, fi = centre(X[q], M[p]); cr, kr, fr = centre(X[q], M[q])
            s = np.take_along_axis(M[p], ki[:, None, :], 1)[:, 0]
            b = np.take_along_axis(O[q], s, 1)
            low = np.full((8, L), L); np.minimum.at(low, (grp, b), lane)
            fight = np.take_along_axis(low, b, 1) == lane
            n = np.take_along_axis(nbs[q], s[:, None, :], 2)
            v = np.take_along_axis(X[q], n.reshape(8, 1, 16 * L), 2).reshape(8, 16, 16, L)
            ei = np.add.reduce(np.abs(v - ci[:, :, None, :]), axis=1)
            er = np.add.reduce(np.abs(v - np.take_along_axis(cr, b[:, None, :], 2)[:, :, None, :]), axis=1)
            lim = T[q][:, None, None] + (wins[q] & 63)
            won = np.count_nonzero(ei < lim, axis=1) > np.count_nonzero(er < lim, axis=1)
            e = np.where(won[:, None, :], ei, er)
            best = np.take_along_axis(n, np.argmin(e, axis=1)[:, None, :], 1)[:, 0]
            worst = np.take_along_axis(n, np.argmax(e, axis=1)[:, None, :], 1)[:, 0]
            g, a = np.nonzero(fight); w = won[g, a]; bb = b[g, a]; ss = s[g, a]
            res.append((q, g, fr[g, bb], bb, np.where(w, worst[g, a], best[g, a])))
            back.append((p, g, np.where(w, fi[g, a], ki[g, a]), a, np.where(w, best[g, a], worst[g, a])))
            O[q][g, ss] = np.where(w, np.where(bb + 1 == L, 0, bb + 1), bb)
            if t < RO - 1: X[q][g, :, ss] = np.maximum(X[q][g, :, ss] - WEAR, 0)
            now[q] = np.count_nonzero(w)
        for r, g, k, a, z in res + back: M[r][g, k, a] = z
        wins = now
    return {"ym": M.reshape(N, 128, L).astype(np.float32), "yown": O.astype(np.float32)}

@@ -1,0 +1,563 @@
+from concourse.mybir import AluOpType as OP, ActivationFunctionType as AF
+import comms_topo
+
+S, L, RO, WEAR = 4096, 256, 3, 8
+BIG = float(2 ** 26)
+B, F, I, U = "bfloat16", "float32", "int32", "uint16"
+SCRATCH = {"OD": ("dram", [8, S], B)}
+for _d, _l in ((B, "XW:4352 OWN:4352 GR:4096 GI:4096 GN:4096 S1:4096 S2:4096 DI:4096 MX:4096 CR:256 CI:256 CB:256 THB:128 ONE:128 IDB:128 IDN:128 "
+                   "IDH:128 IDC:128 BO:128 MHALF:128 DGA:256 SM1:1024 SM2:1024 ERC:2048 WB:32 WID:32 WIX:32 WIG:32 WER:32 WEX:32 WRD:8 JC:512 LJT:256 LJ:1024 "
+                   "NC:512 SEL:1280 SELR:256 MLO:256 MHI:256 TP:128 RP:128 SCM:256 SC:256 B1:256 KRW:256 KRB:256 OHR:256 EQ:2176 NF:256 FT:256 FAM:512 OHI:256 "
+                   "B0W:256 DBA:256 DB:256 OT:256 XU:256"),
+               (F, "EO:256 ER0:256 ER1:256 ER2:256 TA:1 TB:1 ONF:128 IDF:128 KC:1 CM:256 DG:256 SMF:512 SMA:256 R16:16 AI0:16 ALS:16 ALB:16 "
+                   "KSC:512 KSO:512 KSR:256 EI:1024 EK:1024 SD:256 SS:256 SCR:64 CUM:272 DD:80 SELT:104 TS:64 ERV:256 ERW:512 PW:256 WC:1 M1:256"),
+               (I, "NBW:4096 MI:256 THC:1 TE:1 THI:1 TLO:1 WI:1 WJ:1 NI:256 NJ:256 TT:128 TU:128 RT:128 RU:128 M2:256"),
+               (U, "ML:256 LI0:256 LI1:256 LI2:256 LS:16 LB:16 NL:256 LSD:16 LBD:16")):
+    for _e in _l.split():
+        SCRATCH[_e.split(":")[0]] = ("sbuf", [128, int(_e.split(":")[1])], _d)
+PSUM = ["P%d" % i for i in range(8)]
+for _p in PSUM:
+    SCRATCH[_p] = ("psum", [128, 512], F)
+SEMAPHORES = (["q_v", "q_s", "q_t", "q_g"] + ["d_" + n for n in ("x", "m", "o", "nb", "th", "od", "ow", "ym", "yo")]
+              + [n + str(t) for n in ("al", "ae", "sl", "se") for t in range(RO)])
+
+
+def rank_program(g, core, T, topo):
+    rank = T.rank_of(core)
+    if rank is None:
+        return
+    N = len(T.cores)
+    Q = {"v": g.vector, "s": g.scalar, "t": g.tensor, "g": g, "y": g.sync}
+    done = {n: 0 for n in SEMAPHORES}
+    know = {q: {} for q in Q}
+    clock = {}
+    acc = {}
+
+    def A(name, c0=0, c1=None, st=1, p0=None, p1=None):
+        t = T[name]
+        c1 = t.shape[1] if c1 is None else c1
+        ps = slice(None) if p0 is None else slice(p0, p1)
+        return (t[ps, slice(c0, c1) if st == 1 else slice(c0, c1, st)], [(name, c0, c1)])
+
+    def IND(win, off):
+        return (win[0].indirect(off[0]), win[1] + off[1])
+
+    def ext(t):
+        return (t, [])
+
+    def conflicts(q, reads, writes):
+        need = {}
+        for regs, wr in ((reads, False), (writes, True)):
+            for (b, c0, c1) in regs:
+                for (aq, aw, a0, a1, sem, val) in acc.get(b, []):
+                    if b in PSUM:
+                        if aq == q and (q == "t" or not aw or a1 <= c0 or a0 >= c1):
+                            continue
+                    elif not (aw or wr) or a1 <= c0 or a0 >= c1:
+                        continue
+                    need[sem] = max(need.get(sem, 0), val)
+        return need
+
+    def wait(q, sem, val):
+        if know[q].get(sem, 0) >= val:
+            return
+        Q[q].wait_ge(T.sem[sem], val)
+        for k, v in clock.get((sem, val), {}).items():
+            know[q][k] = max(know[q].get(k, 0), v)
+        know[q][sem] = max(know[q].get(sem, 0), val)
+
+    def note(q, reads, writes, sem, val):
+        for regs, wr in ((writes, True), (reads, False)):
+            for (b, c0, c1) in regs:
+                l = acc.setdefault(b, [])
+                if b in PSUM:
+                    l[:] = [x for x in l if x[0] == q and not (x[2] >= c0 and x[3] <= c1 and (wr or not x[1]))]
+                else:
+                    l[:] = [x for x in l if not (x[2] >= c0 and x[3] <= c1 and (wr or (x[0] == q and not x[1])))]
+                l.append((q, wr, c0, c1, sem, val))
+
+    def waits(q, reads, writes):
+        need = conflicts(q, reads, writes)
+        for s in sorted(need, key=lambda s: -sum(1 for o in need if o != s and clock.get((s, need[s]), {}).get(o, 0) >= need[o])):
+            wait(q, s, need[s])
+
+    def flat(l):
+        return [r for x in l for r in x[1]]
+
+    def emit(q, call, writes, reads, sem=None, n=1):
+        reads, writes = flat(reads), flat(writes)
+        waits(q, reads, writes)
+        sem = sem or "q_" + q
+        done[sem] += n
+        call().then_inc(T.sem[sem], n)
+        clock[(sem, done[sem])] = dict(know[q])
+        note(q if n == 1 else "d" + sem, reads, writes, sem, done[sem])
+
+    def w_emit(q, call, out, reads):
+        emit(q, call, [(None, out[1][:1])], list(reads) + [(None, out[1][1:])])
+
+    def cp(out, i):
+        w_emit("v", lambda: g.vector.tensor_copy(out[0], i[0]), out, [i])
+
+    def tt(out, a, b, op):
+        w_emit("v", lambda: g.vector.tensor_tensor(out[0], a[0], b[0], op), out, [a, b])
+
+    def ts(out, a, s1, op0, s2=None, op1=None):
+        col = [s1] if isinstance(s1, tuple) else []
+        v = s1[0] if col else s1
+        if op1 is None:
+            w_emit("v", lambda: g.vector.tensor_scalar(out[0], a[0], v, None, op0), out, [a] + col)
+        else:
+            w_emit("v", lambda: g.vector.tensor_scalar(out[0], a[0], v, s2, op0, op1), out, [a] + col)
+
+    def scan(out, d0, d1, op0, op1, init=0.0):
+        w_emit("v", lambda: g.vector.tensor_tensor_scan(out[0], d0[0], d1[0], init, op0, op1), out, [d0, d1])
+
+    def fill(out, c):
+        w_emit("v", lambda: g.vector.memset(out[0], c), out, [])
+
+    def act(out, i, func, bias=0.0, scale=1.0, accum=None):
+        emit("s", lambda: g.scalar.activation(out[0], i[0], func, bias=bias, scale=scale, accum_out=accum and accum[0]), [out] + ([accum] if accum else []), [i])
+
+    def mm(out, l, r, start=False, stop=False):
+        emit("t", lambda: g.tensor.matmul(out[0], l[0], r[0], start, stop), [out], [l, r])
+
+    def aff(out, i, pat, op, fl, base, cm):
+        emit("g", lambda: g.affine_select(out[0], i[0], pat, op, fl, base, cm), [out], [i])
+
+    def iota(out, pat, cm):
+        emit("g", lambda: g.iota(out[0], pat, 0, cm, allow_small_or_imprecise_dtypes=True), [out], [])
+
+    def dma(q, out, i, sem):
+        emit(q, lambda: Q[q].dma_start(out[0], i[0]), [out], [i], sem, 16)
+
+    def dmas(q, calls, out, i, sem):
+        waits(q, flat(i), out[1])
+        for call in calls:
+            call().then_inc(T.sem[sem], 16)
+        done[sem] += 16 * len(calls)
+        clock[(sem, done[sem])] = dict(know[q])
+        note("d" + sem, flat(i), out[1], sem, done[sem])
+
+    def lanes(src, dst):
+        return topo.engines(src, dst)[:8]
+
+    def send(dst, out, i, rsem, lsem):
+        rid, pid = topo.addr(dst)[:2]
+        eng = lanes(core, dst)
+        waits("g", i[1], [])
+        g.remote_dma(out[0], i[0], T.sem[rsem], T.sem[lsem], pid, rid, sum(1 << e for e in eng))
+        done[lsem] += len(eng)
+        clock[(lsem, done[lsem])] = dict(know["g"])
+        note("r" + lsem, i[1], [], lsem, done[lsem])
+
+    def arrives(name, rsem, src):
+        done[rsem] += len(lanes(src, core))
+        note("n" + rsem, [], A(name)[1], rsem, done[rsem])
+
+    fill(A("THC"), 0)
+    dma("y", A("XW", 0, S), ext(T.x0[:]), "d_x")
+    dma("s", A("MI"), ext(T.m0[:]), "d_m")
+    dma("s", A("NI"), ext(T.own0[:]), "d_o")
+    dmas("y", [lambda r=r: g.sync.dma_start(T.THC[r::16, 0:1], T.th[:]) for r in range(2)], A("THC"), [], "d_th")
+    dma("y", A("NBW"), ext(T.nb[:]), "d_nb")
+    fill(A("ONE"), 1.0)
+    iota(A("CM"), [[0, 16], [1, 16]], 0)
+    iota(A("WI"), [[0, 1]], 1)
+    aff(A("IDB"), A("ONE"), [[-1, 128]], OP.is_equal, 0.0, 0, 1)
+    aff(A("WB"), A("ONE", 0, 32), [[0, 4], [-16, 8]], OP.is_ge, 0.0, 0, 1)
+    aff(A("WB"), A("WB"), [[0, 4], [16, 8]], OP.is_ge, 0.0, 15, -1)
+    aff(A("BO"), A("ONE"), [[-16, 8], [0, 16]], OP.is_ge, 0.0, 0, 1)
+    aff(A("BO"), A("BO"), [[16, 8], [0, 16]], OP.is_ge, 0.0, 15, -1)
+    iota(A("AI0"), [[16, 16]], 0)
+    fill(A("MHALF"), -0.5)
+    ts(A("SM1", 0, 256), A("CM"), 0.0, OP.not_equal)
+    ts(A("SM2", 0, 256), A("CM"), 0.0, OP.is_equal, 1024.0, OP.mult)
+    for c in (256, 512):
+        for n in ("SM1", "SM2"):
+            cp(A(n, c, 2 * c), A(n, 0, c))
+    ts(A("WJ"), A("WI"), 15, OP.bitwise_and)
+    ts(A("IDH"), A("IDB"), 0.5, OP.mult)
+    cp(A("KC"), A("WJ"))
+    cp(A("ML"), A("MI"))
+    arrives("LI0", "al0", T.cores[(rank - 1) % N])
+    send(T.cores[(rank + 1) % N], A("LI0"), A("ML"), "al0", "sl0")
+    cp(A("CB"), A("NI"))
+    dma("y", (T.OD[:], [("OD", 0, S)]), A("CB"), "d_od")
+    dmas("y", [lambda r=r: g.sync.dma_start(T.OWN[r::16, 0:S], T.OD[:]) for r in range(16)], A("OWN", 0, S), [("", [("OD", 0, S)])], "d_ow")
+    ts(A("IDN"), A("IDB"), -1.0, OP.mult)
+    ts(A("WID", 0, 16), A("WB", 0, 16), 1024.0, OP.mult)
+    ts(A("WID", 16, 24), A("WB", 0, 8), -64.0, OP.mult)
+    ts(A("WID", 24, 32), A("WB", 0, 8), 64.0, OP.mult)
+    ts(A("WER", 0, 16), A("WB", 0, 16), -1024.0, OP.mult)
+    ts(A("WER", 16, 32), A("WB", 0, 16), 1024.0, OP.mult)
+    ts(A("WRD"), A("WB", 0, 8), -64.0, OP.mult)
+    ts(A("WIX"), A("WID"), 2.0, OP.mult)
+    ts(A("WIG"), A("WID"), -1.0, OP.mult)
+    ts(A("WEX"), A("WER"), -2.0, OP.mult)
+    fill(A("SEL"), 0.0)
+    fill(A("SELR"), 0.0)
+    ts(A("R16"), A("CM", 0, 16), A("KC"), OP.is_equal)
+    ts(A("LJT", 0, 128), A("CM", 0, 128), A("R16", 0, 1), OP.mult)
+    aff(A("LJT", 0, 128), A("LJT", 0, 128), [[0, 128]], OP.is_equal, 0.0, 0, 1)
+    ts(A("SMF", 0, 256), A("CM"), 0.0, OP.is_equal, BIG, OP.mult)
+    ts(A("SMA"), A("CM"), 0.0, OP.not_equal)
+    ts(A("DG"), A("CM"), A("KC"), OP.is_equal)
+
+    def late_constants():
+        ts(A("JC", 0, 128), A("LJT", 0, 128), 64.0, OP.mult)
+        ts(A("JC", 128, 256), A("LJT", 0, 128), 64.0, OP.mult)
+        cp(A("JC", 256, 384), A("LJT", 0, 128))
+        cp(A("JC", 384, 512), A("LJT", 0, 128))
+        cp(A("IDF"), A("IDB"))
+        ts(A("DGA"), A("DG"), 1001.0, OP.mult, -1000.0, OP.add)
+
+        def sel(name, i, row, weight):
+            o = A(name, 128 * i, 128 * i + 128)
+            aff(o, o, [[-1, 8], [0, 16]], OP.not_equal, weight, -row, 1)
+        for h in range(2):
+            sel("SEL", h, 16 * h, 1.0)
+            sel("SEL", h, 16 * h + 8, 64.0)
+        for h in range(2):
+            sel("SEL", 2 + h, 64 + 8 * h, 1.0)
+            sel("SEL", 4 + h, 80 + 8 * h, 1.0)
+            sel("SEL", 6 + h, 32 * h, 1.0)
+            sel("SEL", 6 + h, 32 * h + 8, 64.0)
+            sel("SEL", 8 + h, 32 * h + 16, 1.0)
+            sel("SEL", 8 + h, 32 * h + 24, 64.0)
+            for i, c in ((6, 8192.0), (8, 4096.0)):
+                o = A("SEL", 128 * (i + h), 128 * (i + h) + 128)
+                aff(o, o, [[0, 128]], OP.not_equal, c, -96, 1)
+            sel("SELR", h, 8 * h, 1.0)
+        for r in range(16):
+            aff(A("ERC", 128 * r, 128 * r + 128), A("IDB"), [[-16, 8], [0, 16]], OP.is_equal, 0.0, -r, 1)
+
+    def later_constants():
+        ts(A("ALS"), A("AI0"), A("KC"), OP.add, float(S), OP.add)
+        ts(A("ALB"), A("AI0"), A("KC"), OP.add, float(L + 1), OP.add)
+        ts(A("LJT", 0, 128), A("CM", 0, 128), A("R16", 2, 3), OP.mult, 64.0, OP.mult)
+        aff(A("LJT", 0, 128), A("LJT", 0, 128), [[0, 128]], OP.is_equal, 0.0, -2, 1)
+        ts(A("LJT", 128, 256), A("BO"), A("R16", 1, 2), OP.mult, -1024.0, OP.mult)
+        for i in range(2):
+            ts(A("NC", 128 * i, 128 * i + 128), A("BO"), -1024.0, OP.mult)
+            ts(A("NC", 128 * i + 256, 128 * i + 384), A("BO"), 1024.0, OP.mult)
+        ts(A("IDC"), A("IDB"), 100.0, OP.mult)
+        fill(A("ONF"), 1.0)
+        fill(A("XW", S, S + L), 0.0)
+        fill(A("OWN", S, S + L), 0.0)
+        fill(A("CUM", 0, 16), 0.0)
+        fill(A("SELT"), 1.0)
+        tt(A("LJT", 128, 256), A("LJT", 128, 256), A("LJT", 0, 128), OP.add)
+        for i in range(8):
+            c = 128 * i
+            if i in (0, 6):
+                ts(A("LJ", c, c + 128), A("BO"), A("R16", 0, 1), OP.mult, -65536.0, OP.mult)
+                tt(A("LJ", c, c + 128), A("LJ", c, c + 128), A("LJT", 128, 256), OP.add)
+            else:
+                cp(A("LJ", c, c + 128), A("LJT", 0, 128))
+        cp(A("SMF", 256, 512), A("SMF", 0, 256))
+
+    later = []
+
+    def some(n):
+        for _ in range(min(n, len(later))):
+            later.pop(0)()
+
+    def limits(first):
+        if first:
+            later.append(lambda: cp(A("TE"), A("THC")))
+        else:
+            later.append(lambda: cp(A("WI"), A("P6", 0, 1)))
+            later.append(lambda: ts(A("WJ"), A("WI"), 4, OP.logical_shift_right, 63, OP.bitwise_and))
+            later.append(lambda: tt(A("TE"), A("THC"), A("WJ"), OP.add))
+        later.append(lambda: ts(A("THI"), A("TE"), 6, OP.logical_shift_right))
+        later.append(lambda: ts(A("TLO"), A("TE"), 63, OP.bitwise_and))
+        later.append(lambda: tt(A("TA"), A("THI"), A("R16", 0, 1), OP.mult))
+        later.append(lambda: tt(A("TB"), A("TLO"), A("R16", 1, 2), OP.mult))
+        later.append(lambda: tt(A("TA"), A("TA"), A("TB"), OP.add))
+        later.append(lambda: tt(A("TB"), A("TA"), A("R16", 2, 3), OP.add))
+        later.append(lambda: ts(A("THB"), A("ONE"), A("TB"), OP.mult))
+
+    def six(lst):
+        later.append(lambda: cp(A("NI"), A(lst)))
+        later.append(lambda: ts(A("NJ"), A("NI"), 63, OP.bitwise_and))
+        later.append(lambda: ts(A("M2"), A("NI"), 6, OP.logical_shift_right))
+        later.append(lambda: cp(A("MLO"), A("NJ")))
+        later.append(lambda: cp(A("MHI"), A("M2")))
+
+    def gather(q, dst, lst, c):
+        out, src = A(dst, 1024 * c, 1024 * c + 1024), IND(A("XW", 0, S), A(lst, 64 * c, 64 * c + 64))
+        if q == "v":
+            cp(out, src)
+        else:
+            act(out, src, AF.Copy)
+
+    def scans(src, c, n=0):
+        o = 1024 * c
+        scan(A("S1", o, o + 1024), A("SM1"), A(src, o, o + 1024), OP.mult, OP.max)
+        some(n)
+        scan(A("S2", o, o + 1024), A("SM2"), A(src, o, o + 1024), OP.add, OP.min, BIG)
+        some(n)
+
+    def centre(dst, a0, n):
+        for a in range(a0, a0 + n, 128):
+            p = A("P2", a - a0, a - a0 + 128)
+            mm(p, A("IDH"), A("S1", 16 * a + 15, 16 * a + 2048, 16), True, False)
+            mm(p, A("IDH"), A("S2", 16 * a + 15, 16 * a + 2048, 16))
+            mm(p, A("IDH"), A("MHALF"), False, True)
+        ts(A(dst, a0, a0 + n), A("P2", 0, n), float(2 ** 23), OP.add, -float(2 ** 23), OP.add)
+
+    turn = [0]
+
+    def diff(src, cen, h, b, banks, hold=False):
+        bank = banks[turn[0] % len(banks)]
+        turn[0] += 1
+        for k in range(4):
+            o = A(bank, 128 * k, 128 * k + 128)
+            mm(o, A("IDB"), A(src, 2048 * h + 4 * b + k, 2048 * (h + 1), 16), True, False)
+            mm(o, A("IDN"), A(cen, 128 * h, 128 * h + 128), False, True)
+
+        def out():
+            act(A("DI", 2048 * h + 512 * b, 2048 * h + 512 * b + 512), A(bank), AF.Abs)
+        return out if hold else out()
+
+    def sum_d(bank, h, b, w, n=32):
+        for k in range(4 * b, 4 * b + 4):
+            mm(A(bank, k, 16 * n, 16), A("DI", 2048 * h + 128 * k, 2048 * h + 128 * k + 128), A(w), False, k == 15)
+
+    def sum_g(bank, src, h, w):
+        for k in range(16):
+            mm(A(bank, k, 512, 16), A(src, 2048 * h + k, 2048 * (h + 1), 16), A(w))
+
+    def sum_x(bank, h, k, w):
+        mm(A(bank, k, 512, 16), A("MX", 256 * k + 128 * h, 256 * k + 128 * h + 128), A(w), False, k == 15)
+
+    def turned(n, bank, src):
+        o = A(bank, 0, 128, 1, 0, n)
+        emit("t", lambda: g.tensor.transpose(o[0], src[0], A("IDF")[0]), [o], [src, A("IDF")])
+
+    def low(n, bank, mask, x="T"):
+        cp(A(x + "T", 0, 128, 1, 0, n), A(bank, 0, 128, 1, 0, n))
+        ts(A(x + "U", 0, 128, 1, 0, n), A(x + "T", 0, 128, 1, 0, n), mask, OP.bitwise_and)
+        cp(A(x + "P", 0, 128, 1, 0, n), A(x + "U", 0, 128, 1, 0, n))
+
+    def spread(bank, o, name, i, n, start=True, x="TP"):
+        for h in range(2):
+            mm(A(bank, o + 128 * h, o + 128 * h + 128), A(name, 128 * (i + h), 128 * (i + h) + 128, 1, 0, n), A(x, 0, 128, 1, 0, n), start, start or h == 1)
+
+    off = [256 + sum(240 - 16 * d for d in range(c)) for c in range(15)]
+
+    def same(c0, c1):
+        for c in range(c0, c1):
+            some(1)
+            if c == 0:
+                tt(A("EQ", 0, 256), A("SC"), A("B1"), OP.is_equal)
+            else:
+                n = 256 - 16 * c
+                ts(A("EQ", off[c - 1], off[c - 1] + n), A("B1", 256 - n, 256), A("SC", 16 * c - 1, 16 * c), OP.is_equal)
+        some(9)
+
+    THREE, TWO, EB, NP = ["P0", "P1", "P6"], ["P0", "P1"], ["P0", "P1", "P2"], 3
+    seq = [(h, b) for h in range(2) for b in range(4)]
+    for t in range(RO):
+        host = T.cores[(rank + 1 + t) % N]
+        guest = T.cores[(rank - 1 - t) % N]
+        LI = "LI%d" % t
+        turn[0] = 0
+        for c in range(4):
+            gather("v" if c == 1 else "s", "GR", "ML", c)
+            if t > 0 and c == 1:
+                act(A("SD"), A("PW"), AF.Copy, accum=A("WC"))
+                mm(A("P6", 0, 1), A("ONF"), A("WC"), True, True)
+        for c in range(4):
+            gather("s", "GI", LI, c)
+        for c in (1, 0, 2, 3):
+            scans("GR", c, 3)
+            if c == 0:
+                if t == 0:
+                    late_constants()
+                six(LI)
+                if t == 0:
+                    limits(True)
+        some(99)
+        if t > 0:
+            limits(False)
+        centre("CR", 0, 256)
+        scans("GI", 0)
+        scans("GI", 1)
+        centre("CI", 0, 128)
+        for h in range(2):
+            mm(A(PSUM[3 + h]), A("ONE"), A("JC"), True, False)
+            mm(A(PSUM[3 + h], 0, 128), A("MLO", 128 * h, 128 * h + 128), A("IDB"))
+            mm(A(PSUM[3 + h], 128, 256), A("MHI", 128 * h, 128 * h + 128), A("IDB"))
+        some(2)
+        scans("GI", 2)
+        scans("GI", 3)
+        diff("GI", "CI", 0, 0, THREE)
+        diff("GI", "CI", 0, 1, THREE)
+        diff("GI", "CI", 0, 2, THREE)
+        centre("CI", 128, 128)
+        mm(A("P7", 0, 128), A("IDB"), A("CI", 128, 256), True, True)
+        diff("GI", "CI", 0, 3, THREE)
+        sum_g("P4", "GI", 1, "WIG")
+        for k in range(16):
+            tt(A("MX", 256 * k + 128, 256 * k + 256), A("GI", 2048 + k, 4096, 16), A("P7", 0, 128), OP.max)
+        for b in range(4):
+            sum_d("P3", 0, b, "WID")
+            for k in range(4 * b, 4 * b + 4):
+                sum_x("P4", 1, k, "WIX")
+        for h in range(2):
+            scan(A("KSC", 256 * h, 256 * h + 256), A("SMF", 0, 256), A(PSUM[3 + h], 0, 256), OP.add, OP.min, BIG)
+        diff("GR", "CR", 0, 0, THREE)
+        turned(32, "P2", A("KSC", 15, 512, 16))
+        some(4)
+        low(32, "P2", 63)
+        some(2)
+        diff("GR", "CR", 0, 1, THREE)
+        spread("P2", 0, "SEL", 0, 32)
+        diff("GR", "CR", 0, 2, THREE)
+        tt(A("SD"), A("P2", 0, 256), A("DG"), OP.mult)
+        scan(A("SS"), A("SMA"), A("SD"), OP.mult, OP.add)
+        cp(A("LS"), A("SS", 15, 256, 16))
+        cp(A("NL"), IND(A("NBW"), A("LS")))
+        some(99)
+        mm(A("P5", 0, 128), A("ONE"), A("JC", 256, 384), True, False)
+        sum_d("P5", 0, 0, "WRD", 8)
+        diff("GR", "CR", 0, 3, THREE)
+        for b in range(1, 4):
+            sum_d("P5", 0, b, "WRD", 8)
+        for c in range(4):
+            gather("s", "GN", "NL", c)
+        tt(A("SCM"), IND(A("OWN", 0, S), A("LS")), A("DGA"), OP.add)
+        ts(A("B1"), IND(A("OWN", 0, S), A("LS")), 1.0, OP.add)
+        scan(A("KSO", 0, 256), A("SMF", 0, 256), A("P3", 256, 512), OP.add, OP.min, BIG)
+        scan(A("SC"), A("SM1", 0, 256), A("SCM"), OP.mult, OP.max)
+        scan(A("KSO", 256, 512), A("SMF", 0, 256), A("P4", 256, 512), OP.add, OP.min, BIG)
+        ts(A("LB"), A("SC", 15, 256, 16), -1.0, OP.add)
+        scan(A("KSR", 0, 128), A("SMF", 0, 128), A("P5", 0, 128), OP.add, OP.min, BIG)
+        cp(A("CB"), IND(A("CR"), A("LB")))
+        mm(A("P7", 256, 512), A("IDB"), A("CI"), True, True)
+        if t == 0:
+            later_constants()
+        for i in range(4):
+            mm(A(PSUM[3 + i]), A("THB"), A("LJ", 512 * (i // 2), 512 * (i // 2) + 512), True, False)
+            if i < 2:
+                mm(A(PSUM[3 + i]), A("CI", 128 * i, 128 * i + 128), A("NC"))
+        six("NL")
+        same(0, 4)
+        for i in range(4):
+            for j in range(4):
+                mm(A(PSUM[3 + i], 128 * j, 128 * j + 128), A("MHI" if j % 2 else "MLO", 128 * (i % 2), 128 * (i % 2) + 128), A("IDB"))
+        for b in range(NP):
+            diff("GN", "CB", 0, b, EB)
+        sum_g("P3", "GN", 0, "WER")
+        same(4, 16)
+        for h in range(2):
+            tt(A("DD", 64 + 8 * h, 72 + 8 * h), A("KSO", 256 * h + 15, 256 * h + 128, 16), A("KSO", 256 * h + 143, 256 * h + 256, 16), OP.subtract)
+        ts(A("DBA"), A("B1"), 256.0, OP.is_equal, -256.0, OP.mult)
+        for i, (h, b) in enumerate(seq):
+            if i == 1:
+                sum_g("P4", "GN", 1, "WER")
+            if 0 < i < 9 - NP:
+                diff("GN", "CB", seq[i + NP - 1][0], seq[i + NP - 1][1], EB)
+            for k in (2 * i, 2 * i + 1):
+                tt(A("MX", 256 * k, 256 * k + 256), A("GN", k, 16 * L, 16), A("P7", 256, 512), OP.max)
+                for hh in range(2):
+                    sum_x(PSUM[3 + hh], hh, k, "WEX")
+            sum_d(PSUM[5 + h], h, b, "WER")
+        held = [diff("GR", "CR", 1, b, TWO, True) for b in range(2)]
+        mm(A("P2", 0, 256), A("BO"), A("EQ", 0, 256), True, False)
+        for c in range(15):
+            n = 240 - 16 * c
+            mm(A("P2", 256 - n, 256), A("BO"), A("EQ", off[c], off[c] + n), False, c == 14)
+        tt(A("SCR", 0, 16), A("ALS"), A("SS", 15, 256, 16), OP.subtract)
+        tt(A("SCR", 32, 48), A("ALB"), A("SC", 15, 256, 16), OP.subtract)
+
+        def fam(o, bank, c):
+            act(A("FAM", o, o + 128), A(bank, c, c + 128), AF.Sign, -0.5, -1.0)
+
+        def key(out, h, bank):
+            scan(A(out, 512 * h, 512 * h + 512), A("SMF"), A(bank), OP.add, OP.min, BIG)
+        key("EK", 0, "P5")
+        fam(128, "P4", 0)
+        key("EI", 0, "P3")
+        fam(256, "P5", 256)
+        fam(384, "P6", 256)
+        key("EI", 1, "P4")
+        fam(0, "P3", 0)
+        key("EK", 1, "P6")
+        mm(A("P7", 0, 128), A("ONE"), A("JC", 256, 384), True, False)
+        for out in held:
+            out()
+        act(A("OT"), A("P2", 0, 256), AF.Sign, -1.5)
+        act(A("NF"), A("OT"), AF.Identity, 0.5, 0.5)
+        for b in (2, 3):
+            diff("GR", "CR", 1, b, TWO)
+        for b in range(4):
+            sum_d("P7", 1, b, "WRD", 8)
+        act(A("B0W"), A("B1"), AF.Identity, -1.0)
+        act(A("DB"), A("DBA"), AF.Identity, 1.0)
+        act(A("FT"), A("NF"), AF.Identity, 1.0, -1.0)
+        act(A("ERW", 0, L), A("SS"), AF.Identity, 0.0, 0.0)
+        tt(A("DD", 0, 64), A("EI", 15, 1024, 16), A("EK", 15, 1024, 16), OP.subtract)
+        scan(A("CUM", 16, 272), A("FAM", 0, 256), A("FAM", 256, 512), OP.add, OP.subtract)
+        tt(A("SELT", 80, 96), A("CUM", 31, 272, 16), A("CUM", 15, 256, 16), OP.is_gt)
+        for h in range(2):
+            for c in range(32 * h, 32 * h + 32, 8):
+                tt(A("TS", c, c + 8), A("DD", c, c + 8), A("SELT", 80 + 8 * h, 88 + 8 * h), OP.mult)
+        tt(A("DD", 64, 80), A("DD", 64, 80), A("SELT", 80, 96), OP.mult)
+        tt(A("SELT", 0, 64), A("TS"), A("EK", 15, 1024, 16), OP.add)
+        for h in range(2):
+            tt(A("SELT", 64 + 8 * h, 72 + 8 * h), A("DD", 64 + 8 * h, 72 + 8 * h), A("KSO", 256 * h + 143, 256 * h + 256, 16), OP.add)
+        turned(97, "P2", A("SELT", 0, 97))
+        scan(A("KSR", 128, 256), A("SMF", 0, 128), A("P7", 0, 128), OP.add, OP.min, BIG)
+        turned(16, "P4", A("KSR", 15, 256, 16))
+        low(97, "P2", 63)
+        low(16, "P4", 15, "R")
+        mm(A("P0", 0, 256), A("IDC"), A("NF"), True, False)
+        spread("P0", 0, "SEL", 2, 97, False)
+        spread("P0", 256, "SEL", 6, 97)
+        spread("P1", 0, "SEL", 8, 97)
+        spread("P1", 256, "SEL", 4, 97)
+        spread("P4", 256, "SELR", 0, 16, True, "RP")
+        for r in range(16):
+            mm(A("P5", 0, 16), A("ERC", 128 * r, 128 * r + 128), A("NF", r, 256, 16), r == 0, r == 15)
+        ts(A("OHI"), A("P0", 0, 256), A("KC"), OP.is_equal)
+        tt(A("EO"), A("OHI"), A("P0", 256, 512), OP.mult)
+        arrives("ER%d" % t, "ae%d" % t, host)
+        send(guest, A("ER%d" % t), A("EO"), "ae%d" % t, "se%d" % t)
+        act(A("KRW"), A("P4", 256, 512), AF.Copy)
+        act(A("KRB"), IND(A("KRW"), A("LB")), AF.Copy)
+        tt(A("SCR", 16, 32), A("SCR", 0, 16), A("P5", 0, 16), OP.mult)
+        tt(A("SCR", 48, 64), A("SCR", 32, 48), A("P5", 0, 16), OP.mult)
+        tt(A("SCR", 0, 16), A("SCR", 16, 32), A("SS", 15, 256, 16), OP.add)
+        tt(A("SCR", 32, 48), A("SCR", 48, 64), A("SC", 15, 256, 16), OP.add)
+        cp(A("LSD"), A("SCR", 0, 16))
+        ts(A("LBD"), A("SCR", 32, 48), -1.0, OP.add)
+        tt(A("OT"), A("DB"), A("P1", 256, 512), OP.mult)
+        if t < RO - 1:
+            act(A("XU"), IND(A("XW"), A("LSD")), AF.Relu, -float(WEAR))
+        ts(A("OHR"), A("KRB"), A("KC"), OP.is_equal)
+        tt(A("ERV"), A("OHR"), A("P1", 0, 256), OP.mult)
+        if t == RO - 1:
+            tt(IND(A("OWN"), A("LSD")), A("OT"), A("B0W"), OP.add)
+            dma("g", ext(T.yown[:]), (T.OWN[0::16, 0:S], [("OWN", 0, S)]), "d_yo")
+        cp(IND(A("ERW"), A("LBD")), A("ERV"))
+        if t < RO - 1:
+            tt(A("PW"), A("FT"), A("P1", 256, 512), OP.mult)
+        tt(A("M1"), A("MI"), A("ERW", 0, L), OP.max)
+        if t < RO - 1:
+            cp(IND(A("XW"), A("LSD")), A("XU"))
+            tt(IND(A("OWN"), A("LSD")), A("OT"), A("B0W"), OP.add)
+        tt(A("M2"), A("M1"), A("ER%d" % t), OP.max)
+        ts(A("MI"), A("M2"), 4095, OP.bitwise_and)
+        if t == RO - 1:
+            cp(A("PW"), A("MI"))
+            dma("y", ext(T.ym[:]), A("PW"), "d_ym")
+        else:
+            cp(A("ML"), A("MI"))
+            arrives("LI%d" % (t + 1), "al%d" % (t + 1), T.cores[(rank - 2 - t) % N])
+            send(T.cores[(rank + 2 + t) % N], A("LI%d" % (t + 1)), A("ML"), "al%d" % (t + 1), "sl%d" % (t + 1))
+    for s in SEMAPHORES:
+        if done[s]:
+            wait("g", s, done[s])

@@ -1,25 +1,28 @@
 from concourse.mybir import AluOpType as OP, ActivationFunctionType as AF
-import comms_topo
 
 S, L, RO, WEAR = 4096, 256, 3, 8
 BIG = float(2 ** 26)
-B, F, I, U = "bfloat16", "float32", "int32", "uint16"
-SCRATCH = {"OD": ("dram", [8, S], B)}
-for _d, _l in ((B, "XW:4352 OWN:4352 GR:4096 GI:4096 GN:4096 S1:4096 S2:4096 DI:4096 MX:4096 CR:256 CI:256 CB:256 THB:128 ONE:128 IDB:128 IDN:128 "
-                   "IDH:128 IDC:128 BO:128 MHALF:128 DGA:256 SM1:1024 SM2:1024 ERC:2048 WB:32 WID:32 WIX:32 WIG:32 WER:32 WEX:32 WRD:8 JC:512 LJT:256 LJ:1024 "
-                   "NC:512 SEL:1280 SELR:256 MLO:256 MHI:256 TP:128 RP:128 SCM:256 SC:256 B1:256 KRW:256 KRB:256 OHR:256 EQ:2176 NF:256 FT:256 FAM:512 OHI:256 "
-                   "B0W:256 DBA:256 DB:256 OT:256 XU:256"),
-               (F, "EO:256 ER0:256 ER1:256 ER2:256 TA:1 TB:1 ONF:128 IDF:128 KC:1 CM:256 DG:256 SMF:512 SMA:256 R16:16 AI0:16 ALS:16 ALB:16 "
-                   "KSC:512 KSO:512 KSR:256 EI:1024 EK:1024 SD:256 SS:256 SCR:64 CUM:272 DD:80 SELT:104 TS:64 ERV:256 ERW:512 PW:256 WC:1 M1:256"),
-               (I, "NBW:4096 MI:256 THC:1 TE:1 THI:1 TLO:1 WI:1 WJ:1 NI:256 NJ:256 TT:128 TU:128 RT:128 RU:128 M2:256"),
-               (U, "ML:256 LI0:256 LI1:256 LI2:256 LS:16 LB:16 NL:256 LSD:16 LBD:16")):
+M64 = 1.5 * 2 ** 29
+B, F, I, U, H = "bfloat16", "float32", "int32", "uint16", "float16"
+SCRATCH = {}
+for _d, _l in ((B, "XW:4352 OWN:4352 GR:4096 GI:4096 GN:4096 S1:8192 S2:8192 MXA:4096 MXB:4096 MXC:4096 DI:2048 CR:256 CI:256 CB:256 ONE:256 IDB:128 IDN:128 "
+                   "IDH:128 IDQ:128 IDS:256 BO:128 R0:128 R0B:128 MHALF:128 DGA:256 SM1:1024 SM2:1024 WB:32 WIG:32 WIX:32 WNG:32 WNX:32 WRG:32 WRX:32 "
+                   "WK:32 JC:512 NC:128 CZ:256 KW:128 SEL:768 AT:272 LM:2048 HIM:256 HIN:256 TP:128 TM:256 RP:128 B0:256 B1:256 SCM:256 SC:256 LT:256 "
+                   "EQ:3200 NF8:16 LO8:16 WF:16 NT:512 NT2:256 CC:32 FAM:512 KRW:256 SQ:256 XU:256"),
+               (H, "ID16:128 LJ:768 THB:128 MSM:256 MSN:256 SL16:16"),
+               (F, "EO:256 ER0:256 ER1:256 ER2:256 IDF:128 PI:1 KC:1 NKC:1 TB:1 COL:16 CM:256 CM2:128 SMF:512 R16:16 ALD:32 KSC:512 KSO:512 KSR:256 "
+                   "EI:1024 EK:1024 RT:128 RM:256 RR:128 RK:32 KK:32 CUM:288 WN:16 DD:80 TS:80 SELT:112 LF:48 ERV:256 ERW:512 PW:256"),
+               (I, "NBW:4096 MI:256 THC:1 TE:1 WI:1 WJ:1 NI:256 M2:256"),
+               (U, "ML:256 LI0:256 LI1:256 LI2:256 LS:16 LB:16 NL:256 LD:48")):
     for _e in _l.split():
         SCRATCH[_e.split(":")[0]] = ("sbuf", [128, int(_e.split(":")[1])], _d)
-PSUM = ["P%d" % i for i in range(8)]
+PSUM = ["P%d" % i for i in range(7)] + ["PB"]
 for _p in PSUM:
-    SCRATCH[_p] = ("psum", [128, 512], F)
-SEMAPHORES = (["q_v", "q_s", "q_t", "q_g"] + ["d_" + n for n in ("x", "m", "o", "nb", "th", "od", "ow", "ym", "yo")]
+    SCRATCH[_p] = ("psum", [128, 1024], B) if _p == "PB" else ("psum", [128, 512], F)
+SEMAPHORES = (["q_v", "q_s", "q_t", "q_g"] + ["d_" + n for n in ("x", "m", "o", "nb", "th", "ow", "ym", "yo")]
               + [n + str(t) for n in ("al", "ae", "sl", "se") for t in range(RO)])
+ON_SCALAR = (False, False)
+WAKE, HOP, ISSUE = 70, 2500, 900
 
 
 def rank_program(g, core, T, topo):
@@ -28,148 +31,136 @@ def rank_program(g, core, T, topo):
         return
     N = len(T.cores)
     Q = {"v": g.vector, "s": g.scalar, "t": g.tensor, "g": g, "y": g.sync}
-    done = {n: 0 for n in SEMAPHORES}
-    know = {q: {} for q in Q}
-    clock = {}
-    acc = {}
+    nodes = []
+    acc, bank = {}, {}
 
-    def A(name, c0=0, c1=None, st=1, p0=None, p1=None):
+    def A(name, c0=0, c1=None, st=1, p=None):
         t = T[name]
         c1 = t.shape[1] if c1 is None else c1
-        ps = slice(None) if p0 is None else slice(p0, p1)
-        return (t[ps, slice(c0, c1) if st == 1 else slice(c0, c1, st)], [(name, c0, c1)])
+        ps = slice(None) if p is None else slice(0, p)
+        return (t[ps, slice(c0, c1) if st == 1 else slice(c0, c1, st)], [(name, c0, c1)], (c1 - c0 + st - 1) // st,
+                SCRATCH[name][2] in (B, H, U), name in PSUM)
 
     def IND(win, off):
-        return (win[0].indirect(off[0]), win[1] + off[1])
+        return (win[0].indirect(off[0]), win[1] + off[1], 16 * off[2], False, False)
 
     def ext(t):
-        return (t, [])
+        return (t, [], 0, False, False)
 
-    def conflicts(q, reads, writes):
-        need = {}
+    def val(s):
+        return s[0] if isinstance(s, tuple) else s
+
+    def node(q, call, writes, reads, ns, sem=None, n=1, hold=None, after=()):
+        me = {"q": q, "call": call, "ns": ns, "hold": ns if hold is None else hold, "sem": sem or "q_" + q, "n": n,
+              "dep": set(), "ord": set(after), "i": len(nodes)}
         for regs, wr in ((reads, False), (writes, True)):
             for (b, c0, c1) in regs:
-                for (aq, aw, a0, a1, sem, val) in acc.get(b, []):
-                    if b in PSUM:
-                        if aq == q and (q == "t" or not aw or a1 <= c0 or a0 >= c1):
-                            continue
-                    elif not (aw or wr) or a1 <= c0 or a0 >= c1:
+                if b in PSUM:
+                    e = bank.setdefault(b, [q, [], []])
+                    if e[0] != q:
+                        e[:] = [q, [], e[1]]
+                        acc[b] = []
+                    me["dep"].update(e[2])
+                    if q == "t":
+                        me["ord"].update(e[1][-1:])
+                    e[1].append(me["i"])
+                    if q == "t":
                         continue
-                    need[sem] = max(need.get(sem, 0), val)
-        return need
-
-    def wait(q, sem, val):
-        if know[q].get(sem, 0) >= val:
-            return
-        Q[q].wait_ge(T.sem[sem], val)
-        for k, v in clock.get((sem, val), {}).items():
-            know[q][k] = max(know[q].get(k, 0), v)
-        know[q][sem] = max(know[q].get(sem, 0), val)
-
-    def note(q, reads, writes, sem, val):
+                for (i, aw, a0, a1) in acc.get(b, []):
+                    if (aw or wr) and a1 > c0 and a0 < c1 and i != me["i"]:
+                        me["dep"].add(i)
         for regs, wr in ((writes, True), (reads, False)):
             for (b, c0, c1) in regs:
                 l = acc.setdefault(b, [])
-                if b in PSUM:
-                    l[:] = [x for x in l if x[0] == q and not (x[2] >= c0 and x[3] <= c1 and (wr or not x[1]))]
-                else:
-                    l[:] = [x for x in l if not (x[2] >= c0 and x[3] <= c1 and (wr or (x[0] == q and not x[1])))]
-                l.append((q, wr, c0, c1, sem, val))
+                if wr:
+                    l[:] = [x for x in l if not (x[2] >= c0 and x[3] <= c1)]
+                l.append((me["i"], wr, c0, c1))
+        me["dep"].discard(me["i"])
+        me["ord"].discard(me["i"])
+        nodes.append(me)
+        return me["i"]
 
-    def waits(q, reads, writes):
-        need = conflicts(q, reads, writes)
-        for s in sorted(need, key=lambda s: -sum(1 for o in need if o != s and clock.get((s, need[s]), {}).get(o, 0) >= need[o])):
-            wait(q, s, need[s])
-
-    def flat(l):
-        return [r for x in l for r in x[1]]
-
-    def emit(q, call, writes, reads, sem=None, n=1):
-        reads, writes = flat(reads), flat(writes)
-        waits(q, reads, writes)
-        sem = sem or "q_" + q
-        done[sem] += n
-        call().then_inc(T.sem[sem], n)
-        clock[(sem, done[sem])] = dict(know[q])
-        note(q if n == 1 else "d" + sem, reads, writes, sem, done[sem])
-
-    def w_emit(q, call, out, reads):
-        emit(q, call, [(None, out[1][:1])], list(reads) + [(None, out[1][1:])])
+    def vec(call, out, full, cols, rate):
+        ins = full + [c for c in cols if isinstance(c, tuple)]
+        n = full[0][2] if full else out[2]
+        if len(out[1]) > 1:
+            ns = 50 + 3.2 * n
+        elif full and len(full[0][1]) > 1:
+            ns = 50 + 1.3 * n
+        else:
+            ns = 0.83 * max(64, n * rate * (0.5 if all(x[3] for x in full + [out]) else 1))
+        return node("v", call, out[1][:1], [r for x in ins for r in x[1]] + out[1][1:], ns)
 
     def cp(out, i):
-        w_emit("v", lambda: g.vector.tensor_copy(out[0], i[0]), out, [i])
+        return vec(lambda: g.vector.tensor_copy(out[0], i[0]), out, [i], [], 1)
 
     def tt(out, a, b, op):
-        w_emit("v", lambda: g.vector.tensor_tensor(out[0], a[0], b[0], op), out, [a, b])
+        return vec(lambda: g.vector.tensor_tensor(out[0], a[0], b[0], op), out, [a, b], [], 1 if a[4] or b[4] else 2)
 
     def ts(out, a, s1, op0, s2=None, op1=None):
-        col = [s1] if isinstance(s1, tuple) else []
-        v = s1[0] if col else s1
         if op1 is None:
-            w_emit("v", lambda: g.vector.tensor_scalar(out[0], a[0], v, None, op0), out, [a] + col)
-        else:
-            w_emit("v", lambda: g.vector.tensor_scalar(out[0], a[0], v, s2, op0, op1), out, [a] + col)
+            return vec(lambda: g.vector.tensor_scalar(out[0], a[0], val(s1), None, op0), out, [a], [s1], 1)
+        return vec(lambda: g.vector.tensor_scalar(out[0], a[0], val(s1), val(s2), op0, op1), out, [a], [s1, s2], 1)
 
     def scan(out, d0, d1, op0, op1, init=0.0):
-        w_emit("v", lambda: g.vector.tensor_tensor_scan(out[0], d0[0], d1[0], init, op0, op1), out, [d0, d1])
+        return vec(lambda: g.vector.tensor_tensor_scan(out[0], d0[0], d1[0], init, op0, op1), out, [d0, d1], [], 1)
 
     def fill(out, c):
-        w_emit("v", lambda: g.vector.memset(out[0], c), out, [])
+        return vec(lambda: g.vector.memset(out[0], c), out, [], [], 1)
 
-    def act(out, i, func, bias=0.0, scale=1.0, accum=None):
-        emit("s", lambda: g.scalar.activation(out[0], i[0], func, bias=bias, scale=scale, accum_out=accum and accum[0]), [out] + ([accum] if accum else []), [i])
+    def act(out, i, func, bias=0.0, scale=1.0, after=()):
+        return node("s", lambda: g.scalar.activation(out[0], i[0], func, bias=val(bias), scale=scale), out[1],
+                    i[1] + (bias[1] if isinstance(bias, tuple) else []), 65 + i[2] * (1.3 if len(i[1]) > 1 else 0.83), after=after)
 
     def mm(out, l, r, start=False, stop=False):
-        emit("t", lambda: g.tensor.matmul(out[0], l[0], r[0], start, stop), [out], [l, r])
+        return node("t", lambda: g.tensor.matmul(out[0], l[0], r[0], start, stop), out[1], l[1] + r[1], 10 + 0.42 * max(min(64, l[2]), r[2]))
+
+    def turn(out, src):
+        return node("t", lambda: g.tensor.transpose(out[0], src[0], A("IDF")[0]), out[1], src[1] + A("IDF")[1], 225)
 
     def aff(out, i, pat, op, fl, base, cm):
-        emit("g", lambda: g.affine_select(out[0], i[0], pat, op, fl, base, cm), [out], [i])
+        return node("g", lambda: g.affine_select(out[0], i[0], pat, op, fl, base, cm), out[1], i[1], 170 + 1.66 * out[2])
 
-    def iota(out, pat, cm):
-        emit("g", lambda: g.iota(out[0], pat, 0, cm, allow_small_or_imprecise_dtypes=True), [out], [])
+    def iota(out, pat, cm, base=0):
+        return node("g", lambda: g.iota(out[0], pat, base, cm, allow_small_or_imprecise_dtypes=True), out[1], [], 130 + 1.66 * out[2])
 
-    def dma(q, out, i, sem):
-        emit(q, lambda: Q[q].dma_start(out[0], i[0]), [out], [i], sem, 16)
-
-    def dmas(q, calls, out, i, sem):
-        waits(q, flat(i), out[1])
-        for call in calls:
-            call().then_inc(T.sem[sem], 16)
-        done[sem] += 16 * len(calls)
-        clock[(sem, done[sem])] = dict(know[q])
-        note("d" + sem, flat(i), out[1], sem, done[sem])
+    def dma(q, out, i, sem, ns, after=()):
+        return node(q, lambda: Q[q].dma_start(out[0], i[0]), out[1], i[1], ns, sem, 16, ISSUE if q == "g" else 60, after)
 
     def lanes(src, dst):
         return topo.engines(src, dst)[:8]
 
-    def send(dst, out, i, rsem, lsem):
+    def swap(dst, src, land, i, rsem, lsem):
         rid, pid = topo.addr(dst)[:2]
         eng = lanes(core, dst)
-        waits("g", i[1], [])
-        g.remote_dma(out[0], i[0], T.sem[rsem], T.sem[lsem], pid, rid, sum(1 << e for e in eng))
-        done[lsem] += len(eng)
-        clock[(lsem, done[lsem])] = dict(know["g"])
-        note("r" + lsem, i[1], [], lsem, done[lsem])
 
-    def arrives(name, rsem, src):
-        done[rsem] += len(lanes(src, core))
-        note("n" + rsem, [], A(name)[1], rsem, done[rsem])
+        def call():
+            g.remote_dma(A(land)[0], i[0], T.sem[rsem], T.sem[lsem], pid, rid, sum(1 << e for e in eng))
+        s = node("g", call, [], i[1], HOP, lsem, len(eng), ISSUE)
+        node("n", None, A(land)[1], [], HOP + (2500 if land == "LI0" else 0), rsem, len(lanes(src, core)), 0, [s])
 
     fill(A("THC"), 0)
-    dma("y", A("XW", 0, S), ext(T.x0[:]), "d_x")
-    dma("s", A("MI"), ext(T.m0[:]), "d_m")
-    dma("s", A("NI"), ext(T.own0[:]), "d_o")
-    dmas("y", [lambda r=r: g.sync.dma_start(T.THC[r::16, 0:1], T.th[:]) for r in range(2)], A("THC"), [], "d_th")
-    dma("y", A("NBW"), ext(T.nb[:]), "d_nb")
+    x = dma("y", A("XW", 0, S), ext(T.x0[:]), "d_x", 6000)
+    dma("s", A("MI"), ext(T.m0[:]), "d_m", 2200)
+    dma("s", A("NI"), ext(T.own0[:]), "d_o", 2400)
+    dma("y", (T.THC[0::16, 0:1], A("THC")[1]), ext(T.th[:]), "d_th", 2200)
+    dma("y", A("NBW"), ext(T.nb[:]), "d_nb", 12000, [x])
+    cp(A("ML"), A("MI"))
+    swap(T.cores[(rank + 1) % N], T.cores[(rank - 1) % N], "LI0", A("ML"), "al0", "sl0")
+    fill(A("OWN"), 0.0)
+    cp(A("CB"), A("NI"))
+    dma("g", (T.OWN[0::16, 0:S], A("OWN", 0, S)[1]), A("CB"), "d_ow", 3000)
     fill(A("ONE"), 1.0)
     iota(A("CM"), [[0, 16], [1, 16]], 0)
     iota(A("WI"), [[0, 1]], 1)
-    aff(A("IDB"), A("ONE"), [[-1, 128]], OP.is_equal, 0.0, 0, 1)
+    aff(A("IDB"), A("ONE", 0, 128), [[-1, 128]], OP.is_equal, 0.0, 0, 1)
     aff(A("WB"), A("ONE", 0, 32), [[0, 4], [-16, 8]], OP.is_ge, 0.0, 0, 1)
     aff(A("WB"), A("WB"), [[0, 4], [16, 8]], OP.is_ge, 0.0, 15, -1)
-    aff(A("BO"), A("ONE"), [[-16, 8], [0, 16]], OP.is_ge, 0.0, 0, 1)
+    aff(A("BO"), A("ONE", 0, 128), [[-16, 8], [0, 16]], OP.is_ge, 0.0, 0, 1)
     aff(A("BO"), A("BO"), [[16, 8], [0, 16]], OP.is_ge, 0.0, 15, -1)
-    iota(A("AI0"), [[16, 16]], 0)
+    iota(A("ALD"), [[S - L, 2], [16, 16]], 0, L)
+    for c in range(256, 3200, 368):
+        iota(A("EQ", c, c + 368), [[0, 368]], 0)
     fill(A("MHALF"), -0.5)
     ts(A("SM1", 0, 256), A("CM"), 0.0, OP.not_equal)
     ts(A("SM2", 0, 256), A("CM"), 0.0, OP.is_equal, 1024.0, OP.mult)
@@ -177,387 +168,373 @@ def rank_program(g, core, T, topo):
         for n in ("SM1", "SM2"):
             cp(A(n, c, 2 * c), A(n, 0, c))
     ts(A("WJ"), A("WI"), 15, OP.bitwise_and)
-    ts(A("IDH"), A("IDB"), 0.5, OP.mult)
+    cp(A("PI"), A("WI"))
     cp(A("KC"), A("WJ"))
-    cp(A("ML"), A("MI"))
-    arrives("LI0", "al0", T.cores[(rank - 1) % N])
-    send(T.cores[(rank + 1) % N], A("LI0"), A("ML"), "al0", "sl0")
-    cp(A("CB"), A("NI"))
-    dma("y", (T.OD[:], [("OD", 0, S)]), A("CB"), "d_od")
-    dmas("y", [lambda r=r: g.sync.dma_start(T.OWN[r::16, 0:S], T.OD[:]) for r in range(16)], A("OWN", 0, S), [("", [("OD", 0, S)])], "d_ow")
-    ts(A("IDN"), A("IDB"), -1.0, OP.mult)
-    ts(A("WID", 0, 16), A("WB", 0, 16), 1024.0, OP.mult)
-    ts(A("WID", 16, 24), A("WB", 0, 8), -64.0, OP.mult)
-    ts(A("WID", 24, 32), A("WB", 0, 8), 64.0, OP.mult)
-    ts(A("WER", 0, 16), A("WB", 0, 16), -1024.0, OP.mult)
-    ts(A("WER", 16, 32), A("WB", 0, 16), 1024.0, OP.mult)
-    ts(A("WRD"), A("WB", 0, 8), -64.0, OP.mult)
-    ts(A("WIX"), A("WID"), 2.0, OP.mult)
-    ts(A("WIG"), A("WID"), -1.0, OP.mult)
-    ts(A("WEX"), A("WER"), -2.0, OP.mult)
-    fill(A("SEL"), 0.0)
-    fill(A("SELR"), 0.0)
+    ts(A("NKC"), A("KC"), -1.0, OP.mult)
+    ts(A("ALD"), A("ALD"), A("KC"), OP.add)
     ts(A("R16"), A("CM", 0, 16), A("KC"), OP.is_equal)
-    ts(A("LJT", 0, 128), A("CM", 0, 128), A("R16", 0, 1), OP.mult)
-    aff(A("LJT", 0, 128), A("LJT", 0, 128), [[0, 128]], OP.is_equal, 0.0, 0, 1)
+    for name, w in (("IDH", 0.5), ("IDN", -1.0), ("IDQ", -16384.0), ("ID16", 1.0), ("IDF", 1.0)):
+        ts(A(name), A("IDB"), w, OP.mult)
+    ts(A("IDS", 0, 128), A("IDB"), -64.0, OP.mult)
+    cp(A("IDS", 128, 256), A("IDB"))
+    for c, n, w in ((0, 16, -1024.0), (16, 8, 64.0), (24, 8, -64.0)):
+        ts(A("WIG", c, c + n), A("WB", 0, n), w, OP.mult)
+    for c, w in ((0, -1024.0), (16, 1024.0)):
+        ts(A("WNG", c, c + 16), A("WB", 0, 16), w, OP.mult)
+    for name, src, w in (("WIX", "WIG", -2.0), ("WNX", "WNG", -2.0), ("WRG", "WNG", -1.0), ("WRX", "WNG", 2.0)):
+        ts(A(name), A(src), w, OP.mult)
+    for c, w in ((0, 64.0), (8, -128.0), (16, -64.0)):
+        ts(A("WK", c, c + 8), A("WB", 0, 8), w, OP.mult)
+    ts(A("NC"), A("BO"), -1024.0, OP.mult)
     ts(A("SMF", 0, 256), A("CM"), 0.0, OP.is_equal, BIG, OP.mult)
-    ts(A("SMA"), A("CM"), 0.0, OP.not_equal)
-    ts(A("DG"), A("CM"), A("KC"), OP.is_equal)
+    cp(A("SMF", 256, 512), A("SMF", 0, 256))
+    ts(A("DGA"), A("CM"), A("KC"), OP.is_equal)
+    ts(A("DGA"), A("DGA"), 1001.0, OP.mult, -1000.0, OP.add)
+    ts(A("R0"), A("ONE", 0, 128), A("R16", 0, 1), OP.mult)
+    ts(A("R0B"), A("BO"), A("R16", 0, 1), OP.mult)
 
-    def late_constants():
-        ts(A("JC", 0, 128), A("LJT", 0, 128), 64.0, OP.mult)
-        ts(A("JC", 128, 256), A("LJT", 0, 128), 64.0, OP.mult)
-        cp(A("JC", 256, 384), A("LJT", 0, 128))
-        cp(A("JC", 384, 512), A("LJT", 0, 128))
-        cp(A("IDF"), A("IDB"))
-        ts(A("DGA"), A("DG"), 1001.0, OP.mult, -1000.0, OP.add)
-
-        def sel(name, i, row, weight):
-            o = A(name, 128 * i, 128 * i + 128)
-            aff(o, o, [[-1, 8], [0, 16]], OP.not_equal, weight, -row, 1)
-        for h in range(2):
-            sel("SEL", h, 16 * h, 1.0)
-            sel("SEL", h, 16 * h + 8, 64.0)
-        for h in range(2):
-            sel("SEL", 2 + h, 64 + 8 * h, 1.0)
-            sel("SEL", 4 + h, 80 + 8 * h, 1.0)
-            sel("SEL", 6 + h, 32 * h, 1.0)
-            sel("SEL", 6 + h, 32 * h + 8, 64.0)
-            sel("SEL", 8 + h, 32 * h + 16, 1.0)
-            sel("SEL", 8 + h, 32 * h + 24, 64.0)
-            for i, c in ((6, 8192.0), (8, 4096.0)):
-                o = A("SEL", 128 * (i + h), 128 * (i + h) + 128)
-                aff(o, o, [[0, 128]], OP.not_equal, c, -96, 1)
-            sel("SELR", h, 8 * h, 1.0)
-        for r in range(16):
-            aff(A("ERC", 128 * r, 128 * r + 128), A("IDB"), [[-16, 8], [0, 16]], OP.is_equal, 0.0, -r, 1)
-
-    def later_constants():
-        ts(A("ALS"), A("AI0"), A("KC"), OP.add, float(S), OP.add)
-        ts(A("ALB"), A("AI0"), A("KC"), OP.add, float(L + 1), OP.add)
-        ts(A("LJT", 0, 128), A("CM", 0, 128), A("R16", 2, 3), OP.mult, 64.0, OP.mult)
-        aff(A("LJT", 0, 128), A("LJT", 0, 128), [[0, 128]], OP.is_equal, 0.0, -2, 1)
-        ts(A("LJT", 128, 256), A("BO"), A("R16", 1, 2), OP.mult, -1024.0, OP.mult)
-        for i in range(2):
-            ts(A("NC", 128 * i, 128 * i + 128), A("BO"), -1024.0, OP.mult)
-            ts(A("NC", 128 * i + 256, 128 * i + 384), A("BO"), 1024.0, OP.mult)
-        ts(A("IDC"), A("IDB"), 100.0, OP.mult)
-        fill(A("ONF"), 1.0)
-        fill(A("XW", S, S + L), 0.0)
-        fill(A("OWN", S, S + L), 0.0)
-        fill(A("CUM", 0, 16), 0.0)
-        fill(A("SELT"), 1.0)
-        tt(A("LJT", 128, 256), A("LJT", 128, 256), A("LJT", 0, 128), OP.add)
-        for i in range(8):
-            c = 128 * i
-            if i in (0, 6):
-                ts(A("LJ", c, c + 128), A("BO"), A("R16", 0, 1), OP.mult, -65536.0, OP.mult)
-                tt(A("LJ", c, c + 128), A("LJ", c, c + 128), A("LJT", 128, 256), OP.add)
+    def rows(c, *parts):
+        o = A("COL", c, c + 1)
+        for i, (r, w) in enumerate(parts):
+            if i == 0:
+                ts(o, A("IDF", r, r + 1), w, OP.mult)
             else:
-                cp(A("LJ", c, c + 128), A("LJT", 0, 128))
-        cp(A("SMF", 256, 512), A("SMF", 0, 256))
-
-    later = []
-
-    def some(n):
-        for _ in range(min(n, len(later))):
-            later.pop(0)()
-
-    def limits(first):
-        if first:
-            later.append(lambda: cp(A("TE"), A("THC")))
+                ts(o, A("IDF", r, r + 1), w, OP.mult, o, OP.add)
+        return o
+    k64, k1 = rows(0, (1, 64.0)), A("IDF", 1, 2)
+    lo, hi = rows(1, (2, -31.5), (3, 10304.0)), rows(2, (2, -31.5), (3, -129.0))
+    lim = A("COL", 3, 4)
+    ts(lim, A("IDF", 4, 5), 32768.0, OP.mult, lo, OP.add)
+    cm = A("CM", 0, 128)
+    ts(A("JC", 0, 128), cm, k64, OP.mult, lo, OP.add)
+    ts(A("JC", 128, 256), cm, k64, OP.mult, hi, OP.add)
+    ts(A("JC", 256, 512), A("CM"), k1, OP.mult)
+    ts(A("RT"), cm, k64, OP.mult, lim, OP.add)
+    ts(A("RR"), A("R0B"), -1024.0, OP.mult)
+    for i in range(6):
+        o = A("LJ", 128 * i, 128 * i + 128)
+        if i % 4 == 0:
+            tt(o, A("RT"), A("RR"), OP.add)
         else:
-            later.append(lambda: cp(A("WI"), A("P6", 0, 1)))
-            later.append(lambda: ts(A("WJ"), A("WI"), 4, OP.logical_shift_right, 63, OP.bitwise_and))
-            later.append(lambda: tt(A("TE"), A("THC"), A("WJ"), OP.add))
-        later.append(lambda: ts(A("THI"), A("TE"), 6, OP.logical_shift_right))
-        later.append(lambda: ts(A("TLO"), A("TE"), 63, OP.bitwise_and))
-        later.append(lambda: tt(A("TA"), A("THI"), A("R16", 0, 1), OP.mult))
-        later.append(lambda: tt(A("TB"), A("TLO"), A("R16", 1, 2), OP.mult))
-        later.append(lambda: tt(A("TA"), A("TA"), A("TB"), OP.add))
-        later.append(lambda: tt(A("TB"), A("TA"), A("R16", 2, 3), OP.add))
-        later.append(lambda: ts(A("THB"), A("ONE"), A("TB"), OP.mult))
+            cp(o, A("JC", 128 * (i % 2), 128 * (i % 2) + 128))
+    ones = A("COL", 4, 5)
+    ts(ones, A("R16", 4, 5), 63.0, OP.mult, 1.0, OP.add)
+    tt(ones, ones, A("R16", 0, 1), OP.subtract)
+    tt(A("CM2"), cm, cm, OP.mult)
+    ts(A("CZ", 0, 128), A("CM2"), rows(5, (1, -16384.0)), OP.mult, rows(6, (2, 8192.0), (3, 2016.0), (4, 31.5)), OP.add)
+    ts(A("CZ", 128, 256), A("ONE", 0, 128), rows(7, (2, 4096.0), (3, 2016.0), (4, 31.5)), OP.mult)
+    ts(A("KW"), cm, 32768.0, OP.mult)
+    ts(A("CC", 0, 16), A("ONE", 0, 16), A("IDF", 0, 1), OP.mult, -1.0, OP.mult)
+    ts(A("CC", 16, 32), A("ONE", 0, 16), A("IDF", 0, 1), OP.mult, 2048.0, OP.mult)
+    magic = A("COL", 8, 9)
+    ts(magic, A("PI"), 80.0, OP.is_ge, 1.5 * 2 ** 40 - M64, OP.mult)
+    ts(magic, magic, M64, OP.add)
+    fill(A("XW", S, S + L), 0.0)
+    fill(A("CUM"), 0.0)
+    cp(A("AT", 256, 264), A("WB", 0, 8))
+    ts(A("AT", 264, 272), A("WB", 0, 8), 64.0, OP.mult)
+    for r in range(16):
+        ts(A("AT", 16 * r, 16 * r + 16), A("AT", 256, 272), A("R16", r, r + 1), OP.mult)
+        mm(A(PSUM[r // 4], 128 * (r % 4), 128 * (r % 4) + 128, 1, 16), A("AT", 16 * r, 16 * r + 16), A("IDB"), True, True)
+        if r % 4 == 3:
+            act(A("LM", 128 * r - 384, 128 * r + 128, 1, 16), A(PSUM[r // 4], 0, 512, 1, 16), AF.Copy)
 
-    def six(lst):
-        later.append(lambda: cp(A("NI"), A(lst)))
-        later.append(lambda: ts(A("NJ"), A("NI"), 63, OP.bitwise_and))
-        later.append(lambda: ts(A("M2"), A("NI"), 6, OP.logical_shift_right))
-        later.append(lambda: cp(A("MLO"), A("NJ")))
-        later.append(lambda: cp(A("MHI"), A("M2")))
-
-    def gather(q, dst, lst, c):
-        out, src = A(dst, 1024 * c, 1024 * c + 1024), IND(A("XW", 0, S), A(lst, 64 * c, 64 * c + 64))
-        if q == "v":
-            cp(out, src)
+    def sel(i, row, step, weight=None, src=None):
+        o = A("SEL", 128 * i, 128 * i + 128)
+        if src:
+            aff(o, A(src, 0, 128), [[-step, 8], [0, 16]], OP.is_equal, 0.0, -row, 1)
         else:
-            act(out, src, AF.Copy)
+            aff(o, o, [[-step, 8], [0, 16]], OP.not_equal, weight, -row, 1)
+    for h in range(2):
+        sel(4 + h, 8 * h, 1, src="ONE")
+        sel(h, 64 + h, 2, src="KW")
+        for row, w in ((0, 1.0), (16, 64.0), (80, -16384.0), (96, -16384.0)):
+            sel(h, row + h, 2, w)
+        sel(2 + h, 32 + h, 2, src="ONE")
+        sel(2 + h, 48 + h, 2, 64.0)
 
-    def scans(src, c, n=0):
-        o = 1024 * c
-        scan(A("S1", o, o + 1024), A("SM1"), A(src, o, o + 1024), OP.mult, OP.max)
-        some(n)
-        scan(A("S2", o, o + 1024), A("SM2"), A(src, o, o + 1024), OP.add, OP.min, BIG)
-        some(n)
+    setup = len(nodes)
+    chain = []
 
-    def centre(dst, a0, n):
-        for a in range(a0, a0 + n, 128):
-            p = A("P2", a - a0, a - a0 + 128)
-            mm(p, A("IDH"), A("S1", 16 * a + 15, 16 * a + 2048, 16), True, False)
-            mm(p, A("IDH"), A("S2", 16 * a + 15, 16 * a + 2048, 16))
-            mm(p, A("IDH"), A("MHALF"), False, True)
-        ts(A(dst, a0, a0 + n), A("P2", 0, n), float(2 ** 23), OP.add, -float(2 ** 23), OP.add)
+    def gather(dst, lst, h):
+        for c in (2 * h, 2 * h + 1):
+            chain[:] = [act(A(dst, 1024 * c, 1024 * c + 1024), IND(A("XW", 0, S), A(lst, 64 * c, 64 * c + 64)), AF.Copy, after=chain)]
 
-    turn = [0]
+    def centre(src, h, slot):
+        for c in range(2):
+            o, i = 2048 * slot + 1024 * c, A(src, 2048 * h + 1024 * c, 2048 * h + 1024 * c + 1024)
+            scan(A("S1", o, o + 1024), A("SM1"), i, OP.mult, OP.max)
+            scan(A("S2", o, o + 1024), A("SM2"), i, OP.add, OP.min, BIG)
+        p = A("P4", 128 * slot, 128 * slot + 128)
+        mm(p, A("IDH"), A("MHALF"), True, False)
+        mm(p, A("IDH"), A("S1", 2048 * slot + 15, 2048 * slot + 2048, 16))
+        mm(p, A("IDH"), A("S2", 2048 * slot + 15, 2048 * slot + 2048, 16), False, True)
+        return p
 
-    def diff(src, cen, h, b, banks, hold=False):
-        bank = banks[turn[0] % len(banks)]
-        turn[0] += 1
-        for k in range(4):
-            o = A(bank, 128 * k, 128 * k + 128)
-            mm(o, A("IDB"), A(src, 2048 * h + 4 * b + k, 2048 * (h + 1), 16), True, False)
-            mm(o, A("IDN"), A(cen, 128 * h, 128 * h + 128), False, True)
+    def whole(out, p):
+        ts(out, p, float(2 ** 23), OP.add, -float(2 ** 23), OP.add)
 
-        def out():
-            act(A("DI", 2048 * h + 512 * b, 2048 * h + 512 * b + 512), A(bank), AF.Abs)
-        return out if hold else out()
+    def half(name, h, o=0):
+        return A(name, o + 128 * h, o + 128 * h + 128)
 
-    def sum_d(bank, h, b, w, n=32):
-        for k in range(4 * b, 4 * b + 4):
-            mm(A(bank, k, 16 * n, 16), A("DI", 2048 * h + 128 * k, 2048 * h + 128 * k + 128), A(w), False, k == 15)
+    def six(lst, ms, hi_, h):
+        ts(half(ms, h), half(lst, h), -2048.0, OP.add)
+        ts(half(hi_, h), half(lst, h), 1 / 64, OP.mult, 129 - 31.5 / 64, OP.add)
 
-    def sum_g(bank, src, h, w):
+    def sites(bk, o, ms, hi_, h):
+        mm(A(bk, o, o + 128), half(ms, h), A("ID16"))
+        mm(A(bk, o, o + 256), half(hi_, h), A("IDS"))
+
+    def sums(bk, o, src, h, w):
         for k in range(16):
-            mm(A(bank, k, 512, 16), A(src, 2048 * h + k, 2048 * (h + 1), 16), A(w))
+            mm(A(bk, o + k, o + 16 * w[2], 16), A(src, 2048 * h + k, 2048 * (h + 1), 16), w)
 
-    def sum_x(bank, h, k, w):
-        mm(A(bank, k, 512, 16), A("MX", 256 * k + 128 * h, 256 * k + 128 * h + 128), A(w), False, k == 15)
+    def larger(bk, o, src, h, cen, mx, w):
+        for k in range(16):
+            m = A(mx, 2048 * h + 128 * k, 2048 * h + 128 * k + 128)
+            tt(m, A(src, 2048 * h + k, 2048 * (h + 1), 16), half("PB", h, cen), OP.max)
+            mm(A(bk, o + k, o + 16 * w[2], 16), m, w, False, k == 15)
 
-    def turned(n, bank, src):
-        o = A(bank, 0, 128, 1, 0, n)
-        emit("t", lambda: g.tensor.transpose(o[0], src[0], A("IDF")[0]), [o], [src, A("IDF")])
+    def low(out, r, p, m=M64):
+        ts(r, p, m, OP.add, m, OP.subtract)
+        tt(out, p, r, OP.subtract)
 
-    def low(n, bank, mask, x="T"):
-        cp(A(x + "T", 0, 128, 1, 0, n), A(bank, 0, 128, 1, 0, n))
-        ts(A(x + "U", 0, 128, 1, 0, n), A(x + "T", 0, 128, 1, 0, n), mask, OP.bitwise_and)
-        cp(A(x + "P", 0, 128, 1, 0, n), A(x + "U", 0, 128, 1, 0, n))
+    def residents(h):
+        mm(half("P5", h), A("ONE", 0, 128), A("JC", 256, 384), True, False)
+        if not ON_SCALAR[h]:
+            cp(half("PB", h, 256), half("CR", h))
+            sums("P5", 128 * h, "GR", h, A("WK", 0, 8))
+            larger("P5", 128 * h, "GR", h, 256, "MXC", A("WK", 8, 16))
+            return
+        for b in range(4):
+            bk = ("P0", "P2")[b % 2]
+            for k in range(4):
+                o = A(bk, 128 * k, 128 * k + 128)
+                mm(o, A("IDB"), A("GR", 2048 * h + 4 * b + k, 2048 * (h + 1), 16), True, False)
+                mm(o, A("IDN"), half("CR", h), False, True)
+            act(A("DI", 512 * b, 512 * b + 512), A(bk), AF.Abs)
+        for k in range(16):
+            mm(A("P5", 128 * h + k, 128 * h + 128, 16), A("DI", 128 * k, 128 * k + 128), A("WK", 16, 24), False, k == 15)
 
-    def spread(bank, o, name, i, n, start=True, x="TP"):
-        for h in range(2):
-            mm(A(bank, o + 128 * h, o + 128 * h + 128), A(name, 128 * (i + h), 128 * (i + h) + 128, 1, 0, n), A(x, 0, 128, 1, 0, n), start, start or h == 1)
+    def lists(bk, o, n, src, c0, out):
+        p = A(bk, o, o + n)
+        for r in range(16):
+            mm(p, A("LM", 128 * r, 128 * r + 128, 1, 8), A(src, r, 16 * n, 16, 8), r == 0, False)
+        if n == 32:
+            mm(A(bk, o, o + 16), A("IDB"), A("SC", 15, 256, 16))
+        mm(A(bk, o + n - 16, o + n), A("ID16"), A("SL16"))
+        mm(p, A("ONE", 0, 128), A("CC", 32 - n, 32), False, True)
+        tt(A("LF", out, out + n), p, A("ALD", c0, c0 + n), OP.min)
+        cp(A("LD", out, out + n), A("LF", out, out + n))
 
-    off = [256 + sum(240 - 16 * d for d in range(c)) for c in range(15)]
+    def block(c):
+        return 256 + 256 * c if c < 8 else 2304 + 128 * (c - 8) - 128
 
-    def same(c0, c1):
-        for c in range(c0, c1):
-            some(1)
-            if c == 0:
-                tt(A("EQ", 0, 256), A("SC"), A("B1"), OP.is_equal)
-            else:
-                n = 256 - 16 * c
-                ts(A("EQ", off[c - 1], off[c - 1] + n), A("B1", 256 - n, 256), A("SC", 16 * c - 1, 16 * c), OP.is_equal)
-        some(9)
-
-    THREE, TWO, EB, NP = ["P0", "P1", "P6"], ["P0", "P1"], ["P0", "P1", "P2"], 3
-    seq = [(h, b) for h in range(2) for b in range(4)]
     for t in range(RO):
-        host = T.cores[(rank + 1 + t) % N]
-        guest = T.cores[(rank - 1 - t) % N]
+        last = t == RO - 1
+        host, guest = T.cores[(rank + 1 + t) % N], T.cores[(rank - 1 - t) % N]
         LI = "LI%d" % t
-        turn[0] = 0
-        for c in range(4):
-            gather("v" if c == 1 else "s", "GR", "ML", c)
-            if t > 0 and c == 1:
-                act(A("SD"), A("PW"), AF.Copy, accum=A("WC"))
-                mm(A("P6", 0, 1), A("ONF"), A("WC"), True, True)
-        for c in range(4):
-            gather("s", "GI", LI, c)
-        for c in (1, 0, 2, 3):
-            scans("GR", c, 3)
-            if c == 0:
-                if t == 0:
-                    late_constants()
-                six(LI)
-                if t == 0:
-                    limits(True)
-        some(99)
-        if t > 0:
-            limits(False)
-        centre("CR", 0, 256)
-        scans("GI", 0)
-        scans("GI", 1)
-        centre("CI", 0, 128)
-        for h in range(2):
-            mm(A(PSUM[3 + h]), A("ONE"), A("JC"), True, False)
-            mm(A(PSUM[3 + h], 0, 128), A("MLO", 128 * h, 128 * h + 128), A("IDB"))
-            mm(A(PSUM[3 + h], 128, 256), A("MHI", 128 * h, 128 * h + 128), A("IDB"))
-        some(2)
-        scans("GI", 2)
-        scans("GI", 3)
-        diff("GI", "CI", 0, 0, THREE)
-        diff("GI", "CI", 0, 1, THREE)
-        diff("GI", "CI", 0, 2, THREE)
-        centre("CI", 128, 128)
-        mm(A("P7", 0, 128), A("IDB"), A("CI", 128, 256), True, True)
-        diff("GI", "CI", 0, 3, THREE)
-        sum_g("P4", "GI", 1, "WIG")
-        for k in range(16):
-            tt(A("MX", 256 * k + 128, 256 * k + 256), A("GI", 2048 + k, 4096, 16), A("P7", 0, 128), OP.max)
-        for b in range(4):
-            sum_d("P3", 0, b, "WID")
-            for k in range(4 * b, 4 * b + 4):
-                sum_x("P4", 1, k, "WIX")
-        for h in range(2):
-            scan(A("KSC", 256 * h, 256 * h + 256), A("SMF", 0, 256), A(PSUM[3 + h], 0, 256), OP.add, OP.min, BIG)
-        diff("GR", "CR", 0, 0, THREE)
-        turned(32, "P2", A("KSC", 15, 512, 16))
-        some(4)
-        low(32, "P2", 63)
-        some(2)
-        diff("GR", "CR", 0, 1, THREE)
-        spread("P2", 0, "SEL", 0, 32)
-        diff("GR", "CR", 0, 2, THREE)
-        tt(A("SD"), A("P2", 0, 256), A("DG"), OP.mult)
-        scan(A("SS"), A("SMA"), A("SD"), OP.mult, OP.add)
-        cp(A("LS"), A("SS", 15, 256, 16))
-        cp(A("NL"), IND(A("NBW"), A("LS")))
-        some(99)
-        mm(A("P5", 0, 128), A("ONE"), A("JC", 256, 384), True, False)
-        sum_d("P5", 0, 0, "WRD", 8)
-        diff("GR", "CR", 0, 3, THREE)
-        for b in range(1, 4):
-            sum_d("P5", 0, b, "WRD", 8)
-        for c in range(4):
-            gather("s", "GN", "NL", c)
-        tt(A("SCM"), IND(A("OWN", 0, S), A("LS")), A("DGA"), OP.add)
-        ts(A("B1"), IND(A("OWN", 0, S), A("LS")), 1.0, OP.add)
-        scan(A("KSO", 0, 256), A("SMF", 0, 256), A("P3", 256, 512), OP.add, OP.min, BIG)
-        scan(A("SC"), A("SM1", 0, 256), A("SCM"), OP.mult, OP.max)
-        scan(A("KSO", 256, 512), A("SMF", 0, 256), A("P4", 256, 512), OP.add, OP.min, BIG)
-        ts(A("LB"), A("SC", 15, 256, 16), -1.0, OP.add)
-        scan(A("KSR", 0, 128), A("SMF", 0, 128), A("P5", 0, 128), OP.add, OP.min, BIG)
-        cp(A("CB"), IND(A("CR"), A("LB")))
-        mm(A("P7", 256, 512), A("IDB"), A("CI"), True, True)
         if t == 0:
-            later_constants()
-        for i in range(4):
-            mm(A(PSUM[3 + i]), A("THB"), A("LJ", 512 * (i // 2), 512 * (i // 2) + 512), True, False)
-            if i < 2:
-                mm(A(PSUM[3 + i]), A("CI", 128 * i, 128 * i + 128), A("NC"))
-        six("NL")
-        same(0, 4)
-        for i in range(4):
-            for j in range(4):
-                mm(A(PSUM[3 + i], 128 * j, 128 * j + 128), A("MHI" if j % 2 else "MLO", 128 * (i % 2), 128 * (i % 2) + 128), A("IDB"))
-        for b in range(NP):
-            diff("GN", "CB", 0, b, EB)
-        sum_g("P3", "GN", 0, "WER")
-        same(4, 16)
-        for h in range(2):
-            tt(A("DD", 64 + 8 * h, 72 + 8 * h), A("KSO", 256 * h + 15, 256 * h + 128, 16), A("KSO", 256 * h + 143, 256 * h + 256, 16), OP.subtract)
-        ts(A("DBA"), A("B1"), 256.0, OP.is_equal, -256.0, OP.mult)
-        for i, (h, b) in enumerate(seq):
-            if i == 1:
-                sum_g("P4", "GN", 1, "WER")
-            if 0 < i < 9 - NP:
-                diff("GN", "CB", seq[i + NP - 1][0], seq[i + NP - 1][1], EB)
-            for k in (2 * i, 2 * i + 1):
-                tt(A("MX", 256 * k, 256 * k + 256), A("GN", k, 16 * L, 16), A("P7", 256, 512), OP.max)
-                for hh in range(2):
-                    sum_x(PSUM[3 + hh], hh, k, "WEX")
-            sum_d(PSUM[5 + h], h, b, "WER")
-        held = [diff("GR", "CR", 1, b, TWO, True) for b in range(2)]
-        mm(A("P2", 0, 256), A("BO"), A("EQ", 0, 256), True, False)
-        for c in range(15):
-            n = 240 - 16 * c
-            mm(A("P2", 256 - n, 256), A("BO"), A("EQ", off[c], off[c] + n), False, c == 14)
-        tt(A("SCR", 0, 16), A("ALS"), A("SS", 15, 256, 16), OP.subtract)
-        tt(A("SCR", 32, 48), A("ALB"), A("SC", 15, 256, 16), OP.subtract)
-
-        def fam(o, bank, c):
-            act(A("FAM", o, o + 128), A(bank, c, c + 128), AF.Sign, -0.5, -1.0)
-
-        def key(out, h, bank):
-            scan(A(out, 512 * h, 512 * h + 512), A("SMF"), A(bank), OP.add, OP.min, BIG)
-        key("EK", 0, "P5")
-        fam(128, "P4", 0)
-        key("EI", 0, "P3")
-        fam(256, "P5", 256)
-        fam(384, "P6", 256)
-        key("EI", 1, "P4")
-        fam(0, "P3", 0)
-        key("EK", 1, "P6")
-        mm(A("P7", 0, 128), A("ONE"), A("JC", 256, 384), True, False)
-        for out in held:
-            out()
-        act(A("OT"), A("P2", 0, 256), AF.Sign, -1.5)
-        act(A("NF"), A("OT"), AF.Identity, 0.5, 0.5)
-        for b in (2, 3):
-            diff("GR", "CR", 1, b, TWO)
-        for b in range(4):
-            sum_d("P7", 1, b, "WRD", 8)
-        act(A("B0W"), A("B1"), AF.Identity, -1.0)
-        act(A("DB"), A("DBA"), AF.Identity, 1.0)
-        act(A("FT"), A("NF"), AF.Identity, 1.0, -1.0)
-        act(A("ERW", 0, L), A("SS"), AF.Identity, 0.0, 0.0)
-        tt(A("DD", 0, 64), A("EI", 15, 1024, 16), A("EK", 15, 1024, 16), OP.subtract)
-        scan(A("CUM", 16, 272), A("FAM", 0, 256), A("FAM", 256, 512), OP.add, OP.subtract)
-        tt(A("SELT", 80, 96), A("CUM", 31, 272, 16), A("CUM", 15, 256, 16), OP.is_gt)
-        for h in range(2):
-            for c in range(32 * h, 32 * h + 32, 8):
-                tt(A("TS", c, c + 8), A("DD", c, c + 8), A("SELT", 80 + 8 * h, 88 + 8 * h), OP.mult)
-        tt(A("DD", 64, 80), A("DD", 64, 80), A("SELT", 80, 96), OP.mult)
-        tt(A("SELT", 0, 64), A("TS"), A("EK", 15, 1024, 16), OP.add)
-        for h in range(2):
-            tt(A("SELT", 64 + 8 * h, 72 + 8 * h), A("DD", 64 + 8 * h, 72 + 8 * h), A("KSO", 256 * h + 143, 256 * h + 256, 16), OP.add)
-        turned(97, "P2", A("SELT", 0, 97))
-        scan(A("KSR", 128, 256), A("SMF", 0, 128), A("P7", 0, 128), OP.add, OP.min, BIG)
-        turned(16, "P4", A("KSR", 15, 256, 16))
-        low(97, "P2", 63)
-        low(16, "P4", 15, "R")
-        mm(A("P0", 0, 256), A("IDC"), A("NF"), True, False)
-        spread("P0", 0, "SEL", 2, 97, False)
-        spread("P0", 256, "SEL", 6, 97)
-        spread("P1", 0, "SEL", 8, 97)
-        spread("P1", 256, "SEL", 4, 97)
-        spread("P4", 256, "SELR", 0, 16, True, "RP")
-        for r in range(16):
-            mm(A("P5", 0, 16), A("ERC", 128 * r, 128 * r + 128), A("NF", r, 256, 16), r == 0, r == 15)
-        ts(A("OHI"), A("P0", 0, 256), A("KC"), OP.is_equal)
-        tt(A("EO"), A("OHI"), A("P0", 256, 512), OP.mult)
-        arrives("ER%d" % t, "ae%d" % t, host)
-        send(guest, A("ER%d" % t), A("EO"), "ae%d" % t, "se%d" % t)
-        act(A("KRW"), A("P4", 256, 512), AF.Copy)
-        act(A("KRB"), IND(A("KRW"), A("LB")), AF.Copy)
-        tt(A("SCR", 16, 32), A("SCR", 0, 16), A("P5", 0, 16), OP.mult)
-        tt(A("SCR", 48, 64), A("SCR", 32, 48), A("P5", 0, 16), OP.mult)
-        tt(A("SCR", 0, 16), A("SCR", 16, 32), A("SS", 15, 256, 16), OP.add)
-        tt(A("SCR", 32, 48), A("SCR", 48, 64), A("SC", 15, 256, 16), OP.add)
-        cp(A("LSD"), A("SCR", 0, 16))
-        ts(A("LBD"), A("SCR", 32, 48), -1.0, OP.add)
-        tt(A("OT"), A("DB"), A("P1", 256, 512), OP.mult)
-        if t < RO - 1:
-            act(A("XU"), IND(A("XW"), A("LSD")), AF.Relu, -float(WEAR))
-        ts(A("OHR"), A("KRB"), A("KC"), OP.is_equal)
-        tt(A("ERV"), A("OHR"), A("P1", 0, 256), OP.mult)
-        if t == RO - 1:
-            tt(IND(A("OWN"), A("LSD")), A("OT"), A("B0W"), OP.add)
-            dma("g", ext(T.yown[:]), (T.OWN[0::16, 0:S], [("OWN", 0, S)]), "d_yo")
-        cp(IND(A("ERW"), A("LBD")), A("ERV"))
-        if t < RO - 1:
-            tt(A("PW"), A("FT"), A("P1", 256, 512), OP.mult)
-        tt(A("M1"), A("MI"), A("ERW", 0, L), OP.max)
-        if t < RO - 1:
-            cp(IND(A("XW"), A("LSD")), A("XU"))
-            tt(IND(A("OWN"), A("LSD")), A("OT"), A("B0W"), OP.add)
-        tt(A("M2"), A("M1"), A("ER%d" % t), OP.max)
-        ts(A("MI"), A("M2"), 4095, OP.bitwise_and)
-        if t == RO - 1:
-            cp(A("PW"), A("MI"))
-            dma("y", ext(T.ym[:]), A("PW"), "d_ym")
+            cp(A("TE"), A("THC"))
         else:
-            cp(A("ML"), A("MI"))
-            arrives("LI%d" % (t + 1), "al%d" % (t + 1), T.cores[(rank - 2 - t) % N])
-            send(T.cores[(rank + 2 + t) % N], A("LI%d" % (t + 1)), A("ML"), "al%d" % (t + 1), "sl%d" % (t + 1))
+            cp(A("WI"), A("P3", 0, 1))
+            ts(A("WJ"), A("WI"), 63, OP.bitwise_and)
+            tt(A("TE"), A("THC"), A("WJ"), OP.add)
+        ts(A("TB"), A("TE"), 4081.0, OP.min, -2048.0, OP.add)
+        ts(A("THB"), A("R0"), A("TB"), OP.mult, ones, OP.add)
+        iota(A("ERW", 0, L), [[0, L]], 0)
+        gather("GR", "ML", 0)
+        whole(half("CR", 0), centre("GR", 0, 0))
+        if not ON_SCALAR[0]:
+            residents(0)
+        for h in range(2):
+            bk = PSUM[h]
+            gather("GI", LI, h)
+            whole(half("CI", h), centre("GI", h, 1 + h))
+            cp(half("PB", h), half("CI", h))
+            six(LI, "MSM", "HIM", h)
+            mm(A(bk), A("ONE", 0, 128), A("JC"), True, False)
+            sites(bk, 0, "MSM", "HIM", h)
+            sums(bk, 0, "GI", h, A("WIG"))
+            larger(bk, 0, "GI", h, 0, "MXA", A("WIX"))
+            scan(A("KSC", 256 * h, 256 * h + 256), A("SMF", 0, 256), A(bk, 0, 256), OP.add, OP.min, BIG)
+            p = A("P6", 0, 128, 1, 16)
+            turn(p, A("KSC", 256 * h + 15, 256 * h + 256, 16))
+            low(A("TM", 128 * h, 128 * h + 128, 1, 16), A("RM", 128 * h, 128 * h + 128, 1, 16), p)
+            p = A("P6", 128 + 8 * h, 136 + 8 * h)
+            for r in range(16):
+                mm(p, A("LM", 128 * r, 128 * r + 128, 1, 16), A("TM", 128 * h + r, 128 * h + 128, 16, 16), r == 0, r == 15)
+            ts(A("LS", 8 * h, 8 * h + 8), p, 2047.5, OP.add)
+            ts(A("SL16", 8 * h, 8 * h + 8), p, -0.5, OP.add)
+            cp(half("NL", h), IND(A("NBW"), A("LS", 8 * h, 8 * h + 8)))
+            scan(A("KSO", 256 * h, 256 * h + 256), A("SMF", 0, 256), A(bk, 256, 512), OP.add, OP.min, BIG)
+            low(A("KK", h, 32, 2), A("RK", 16 * h, 16 * h + 16), A("KSO", 256 * h + 15, 256 * h + 256, 16))
+        gather("GR", "ML", 1)
+        whole(half("CR", 1), centre("GR", 1, 3))
+        tt(A("DD", 64, 80), A("KK", 0, 16), A("KK", 16, 32), OP.subtract)
+        cp(A("B0"), IND(A("OWN", 0, S), A("LS")))
+        mm(A("P4", 0, 256), A("R0B"), A("B0"), True, True)
+        tt(A("SCM"), A("P4", 0, 256), A("DGA"), OP.add)
+        ts(A("B1"), A("P4", 0, 256), 1.0, OP.add)
+        scan(A("SC"), A("SM1", 0, 256), A("SCM"), OP.mult, OP.max)
+        ts(A("LB"), A("SC", 15, 256, 16), -1.0, OP.add)
+        cp(A("CB"), IND(A("CR"), A("LB")))
+        cp(A("PB", 512, 768), A("CB"))
+        ts(A("LT"), A("B1"), 256.0, OP.is_lt)
+
+        def neighbours(h):
+            gather("GN", "NL", h)
+            six("NL", "MSN", "HIN", h)
+            for bk, o, cen, wg in ((PSUM[h], 0, "CI", "WNG"), (PSUM[2 + h], 256, "CB", "WRG")):
+                mm(A(bk), A("THB"), A("LJ", o, o + 512), True, False)
+                for o2 in (0, 256):
+                    sites(bk, o2, "MSN", "HIN", h)
+                mm(A(bk, o, o + 128), half(cen, h), A("NC"))
+                sums(bk, 0, "GN", h, A(wg))
+            larger(PSUM[h], 0, "GN", h, 0, "MXA", A("WNX"))
+            larger(PSUM[2 + h], 0, "GN", h, 512, "MXB", A("WRX"))
+            act(half("FAM", h), A(PSUM[h], 0, 128), AF.Sign, 2.0 ** 22 - 32, -1.0)
+            act(half("FAM", h, 256), A(PSUM[2 + h], 256, 384), AF.Sign, 2.0 ** 22 - 32, -1.0)
+            scan(A("EI", 512 * h, 512 * h + 512), A("SMF"), A(PSUM[h]), OP.add, OP.min, BIG)
+            scan(A("EK", 512 * h, 512 * h + 512), A("SMF"), A(PSUM[2 + h]), OP.add, OP.min, BIG)
+            c = 144 * h
+            scan(A("CUM", c + 16, c + 144), half("FAM", h), half("FAM", h, 256), OP.add, OP.subtract)
+            tt(A("WN", h, 16, 2), A("CUM", c + 31, c + 144, 16), A("CUM", c + 15, c + 128, 16), OP.is_gt)
+            tt(A("DD", h, 64, 2), A("EI", 512 * h + 15, 512 * h + 512, 16), A("EK", 512 * h + 15, 512 * h + 512, 16), OP.subtract)
+        neighbours(0)
+        tt(A("EQ", 0, 256), A("SC"), A("B1"), OP.is_equal)
+        for c in range(15):
+            ts(A("EQ", block(c) + 16 * c + 16, block(c) + 256), A("B1", 16 * c + 16, 256), A("SC", 16 * c + 15, 16 * c + 16), OP.is_equal)
+        for h in range(2):
+            src = [0] + [block(c) for c in range(7 + 8 * h)]
+            for o in src:
+                mm(A("P5", 256 + h, 272, 2), half("EQ", h, o), A("WB", 0, 8), o == 0, o == src[-1])
+        ts(A("SELT", 96, 112), A("P5", 256, 272), 1.5, OP.is_gt)
+        ts(A("NF8"), A("P5", 256, 272), 1.5, OP.is_gt, 8192.0, OP.mult)
+        for i in range(4):
+            mm(A("P6", 128 * i, 128 * i + 128, 1, 8), A("NF8", i % 2, 16, 2), A("IDB"), True, True)
+        act(A("NT", 0, 512, 1, 8), A("P6", 0, 512, 1, 8), AF.Copy)
+        lists("P6", 0, 32, "NT", 0, 0)
+        LBD, LSD, LSW = A("LD", 0, 16), A("LD", 16, 32), A("LD", 32, 48)
+        if not ON_SCALAR[1]:
+            residents(1)
+        neighbours(1)
+        for h in range(2):
+            if ON_SCALAR[h]:
+                residents(h)
+        if not last:
+            act(A("XU"), IND(A("XW"), LSD), AF.Relu, -float(WEAR))
+            cp(IND(A("XW"), LSD), A("XU"))
+        scan(A("KSR"), A("SMF", 0, 256), A("P5", 0, 256), OP.add, OP.min, BIG)
+        p = A("P2", 0, 128, 1, 16)
+        turn(p, A("KSR", 15, 256, 16))
+        low(A("RP", 0, 128, 1, 16), A("RR", 0, 128, 1, 16), p)
+        for h in range(2):
+            mm(half("P2", h, 256), A("SEL", 512 + 128 * h, 640 + 128 * h, 1, 16), A("RP", 0, 128, 1, 16), True, True)
+        act(A("KRW"), A("P2", 256, 512), AF.Copy)
+        act(A("SQ"), IND(A("KRW"), A("LB")), AF.Square, A("NKC"))
+        for c in (64, 0, 16, 32, 48):
+            tt(A("TS", c, c + 16), A("DD", c, c + 16), A("WN"), OP.mult)
+        tt(A("SELT", 64, 80), A("TS", 64, 80), A("KK", 16, 32), OP.add)
+        tt(A("SELT", 80, 96), A("SELT", 64, 80), A("SELT", 64, 80), OP.mult)
+        for h in range(2):
+            tt(A("SELT", h, 64, 2), A("TS", h, 64, 2), A("EK", 512 * h + 15, 512 * h + 512, 16), OP.add)
+        p = A("P4", 0, 128, 1, 112)
+        turn(p, A("SELT"))
+        low(A("TP", 0, 128, 1, 112), A("RT", 0, 128, 1, 112), p, A("COL", 8, 9, 1, 112))
+        mm(A("P6", 0, 256), A("CZ", 0, 128), A("ONE"), True, False)
+        for h in range(2):
+            mm(half("P6", h), A("SEL", 128 * h, 128 * h + 128, 1, 112), A("TP", 0, 128, 1, 112), False, h == 1)
+        cp(A("EO"), A("P6", 0, 256))
+        swap(guest, host, "ER%d" % t, A("EO"), "ae%d" % t, "se%d" % t)
+        mm(A("P5", 256, 512), A("CZ", 128, 256), A("ONE"), True, False)
+        mm(A("P5", 256, 512), A("IDQ"), A("SQ"))
+        for h in range(2):
+            mm(half("P5", h, 256), A("SEL", 256 + 128 * h, 384 + 128 * h, 1, 112), A("TP", 0, 128, 1, 112), False, h == 1)
+        act(A("ERV"), A("P5", 256, 512), AF.Copy)
+        cp(IND(A("ERW"), LBD), A("ERV"))
+        ts(A("LO8"), A("WN"), -8192.0, OP.mult, 8192.0, OP.add)
+        for h in range(2):
+            o = A("P1", 128 * h, 128 * h + 128, 1, 8)
+            mm(o, A("NF8", h, 16, 2), A("IDB"), True, False)
+            mm(o, A("LO8", h, 16, 2), A("IDB"), False, True)
+        act(A("NT2", 0, 256, 1, 8), A("P1", 0, 256, 1, 8), AF.Copy)
+        lists("P1", 256, 16, "NT2", 16, 32)
+        tt(IND(A("OWN"), LSW), A("B1"), A("LT"), OP.mult)
+        if last:
+            dma("g", ext(T.yown[:]), (T.OWN[0::16, 0:S], A("OWN", 0, S)[1]), "d_yo", 2500)
+        else:
+            tt(A("WF"), A("WN"), A("SELT", 96, 112), OP.is_gt)
+            for c in range(16):
+                mm(A("P3", 0, 1), A("ONE", 0, 128), A("WF", c, c + 1), c == 0, c == 15)
+        act(A("P3", 256, 512), A("ERW", 0, L), AF.Copy)
+        tt(A("P3", 256, 512), A("MI"), A("P3", 256, 512), OP.max)
+        for h in range(2):
+            tt(half("M2", h), half("ER%d" % t, h), half("P3", h, 256), OP.max)
+            ts(half("MI", h), half("M2", h), 4095, OP.bitwise_and)
+            cp(half("PW" if last else "ML", h), half("MI", h))
+        if last:
+            dma("y", ext(T.ym[:]), A("PW"), "d_ym", 2200)
+        else:
+            swap(T.cores[(rank + 2 + t) % N], T.cores[(rank - 2 - t) % N], "LI%d" % (t + 1), A("ML"), "al%d" % (t + 1), "sl%d" % (t + 1))
+
+    after = [[] for _ in nodes]
+    for x in nodes:
+        for d in x["dep"] | x["ord"]:
+            after[d].append(x["i"])
+        x["left"], x["ready"] = len(x["dep"] | x["ord"]), 0.0
+    for x in reversed(nodes):
+        x["way"] = max([x["ns"]] + [nodes[j]["way"] + (x["ns"] + WAKE if x["i"] in nodes[j]["dep"] else x["hold"] if x["q"] != "g" else 0)
+                                    for j in after[x["i"]]])
+    for x in nodes[:setup]:
+        x["way"] += 1e6
+    free = {q: 0.0 for q in "vstgyn"}
+    cand = {q: [] for q in free}
+    for x in nodes:
+        if not x["left"]:
+            cand[x["q"]].append(x)
+    order = []
+    while len(order) < len(nodes):
+        best = None
+        for q, l in cand.items():
+            if l:
+                x = max(l, key=lambda y: y["way"] - 8 * max(0.0, y["ready"] - free[q]))
+                gap = x["ready"] - free[q]
+                fit = [y for y in l if max(y["ready"], free[q]) + y["hold"] <= x["ready"] + 20] if gap > 0 else []
+                if fit:
+                    x = max(fit, key=lambda y: y["way"])
+                if best is None or max(x["ready"], free[q]) < max(best["ready"], free[best["q"]]):
+                    best = x
+        x, q = best, best["q"]
+        start = max(x["ready"], free[q])
+        free[q] = start + x["hold"]
+        cand[q].remove(x)
+        order.append(x)
+        for j in after[x["i"]]:
+            y = nodes[j]
+            y["ready"] = max(y["ready"], start + x["ns"] + WAKE if x["i"] in y["dep"] else start)
+            y["left"] -= 1
+            if not y["left"]:
+                cand[y["q"]].append(y)
+
+    done = {n: 0 for n in SEMAPHORES}
+    know = {q: {} for q in free}
+
+    def wait(q, x):
+        if know[q].get(x["sem"], 0) < x["val"]:
+            Q[q].wait_ge(T.sem[x["sem"]], x["val"])
+            for k, v in list(x["knew"].items()) + [(x["sem"], x["val"])]:
+                know[q][k] = max(know[q].get(k, 0), v)
+    for at, x in enumerate(order):
+        q = x["q"]
+        for d in sorted((nodes[d] for d in x["dep"]), key=lambda y: -y["at"]):
+            wait(q, d)
+        done[x["sem"]] += x["n"]
+        x["at"], x["val"], x["knew"] = at, done[x["sem"]], dict(know[q])
+        if q != "n":
+            ins = x["call"]()
+            if ins is not None:
+                ins.then_inc(T.sem[x["sem"]], x["n"])
     for s in SEMAPHORES:
         if done[s]:
-            wait("g", s, done[s])
+            wait("g", {"sem": s, "val": done[s], "knew": {}})

@@ -5,24 +5,33 @@ BIG = float(2 ** 26)
 M64 = 1.5 * 2 ** 29
 B, F, I, U, H = "bfloat16", "float32", "int32", "uint16", "float16"
 SCRATCH = {}
-for _d, _l in ((B, "XW:4352 OWN:4352 GR:4096 GI:4096 GN:4096 S1:8192 S2:8192 MXA:4096 MXB:4096 MXC:4096 DI:2048 CR:256 CI:256 CB:256 ONE:256 IDB:128 IDN:128 "
-                   "IDH:128 IDQ:128 IDS:256 BO:128 R0:128 R0B:128 MHALF:128 DGA:256 SM1:1024 SM2:1024 WB:32 WIG:32 WIX:32 WNG:32 WNX:32 WRG:32 WRX:32 "
-                   "WK:32 JC:512 NC:128 CZ:256 KW:128 SEL:768 AT:272 LM:2048 HIM:256 HIN:256 TP:128 TM:256 RP:128 B0:256 B1:256 SCM:256 SC:256 LT:256 "
-                   "EQ:3200 NF8:16 LO8:16 WF:16 NT:512 NT2:256 CC:32 FAM:512 KRW:256 SQ:256 XU:256"),
-               (H, "ID16:128 LJ:768 THB:128 MSM:256 MSN:256 SL16:16"),
-               (F, "EO:256 ER0:256 ER1:256 ER2:256 IDF:128 PI:1 KC:1 NKC:1 TB:1 COL:16 CM:256 CM2:128 SMF:512 R16:16 ALD:32 KSC:512 KSO:512 KSR:256 "
+for _d, _l in ((B, "XW:4352 OWN:4352 GR:4096 GI:4096 GN:4096 S1:8192 S2:8192 MXA:4096 MXB:4096 MXC:4096 CR:256 CI:256 CB:256 ONE:256 IDB:128 IDN:128 "
+                   "IDH:128 NEG:128 IDS:256 BO:128 R0:128 R0B:128 MHALF:128 DGA:256 SM1:1024 SM2:1024 WB:32 WX:72 WG:72 WD:72 NR:128 MID:112 E0:128 "
+                   "JC:512 NC:128 CZ:384 KW:128 SEL:1024 AT:272 LM:2048 HIM:256 HIN:256 TP:128 TM:256 RP:128 B0:256 B1:256 SCM:256 SC:256 LT:256 "
+                   "EQ:3200 NF8:16 LO8:16 WF:16 NT:768 CC:48 ER0:128 ER1:128 ER2:128 FAM:512 RQ:128 XU:256"),
+               (H, "ID16:128 LJ:512 THB:128 MSM:256 MSN:256 SL16:16"),
+               (F, "IDF:128 KC:1 TB:1 COL:16 CM:256 SMF:256 SMX:256 R16:16 ALD:48 KSC:512 KSO:512 KSR:256 "
                    "EI:1024 EK:1024 RT:128 RM:256 RR:128 RK:32 KK:32 CUM:288 WN:16 DD:80 TS:80 SELT:112 LF:48 ERV:256 ERW:512 PW:256"),
                (I, "NBW:4096 MI:256 THC:1 TE:1 WI:1 WJ:1 NI:256 M2:256"),
                (U, "ML:256 LI0:256 LI1:256 LI2:256 LS:16 LB:16 NL:256 LD:48")):
     for _e in _l.split():
         SCRATCH[_e.split(":")[0]] = ("sbuf", [128, int(_e.split(":")[1])], _d)
-PSUM = ["P%d" % i for i in range(7)] + ["PB"]
+PSUM = ["P%d" % i for i in range(8)]
 for _p in PSUM:
-    SCRATCH[_p] = ("psum", [128, 1024], B) if _p == "PB" else ("psum", [128, 512], F)
+    SCRATCH[_p] = ("psum", [128, 512], F)
 SEMAPHORES = (["q_v", "q_s", "q_t", "q_g"] + ["d_" + n for n in ("x", "m", "o", "nb", "th", "ow", "ym", "yo")]
-              + [n + str(t) for n in ("al", "ae", "sl", "se") for t in range(RO)])
-ON_SCALAR = (False, False)
-WAKE, HOP, ISSUE = 70, 2500, 900
+              + [n + str(t) for n in ("ae", "se") for t in range(RO)] + ["%s%d%d" % (n, t, h) for n in ("al", "sl") for t in range(RO) for h in range(2)])
+ON_SCALAR = {"R0": 0, "R1": 4, "N0": 0, "N1": 4, "I0": 0, "I1": 0}
+WAKE, HOP, ISSUE = 90, 3000, 900
+TURNS, HURRY, EARLY, LATE = 3, 8, 2, False
+MERGED, SPLIT = False, False
+ON_VECTOR = []
+DIFF = ("P6", "P3")
+B1S = False
+FIRST = 1
+PRE = False
+START = 0
+ORDER = []
 
 
 def rank_program(g, core, T, topo):
@@ -32,14 +41,20 @@ def rank_program(g, core, T, topo):
     N = len(T.cores)
     Q = {"v": g.vector, "s": g.scalar, "t": g.tensor, "g": g, "y": g.sync}
     nodes = []
-    acc, bank = {}, {}
+    acc, bank, sent = {}, {}, []
 
     def A(name, c0=0, c1=None, st=1, p=None):
         t = T[name]
         c1 = t.shape[1] if c1 is None else c1
         ps = slice(None) if p is None else slice(0, p)
         return (t[ps, slice(c0, c1) if st == 1 else slice(c0, c1, st)], [(name, c0, c1)], (c1 - c0 + st - 1) // st,
-                SCRATCH[name][2] in (B, H, U), name in PSUM)
+                st == 1 and SCRATCH[name][2] in (B, H, U), name in PSUM)
+
+    def half(name, h, o=0):
+        return A(name, o + 128 * h, o + 128 * h + 128)
+
+    def mem(name, h, k):
+        return A(name, 2048 * h + k, 2048 * (h + 1), 16)
 
     def IND(win, off):
         return (win[0].indirect(off[0]), win[1] + off[1], 16 * off[2], False, False)
@@ -80,7 +95,7 @@ def rank_program(g, core, T, topo):
         nodes.append(me)
         return me["i"]
 
-    def vec(call, out, full, cols, rate):
+    def vec(call, out, full, cols, rate=None):
         ins = full + [c for c in cols if isinstance(c, tuple)]
         n = full[0][2] if full else out[2]
         if len(out[1]) > 1:
@@ -88,35 +103,37 @@ def rank_program(g, core, T, topo):
         elif full and len(full[0][1]) > 1:
             ns = 50 + 1.3 * n
         else:
-            ns = 0.83 * max(64, n * rate * (0.5 if all(x[3] for x in full + [out]) else 1))
+            ns = 0.83 * max(64, n * (rate or (0.5 if all(x[3] for x in full + [out]) else 1)))
         return node("v", call, out[1][:1], [r for x in ins for r in x[1]] + out[1][1:], ns)
 
     def cp(out, i):
-        return vec(lambda: g.vector.tensor_copy(out[0], i[0]), out, [i], [], 1)
+        return vec(lambda: g.vector.tensor_copy(out[0], i[0]), out, [i], [])
 
     def tt(out, a, b, op):
         return vec(lambda: g.vector.tensor_tensor(out[0], a[0], b[0], op), out, [a, b], [], 1 if a[4] or b[4] else 2)
 
     def ts(out, a, s1, op0, s2=None, op1=None):
         if op1 is None:
-            return vec(lambda: g.vector.tensor_scalar(out[0], a[0], val(s1), None, op0), out, [a], [s1], 1)
-        return vec(lambda: g.vector.tensor_scalar(out[0], a[0], val(s1), val(s2), op0, op1), out, [a], [s1, s2], 1)
+            return vec(lambda: g.vector.tensor_scalar(out[0], a[0], val(s1), None, op0), out, [a], [s1])
+        return vec(lambda: g.vector.tensor_scalar(out[0], a[0], val(s1), val(s2), op0, op1), out, [a], [s1, s2])
 
     def scan(out, d0, d1, op0, op1, init=0.0):
-        return vec(lambda: g.vector.tensor_tensor_scan(out[0], d0[0], d1[0], init, op0, op1), out, [d0, d1], [], 1)
+        return vec(lambda: g.vector.tensor_tensor_scan(out[0], d0[0], d1[0], init, op0, op1), out, [d0, d1], [])
 
     def fill(out, c):
-        return vec(lambda: g.vector.memset(out[0], c), out, [], [], 1)
+        return vec(lambda: g.vector.memset(out[0], c), out, [], [])
 
     def act(out, i, func, bias=0.0, scale=1.0, after=()):
         return node("s", lambda: g.scalar.activation(out[0], i[0], func, bias=val(bias), scale=scale), out[1],
-                    i[1] + (bias[1] if isinstance(bias, tuple) else []), 65 + i[2] * (1.3 if len(i[1]) > 1 else 0.83), after=after)
+                    i[1] + (bias[1] if isinstance(bias, tuple) else []), 120 + i[2] * (1.3 if len(i[1]) > 1 else 0.83), after=after)
 
     def mm(out, l, r, start=False, stop=False):
-        return node("t", lambda: g.tensor.matmul(out[0], l[0], r[0], start, stop), out[1], l[1] + r[1], 10 + 0.42 * max(min(64, l[2]), r[2]))
+        return node("t", lambda: g.tensor.matmul(out[0], l[0], r[0], start, stop), out[1], l[1] + r[1], 5 + 0.42 * max(min(64, l[2]), r[2]))
 
-    def turn(out, src):
-        return node("t", lambda: g.tensor.transpose(out[0], src[0], A("IDF")[0]), out[1], src[1] + A("IDF")[1], 225)
+    def turn(out, src, mid=True):
+        if mid:
+            mm(out, A("MID", 0, src[2]), A("ONE", 0, 128), True, False)
+        return node("t", lambda: g.tensor.matmul(out[0], src[0], A("IDF")[0], not mid, True), out[1], src[1] + A("IDF")[1], 225)
 
     def aff(out, i, pat, op, fl, base, cm):
         return node("g", lambda: g.affine_select(out[0], i[0], pat, op, fl, base, cm), out[1], i[1], 170 + 1.66 * out[2])
@@ -135,9 +152,10 @@ def rank_program(g, core, T, topo):
         eng = lanes(core, dst)
 
         def call():
-            g.remote_dma(A(land)[0], i[0], T.sem[rsem], T.sem[lsem], pid, rid, sum(1 << e for e in eng))
+            g.remote_dma(land[0], i[0], T.sem[rsem], T.sem[lsem], pid, rid, sum(1 << e for e in eng))
         s = node("g", call, [], i[1], HOP, lsem, len(eng), ISSUE)
-        node("n", None, A(land)[1], [], HOP + (2500 if land == "LI0" else 0), rsem, len(lanes(src, core)), 0, [s])
+        sent.append(s)
+        node("n", None, land[1], [], HOP + (2500 if rsem == "al01" else 0), rsem, len(lanes(src, core)), 0, [s])
 
     fill(A("THC"), 0)
     x = dma("y", A("XW", 0, S), ext(T.x0[:]), "d_x", 6000)
@@ -146,10 +164,10 @@ def rank_program(g, core, T, topo):
     dma("y", (T.THC[0::16, 0:1], A("THC")[1]), ext(T.th[:]), "d_th", 2200)
     dma("y", A("NBW"), ext(T.nb[:]), "d_nb", 12000, [x])
     cp(A("ML"), A("MI"))
-    swap(T.cores[(rank + 1) % N], T.cores[(rank - 1) % N], "LI0", A("ML"), "al0", "sl0")
+    swap(T.cores[(rank + 1) % N], T.cores[(rank - 1) % N], A("LI0"), A("ML"), "al01", "sl01")
     fill(A("OWN"), 0.0)
-    cp(A("CB"), A("NI"))
-    dma("g", (T.OWN[0::16, 0:S], A("OWN", 0, S)[1]), A("CB"), "d_ow", 3000)
+    cp(A("B0"), A("NI"))
+    dma("g", (T.OWN[0::16, 0:S], A("OWN", 0, S)[1]), A("B0"), "d_ow", 3000)
     fill(A("ONE"), 1.0)
     iota(A("CM"), [[0, 16], [1, 16]], 0)
     iota(A("WI"), [[0, 1]], 1)
@@ -158,7 +176,8 @@ def rank_program(g, core, T, topo):
     aff(A("WB"), A("WB"), [[0, 4], [16, 8]], OP.is_ge, 0.0, 15, -1)
     aff(A("BO"), A("ONE", 0, 128), [[-16, 8], [0, 16]], OP.is_ge, 0.0, 0, 1)
     aff(A("BO"), A("BO"), [[16, 8], [0, 16]], OP.is_ge, 0.0, 15, -1)
-    iota(A("ALD"), [[S - L, 2], [16, 16]], 0, L)
+    iota(A("ALD", 0, 16), [[16, 16]], 0, L)
+    iota(A("ALD", 16, 48), [[0, 2], [16, 16]], 0, S)
     for c in range(256, 3200, 368):
         iota(A("EQ", c, c + 368), [[0, 368]], 0)
     fill(A("MHALF"), -0.5)
@@ -168,30 +187,28 @@ def rank_program(g, core, T, topo):
         for n in ("SM1", "SM2"):
             cp(A(n, c, 2 * c), A(n, 0, c))
     ts(A("WJ"), A("WI"), 15, OP.bitwise_and)
-    cp(A("PI"), A("WI"))
     cp(A("KC"), A("WJ"))
-    ts(A("NKC"), A("KC"), -1.0, OP.mult)
+    magic = A("COL", 8, 9)
+    ts(magic, A("WI"), 80.0, OP.is_ge, 1.5 * 2 ** 40 - M64, OP.mult)
+    ts(magic, magic, M64, OP.add)
     ts(A("ALD"), A("ALD"), A("KC"), OP.add)
     ts(A("R16"), A("CM", 0, 16), A("KC"), OP.is_equal)
-    for name, w in (("IDH", 0.5), ("IDN", -1.0), ("IDQ", -16384.0), ("ID16", 1.0), ("IDF", 1.0)):
+    for name, w in (("IDH", 0.5), ("IDN", -1.0), ("ID16", 1.0), ("IDF", 1.0)):
         ts(A(name), A("IDB"), w, OP.mult)
     ts(A("IDS", 0, 128), A("IDB"), -64.0, OP.mult)
     cp(A("IDS", 128, 256), A("IDB"))
-    for c, n, w in ((0, 16, -1024.0), (16, 8, 64.0), (24, 8, -64.0)):
-        ts(A("WIG", c, c + n), A("WB", 0, n), w, OP.mult)
-    for c, w in ((0, -1024.0), (16, 1024.0)):
-        ts(A("WNG", c, c + 16), A("WB", 0, 16), w, OP.mult)
-    for name, src, w in (("WIX", "WIG", -2.0), ("WNX", "WNG", -2.0), ("WRG", "WNG", -1.0), ("WRX", "WNG", 2.0)):
-        ts(A(name), A(src), w, OP.mult)
-    for c, w in ((0, 64.0), (8, -128.0), (16, -64.0)):
-        ts(A("WK", c, c + 8), A("WB", 0, 8), w, OP.mult)
+    for c, n, w in ((0, 32, 2048.0), (32, 16, 2048.0), (48, 8, -128.0), (56, 8, 128.0), (64, 8, -128.0)):
+        ts(A("WX", c, c + n), A("WB", 0, n), w, OP.mult)
+    ts(A("WG"), A("WX"), -0.5, OP.mult)
+    ts(A("WD"), A("WX"), 0.5, OP.mult)
     ts(A("NC"), A("BO"), -1024.0, OP.mult)
-    ts(A("SMF", 0, 256), A("CM"), 0.0, OP.is_equal, BIG, OP.mult)
-    cp(A("SMF", 256, 512), A("SMF", 0, 256))
-    ts(A("DGA"), A("CM"), A("KC"), OP.is_equal)
-    ts(A("DGA"), A("DGA"), 1001.0, OP.mult, -1000.0, OP.add)
+    ts(A("SMF"), A("CM"), 0.0, OP.is_equal, BIG, OP.mult)
+    ts(A("SMX"), A("SMF"), -1.0, OP.mult, 128.0, OP.add)
+    ts(A("DGA"), A("CM"), A("KC"), OP.not_equal, -1024.0, OP.mult)
     ts(A("R0"), A("ONE", 0, 128), A("R16", 0, 1), OP.mult)
     ts(A("R0B"), A("BO"), A("R16", 0, 1), OP.mult)
+    ts(A("NR"), A("R0B"), -1024.0, OP.mult)
+    ts(A("E0"), A("ONE", 0, 128), A("IDF", 0, 1), OP.mult)
 
     def rows(c, *parts):
         o = A("COL", c, c + 1)
@@ -202,33 +219,27 @@ def rank_program(g, core, T, topo):
                 ts(o, A("IDF", r, r + 1), w, OP.mult, o, OP.add)
         return o
     k64, k1 = rows(0, (1, 64.0)), A("IDF", 1, 2)
-    lo, hi = rows(1, (2, -31.5), (3, 10304.0)), rows(2, (2, -31.5), (3, -129.0))
-    lim = A("COL", 3, 4)
-    ts(lim, A("IDF", 4, 5), 32768.0, OP.mult, lo, OP.add)
+    lo, hi = rows(1, (3, 10304.0)), rows(2, (3, -129.0))
+    fill(A("MID", 64, 112), 0.0)
+    ts(A("MID", 0, 64), A("E0", 0, 64), -31.5, OP.mult)
     cm = A("CM", 0, 128)
     ts(A("JC", 0, 128), cm, k64, OP.mult, lo, OP.add)
     ts(A("JC", 128, 256), cm, k64, OP.mult, hi, OP.add)
     ts(A("JC", 256, 512), A("CM"), k1, OP.mult)
-    ts(A("RT"), cm, k64, OP.mult, lim, OP.add)
-    ts(A("RR"), A("R0B"), -1024.0, OP.mult)
-    for i in range(6):
-        o = A("LJ", 128 * i, 128 * i + 128)
-        if i % 4 == 0:
-            tt(o, A("RT"), A("RR"), OP.add)
-        else:
-            cp(o, A("JC", 128 * (i % 2), 128 * (i % 2) + 128))
+    tt(A("LJ", 0, 128), A("JC", 0, 128), A("NR"), OP.add)
+    cp(A("LJ", 128, 256), A("JC", 128, 256))
+    cp(A("LJ", 256, 512), A("LJ", 0, 256))
+    fill(A("TP"), 0.0)
     ones = A("COL", 4, 5)
-    ts(ones, A("R16", 4, 5), 63.0, OP.mult, 1.0, OP.add)
-    tt(ones, ones, A("R16", 0, 1), OP.subtract)
-    tt(A("CM2"), cm, cm, OP.mult)
-    ts(A("CZ", 0, 128), A("CM2"), rows(5, (1, -16384.0)), OP.mult, rows(6, (2, 8192.0), (3, 2016.0), (4, 31.5)), OP.add)
+    ts(ones, A("R16", 0, 1), -1.0, OP.mult, 1.0, OP.add)
+    tt(A("RM", 0, 128), cm, cm, OP.mult)
+    ts(A("CZ", 256, 384), A("RM", 0, 128), rows(5, (1, -16384.0)), OP.mult)
+    ts(A("CZ", 0, 128), A("CZ", 256, 384), rows(6, (2, 8192.0), (3, 2016.0), (4, 31.5)), OP.add)
+    fill(A("NEG"), -16384.0)
     ts(A("CZ", 128, 256), A("ONE", 0, 128), rows(7, (2, 4096.0), (3, 2016.0), (4, 31.5)), OP.mult)
     ts(A("KW"), cm, 32768.0, OP.mult)
-    ts(A("CC", 0, 16), A("ONE", 0, 16), A("IDF", 0, 1), OP.mult, -1.0, OP.mult)
-    ts(A("CC", 16, 32), A("ONE", 0, 16), A("IDF", 0, 1), OP.mult, 2048.0, OP.mult)
-    magic = A("COL", 8, 9)
-    ts(magic, A("PI"), 80.0, OP.is_ge, 1.5 * 2 ** 40 - M64, OP.mult)
-    ts(magic, magic, M64, OP.add)
+    ts(A("CC", 0, 16), A("E0", 0, 16), -1.0, OP.mult)
+    ts(A("CC", 16, 48), A("E0", 0, 32), 2048.0, OP.mult)
     fill(A("XW", S, S + L), 0.0)
     fill(A("CUM"), 0.0)
     cp(A("AT", 256, 264), A("WB", 0, 8))
@@ -246,7 +257,8 @@ def rank_program(g, core, T, topo):
         else:
             aff(o, o, [[-step, 8], [0, 16]], OP.not_equal, weight, -row, 1)
     for h in range(2):
-        sel(4 + h, 8 * h, 1, src="ONE")
+        sel(4 + h, 8 * h, 1, src="KW")
+        sel(6 + h, 8 * h, 1, src="NEG")
         sel(h, 64 + h, 2, src="KW")
         for row, w in ((0, 1.0), (16, 64.0), (80, -16384.0), (96, -16384.0)):
             sel(h, row + h, 2, w)
@@ -256,26 +268,24 @@ def rank_program(g, core, T, topo):
     setup = len(nodes)
     chain = []
 
-    def gather(dst, lst, h):
-        for c in (2 * h, 2 * h + 1):
-            chain[:] = [act(A(dst, 1024 * c, 1024 * c + 1024), IND(A("XW", 0, S), A(lst, 64 * c, 64 * c + 64)), AF.Copy, after=chain)]
+    def gather(dst, lst, h, parts=None):
+        for c in parts or (2 * h, 2 * h + 1):
+            out, src = A(dst, 1024 * c, 1024 * c + 1024), IND(A("XW", 0, S), A(lst, 64 * c, 64 * c + 64))
+            if (dst, c) in ON_VECTOR:
+                cp(out, src)
+            else:
+                chain[:] = [act(out, src, AF.Copy, after=chain)]
 
-    def centre(src, h, slot):
+    def centre(out, src, h, slot):
         for c in range(2):
             o, i = 2048 * slot + 1024 * c, A(src, 2048 * h + 1024 * c, 2048 * h + 1024 * c + 1024)
             scan(A("S1", o, o + 1024), A("SM1"), i, OP.mult, OP.max)
             scan(A("S2", o, o + 1024), A("SM2"), i, OP.add, OP.min, BIG)
-        p = A("P4", 128 * slot, 128 * slot + 128)
+        p = half("P4", slot)
         mm(p, A("IDH"), A("MHALF"), True, False)
-        mm(p, A("IDH"), A("S1", 2048 * slot + 15, 2048 * slot + 2048, 16))
-        mm(p, A("IDH"), A("S2", 2048 * slot + 15, 2048 * slot + 2048, 16), False, True)
-        return p
-
-    def whole(out, p):
-        ts(out, p, float(2 ** 23), OP.add, -float(2 ** 23), OP.add)
-
-    def half(name, h, o=0):
-        return A(name, o + 128 * h, o + 128 * h + 128)
+        mm(p, A("IDH"), mem("S1", slot, 15))
+        mm(p, A("IDH"), mem("S2", slot, 15), False, True)
+        ts(half(out, h), p, float(2 ** 23), OP.add, -float(2 ** 23), OP.add)
 
     def six(lst, ms, hi_, h):
         ts(half(ms, h), half(lst, h), -2048.0, OP.add)
@@ -285,47 +295,59 @@ def rank_program(g, core, T, topo):
         mm(A(bk, o, o + 128), half(ms, h), A("ID16"))
         mm(A(bk, o, o + 256), half(hi_, h), A("IDS"))
 
-    def sums(bk, o, src, h, w):
+    def far(bk, o, src, h, cen, at, mx, w, n, ns, banks=None, limit=None, gn=None, stop=True):
+        def key(k):
+            return A(bk, o + k, o + 16 * n, 16)
+        nv = 16 - 4 * ns
+        if nv:
+            if at is not None:
+                mm(half("P7", at), A("IDB"), half(cen, h), True, True)
+            if limit is not None and not ns:
+                mm(A(bk, limit, limit + 128), half(cen, h), A("NC"))
+            for k in range(nv):
+                if ns:
+                    mm(key(k), half(cen, h), A("WG", w, w + n))
+                if gn != 0:
+                    mm(A(bk, o + k, o + 16 * (gn or n), 16), mem(src, h, k), A("WG", w, w + (gn or n)))
+        for b in range(4 - ns, 4):
+            d = banks[b % 2]
+            for k in range(4):
+                mm(half(d, k), A("IDB"), mem(src, h, 4 * b + k), True, False)
+                mm(half(d, k), A("IDN"), half(cen, h), False, True)
+            act(A(mx, 2048 * h + 512 * b, 2048 * h + 512 * b + 512), A(d), AF.Abs)
         for k in range(16):
-            mm(A(bk, o + k, o + 16 * w[2], 16), A(src, 2048 * h + k, 2048 * (h + 1), 16), w)
-
-    def larger(bk, o, src, h, cen, mx, w):
-        for k in range(16):
-            m = A(mx, 2048 * h + 128 * k, 2048 * h + 128 * k + 128)
-            tt(m, A(src, 2048 * h + k, 2048 * (h + 1), 16), half("PB", h, cen), OP.max)
-            mm(A(bk, o + k, o + 16 * w[2], 16), m, w, False, k == 15)
+            m = half(mx, 16 * h + k)
+            if k < nv:
+                tt(m, mem(src, h, k), half("P7", h if at is None else at), OP.max)
+            mm(key(k), m, A("WX" if k < nv else "WD", w, w + n), False, stop and k == 15)
 
     def low(out, r, p, m=M64):
         ts(r, p, m, OP.add, m, OP.subtract)
         tt(out, p, r, OP.subtract)
 
-    def residents(h):
+    def residents(h, banks):
         mm(half("P5", h), A("ONE", 0, 128), A("JC", 256, 384), True, False)
-        if not ON_SCALAR[h]:
-            cp(half("PB", h, 256), half("CR", h))
-            sums("P5", 128 * h, "GR", h, A("WK", 0, 8))
-            larger("P5", 128 * h, "GR", h, 256, "MXC", A("WK", 8, 16))
-            return
-        for b in range(4):
-            bk = ("P0", "P2")[b % 2]
-            for k in range(4):
-                o = A(bk, 128 * k, 128 * k + 128)
-                mm(o, A("IDB"), A("GR", 2048 * h + 4 * b + k, 2048 * (h + 1), 16), True, False)
-                mm(o, A("IDN"), half("CR", h), False, True)
-            act(A("DI", 512 * b, 512 * b + 512), A(bk), AF.Abs)
-        for k in range(16):
-            mm(A("P5", 128 * h + k, 128 * h + 128, 16), A("DI", 128 * k, 128 * k + 128), A("WK", 16, 24), False, k == 15)
+        far("P5", 128 * h, "GR", h, "CR", 2 + h, "MXC", 64, 8, ON_SCALAR["R%d" % h], banks)
+        scan(half("KSR", h), A("SMF", 0, 128), half("P5", h), OP.add, OP.min, BIG)
 
-    def lists(bk, o, n, src, c0, out):
-        p = A(bk, o, o + n)
+    def outermost():
+        p = A("P5", 256, 384, 1, 16)
+        turn(p, A("KSR", 15, 256, 16), False)
+        low(A("RP", 0, 128, 1, 16), A("RR", 0, 128, 1, 16), p)
+        tt(A("RQ", 0, 128, 1, 16), A("RP", 0, 128, 1, 16), A("RP", 0, 128, 1, 16), OP.mult)
+        mm(A("P5", 0, 256), A("CZ", 256, 384), A("ONE"), True, False)
+        for i in range(4):
+            mm(half("P5", i % 2), A("SEL", 512 + 128 * i, 640 + 128 * i, 1, 16), A("RQ" if i > 1 else "RP", 0, 128, 1, 16), False, i == 3)
+
+    def lists(bk, i0, i1):
+        p = A(bk, 16 * i0, 16 * i1)
+        mm(p, A("ONE", 0, 128), A("CC", 16 * i0, 16 * i1), True, False)
+        for i in range(i0, i1):
+            mm(A(bk, 16 * i, 16 * i + 16), A("ID16" if i else "IDB"), A("SL16") if i else A("SC", 15, 256, 16))
         for r in range(16):
-            mm(p, A("LM", 128 * r, 128 * r + 128, 1, 8), A(src, r, 16 * n, 16, 8), r == 0, False)
-        if n == 32:
-            mm(A(bk, o, o + 16), A("IDB"), A("SC", 15, 256, 16))
-        mm(A(bk, o + n - 16, o + n), A("ID16"), A("SL16"))
-        mm(p, A("ONE", 0, 128), A("CC", 32 - n, 32), False, True)
-        tt(A("LF", out, out + n), p, A("ALD", c0, c0 + n), OP.min)
-        cp(A("LD", out, out + n), A("LF", out, out + n))
+            mm(p, A("LM", 128 * r, 128 * r + 128, 1, 8), A("NT", 256 * i0 + r, 256 * i1, 16, 8), False, r == 15)
+        tt(A("LF", 16 * i0, 16 * i1), p, A("ALD", 16 * i0, 16 * i1), OP.min)
+        cp(A("LD", 16 * i0, 16 * i1), A("LF", 16 * i0, 16 * i1))
 
     def block(c):
         return 256 + 256 * c if c < 8 else 2304 + 128 * (c - 8) - 128
@@ -337,31 +359,33 @@ def rank_program(g, core, T, topo):
         if t == 0:
             cp(A("TE"), A("THC"))
         else:
-            cp(A("WI"), A("P3", 0, 1))
             ts(A("WJ"), A("WI"), 63, OP.bitwise_and)
             tt(A("TE"), A("THC"), A("WJ"), OP.add)
         ts(A("TB"), A("TE"), 4081.0, OP.min, -2048.0, OP.add)
         ts(A("THB"), A("R0"), A("TB"), OP.mult, ones, OP.add)
-        iota(A("ERW", 0, L), [[0, L]], 0)
-        gather("GR", "ML", 0)
-        whole(half("CR", 0), centre("GR", 0, 0))
-        if not ON_SCALAR[0]:
-            residents(0)
+        nodes[iota(A("ERW", 0, L), [[0, L]], 0)]["ord"].update(sent[-1:])
+        def own(h):
+            gather("GR", "ML", h, ((0, 1, 2), (3,))[h] if PRE else None)
+            centre("CR", "GR", h, 3 * h)
+            if not ON_SCALAR["R%d" % h]:
+                residents(h, None)
+        for h in range(FIRST):
+            own(h)
         for h in range(2):
             bk = PSUM[h]
             gather("GI", LI, h)
-            whole(half("CI", h), centre("GI", h, 1 + h))
-            cp(half("PB", h), half("CI", h))
+            centre("CI", "GI", h, 1 + h)
             six(LI, "MSM", "HIM", h)
             mm(A(bk), A("ONE", 0, 128), A("JC"), True, False)
             sites(bk, 0, "MSM", "HIM", h)
-            sums(bk, 0, "GI", h, A("WIG"))
-            larger(bk, 0, "GI", h, 0, "MXA", A("WIX"))
+            far(bk, 0, "GI", h, "CI", h, "MXA", 32, 32, ON_SCALAR["I%d" % h], DIFF)
+            if ON_SCALAR["I%d" % h] == 4:
+                mm(half("P7", h), A("IDB"), half("CI", h), True, True)
             scan(A("KSC", 256 * h, 256 * h + 256), A("SMF", 0, 256), A(bk, 0, 256), OP.add, OP.min, BIG)
-            p = A("P6", 0, 128, 1, 16)
+            p = A("P2", 0, 128, 1, 16)
             turn(p, A("KSC", 256 * h + 15, 256 * h + 256, 16))
             low(A("TM", 128 * h, 128 * h + 128, 1, 16), A("RM", 128 * h, 128 * h + 128, 1, 16), p)
-            p = A("P6", 128 + 8 * h, 136 + 8 * h)
+            p = A("P2", 128, 136)
             for r in range(16):
                 mm(p, A("LM", 128 * r, 128 * r + 128, 1, 16), A("TM", 128 * h + r, 128 * h + 128, 16, 16), r == 0, r == 15)
             ts(A("LS", 8 * h, 8 * h + 8), p, 2047.5, OP.add)
@@ -369,70 +393,74 @@ def rank_program(g, core, T, topo):
             cp(half("NL", h), IND(A("NBW"), A("LS", 8 * h, 8 * h + 8)))
             scan(A("KSO", 256 * h, 256 * h + 256), A("SMF", 0, 256), A(bk, 256, 512), OP.add, OP.min, BIG)
             low(A("KK", h, 32, 2), A("RK", 16 * h, 16 * h + 16), A("KSO", 256 * h + 15, 256 * h + 256, 16))
-        gather("GR", "ML", 1)
-        whole(half("CR", 1), centre("GR", 1, 3))
+            for hh in range(FIRST):
+                if h == EARLY and ON_SCALAR["R%d" % hh]:
+                    residents(hh, DIFF)
+        for h in range(FIRST, 2):
+            own(h)
+            if ON_SCALAR["R%d" % h] and EARLY < 2:
+                residents(h, DIFF)
+        if EARLY < 2:
+            outermost()
         tt(A("DD", 64, 80), A("KK", 0, 16), A("KK", 16, 32), OP.subtract)
-        cp(A("B0"), IND(A("OWN", 0, S), A("LS")))
+        act(A("B0"), IND(A("OWN", 0, S), A("LS")), AF.Identity, 1.0)
         mm(A("P4", 0, 256), A("R0B"), A("B0"), True, True)
         tt(A("SCM"), A("P4", 0, 256), A("DGA"), OP.add)
-        ts(A("B1"), A("P4", 0, 256), 1.0, OP.add)
         scan(A("SC"), A("SM1", 0, 256), A("SCM"), OP.mult, OP.max)
         ts(A("LB"), A("SC", 15, 256, 16), -1.0, OP.add)
-        cp(A("CB"), IND(A("CR"), A("LB")))
-        cp(A("PB", 512, 768), A("CB"))
+        tt(A("EQ", 0, 256), A("SC"), A("P4", 0, 256), OP.is_equal)
+        if B1S:
+            act(A("B1"), A("P4", 0, 256), AF.Copy)
+        else:
+            cp(A("B1"), A("P4", 0, 256))
+        act(A("CB"), IND(A("CR"), A("LB")), AF.Copy)
         ts(A("LT"), A("B1"), 256.0, OP.is_lt)
 
-        def neighbours(h):
+        def neighbours(h, banks):
             gather("GN", "NL", h)
             six("NL", "MSN", "HIN", h)
-            for bk, o, cen, wg in ((PSUM[h], 0, "CI", "WNG"), (PSUM[2 + h], 256, "CB", "WRG")):
-                mm(A(bk), A("THB"), A("LJ", o, o + 512), True, False)
-                for o2 in (0, 256):
-                    sites(bk, o2, "MSN", "HIN", h)
-                mm(A(bk, o, o + 128), half(cen, h), A("NC"))
-                sums(bk, 0, "GN", h, A(wg))
-            larger(PSUM[h], 0, "GN", h, 0, "MXA", A("WNX"))
-            larger(PSUM[2 + h], 0, "GN", h, 512, "MXB", A("WRX"))
-            act(half("FAM", h), A(PSUM[h], 0, 128), AF.Sign, 2.0 ** 22 - 32, -1.0)
-            act(half("FAM", h, 256), A(PSUM[2 + h], 256, 384), AF.Sign, 2.0 ** 22 - 32, -1.0)
-            scan(A("EI", 512 * h, 512 * h + 512), A("SMF"), A(PSUM[h]), OP.add, OP.min, BIG)
-            scan(A("EK", 512 * h, 512 * h + 512), A("SMF"), A(PSUM[2 + h]), OP.add, OP.min, BIG)
+            ns = ON_SCALAR["N%d" % h]
+            bk = PSUM[h]
+            mm(A(bk), A("THB"), A("LJ"), True, False)
+            sites(bk, 0, "MSN", "HIN", h)
+            sites(bk, 256, "MSN", "HIN", h)
+            far(bk, 0, "GN", h, "CI", None, "MXA", 0, 16, 0, None, 0, 16 if ns else 32, False)
+            far(bk, 256, "GN", h, "CB", 2 + h, "MXB", 0, 16, ns, banks, 256, None if ns else 0)
+
+        def fights(h):
+            bi = br = PSUM[h]
             c = 144 * h
+            for bk, o in ((bi, 0), (br, 256)):
+                act(half("FAM", h, o), A(bk, o, o + 128), AF.Sign, 2.0 ** 21 - 0.5, -1.0)
+            for bk, o, out in ((bi, 0, "EI"), (br, 256, "EK")):
+                scan(A(out, 512 * h + o, 512 * h + o + 256), A("SMF"), A(bk, o, o + 256), OP.add, OP.min, BIG)
+                scan(A(out, 512 * h + 256 - o, 512 * h + 512 - o), A("SMX"), A(bk, o, o + 256), OP.add, OP.max)
             scan(A("CUM", c + 16, c + 144), half("FAM", h), half("FAM", h, 256), OP.add, OP.subtract)
             tt(A("WN", h, 16, 2), A("CUM", c + 31, c + 144, 16), A("CUM", c + 15, c + 128, 16), OP.is_gt)
             tt(A("DD", h, 64, 2), A("EI", 512 * h + 15, 512 * h + 512, 16), A("EK", 512 * h + 15, 512 * h + 512, 16), OP.subtract)
-        neighbours(0)
-        tt(A("EQ", 0, 256), A("SC"), A("B1"), OP.is_equal)
+        neighbours(0, DIFF)
+        fights(0)
         for c in range(15):
             ts(A("EQ", block(c) + 16 * c + 16, block(c) + 256), A("B1", 16 * c + 16, 256), A("SC", 16 * c + 15, 16 * c + 16), OP.is_equal)
         for h in range(2):
             src = [0] + [block(c) for c in range(7 + 8 * h)]
             for o in src:
-                mm(A("P5", 256 + h, 272, 2), half("EQ", h, o), A("WB", 0, 8), o == 0, o == src[-1])
-        ts(A("SELT", 96, 112), A("P5", 256, 272), 1.5, OP.is_gt)
-        ts(A("NF8"), A("P5", 256, 272), 1.5, OP.is_gt, 8192.0, OP.mult)
+                mm(A("P4", 256 + h, 272, 2), half("EQ", h, o), A("WB", 0, 8), o == 0, o == src[-1])
+        ts(A("SELT", 96, 112), A("P4", 256, 272), 1.5, OP.is_gt)
+        ts(A("NF8"), A("P4", 256, 272), 1.5, OP.is_gt, 8192.0, OP.mult)
         for i in range(4):
-            mm(A("P6", 128 * i, 128 * i + 128, 1, 8), A("NF8", i % 2, 16, 2), A("IDB"), True, True)
-        act(A("NT", 0, 512, 1, 8), A("P6", 0, 512, 1, 8), AF.Copy)
-        lists("P6", 0, 32, "NT", 0, 0)
+            mm(A("P4", 128 * i, 128 * i + 128, 1, 8), A("NF8", i % 2, 16, 2), A("IDB"), True, True)
+        act(A("NT", 0, 512, 1, 8), A("P4", 0, 512, 1, 8), AF.Copy)
+        if not MERGED:
+            lists("P4", 0, 2)
         LBD, LSD, LSW = A("LD", 0, 16), A("LD", 16, 32), A("LD", 32, 48)
-        if not ON_SCALAR[1]:
-            residents(1)
-        neighbours(1)
-        for h in range(2):
-            if ON_SCALAR[h]:
-                residents(h)
-        if not last:
-            act(A("XU"), IND(A("XW"), LSD), AF.Relu, -float(WEAR))
-            cp(IND(A("XW"), LSD), A("XU"))
-        scan(A("KSR"), A("SMF", 0, 256), A("P5", 0, 256), OP.add, OP.min, BIG)
-        p = A("P2", 0, 128, 1, 16)
-        turn(p, A("KSR", 15, 256, 16))
-        low(A("RP", 0, 128, 1, 16), A("RR", 0, 128, 1, 16), p)
-        for h in range(2):
-            mm(half("P2", h, 256), A("SEL", 512 + 128 * h, 640 + 128 * h, 1, 16), A("RP", 0, 128, 1, 16), True, True)
-        act(A("KRW"), A("P2", 256, 512), AF.Copy)
-        act(A("SQ"), IND(A("KRW"), A("LB")), AF.Square, A("NKC"))
+        neighbours(1, DIFF)
+        fights(1)
+        if EARLY == 2:
+            for hh in range(2):
+                if ON_SCALAR["R%d" % hh]:
+                    residents(hh, DIFF)
+            outermost()
         for c in (64, 0, 16, 32, 48):
             tt(A("TS", c, c + 16), A("DD", c, c + 16), A("WN"), OP.mult)
         tt(A("SELT", 64, 80), A("TS", 64, 80), A("KK", 16, 32), OP.add)
@@ -442,83 +470,96 @@ def rank_program(g, core, T, topo):
         p = A("P4", 0, 128, 1, 112)
         turn(p, A("SELT"))
         low(A("TP", 0, 128, 1, 112), A("RT", 0, 128, 1, 112), p, A("COL", 8, 9, 1, 112))
-        mm(A("P6", 0, 256), A("CZ", 0, 128), A("ONE"), True, False)
-        for h in range(2):
-            mm(half("P6", h), A("SEL", 128 * h, 128 * h + 128, 1, 112), A("TP", 0, 128, 1, 112), False, h == 1)
-        cp(A("EO"), A("P6", 0, 256))
-        swap(guest, host, "ER%d" % t, A("EO"), "ae%d" % t, "se%d" % t)
-        mm(A("P5", 256, 512), A("CZ", 128, 256), A("ONE"), True, False)
-        mm(A("P5", 256, 512), A("IDQ"), A("SQ"))
-        for h in range(2):
-            mm(half("P5", h, 256), A("SEL", 256 + 128 * h, 384 + 128 * h, 1, 112), A("TP", 0, 128, 1, 112), False, h == 1)
-        act(A("ERV"), A("P5", 256, 512), AF.Copy)
-        cp(IND(A("ERW"), LBD), A("ERV"))
+        swap(guest, host, A("ER%d" % t), A("TP"), "ae%d" % t, "se%d" % t)
         ts(A("LO8"), A("WN"), -8192.0, OP.mult, 8192.0, OP.add)
         for h in range(2):
             o = A("P1", 128 * h, 128 * h + 128, 1, 8)
             mm(o, A("NF8", h, 16, 2), A("IDB"), True, False)
             mm(o, A("LO8", h, 16, 2), A("IDB"), False, True)
-        act(A("NT2", 0, 256, 1, 8), A("P1", 0, 256, 1, 8), AF.Copy)
-        lists("P1", 256, 16, "NT2", 16, 32)
-        tt(IND(A("OWN"), LSW), A("B1"), A("LT"), OP.mult)
+        act(A("NT", 512, 768, 1, 8), A("P1", 0, 256, 1, 8), AF.Copy)
+        lists("P1", 0 if MERGED else 2, 3)
+        if not last:
+            act(A("XU"), IND(A("XW"), LSD), AF.Relu, -float(WEAR))
+            cp(IND(A("XW"), LSD), A("XU"))
+        mm(A("P2", 256, 512), A("CZ", 128, 256), A("ONE"), True, False)
+        for h in range(2):
+            mm(half("P2", h, 256), A("SEL", 256 + 128 * h, 384 + 128 * h, 1, 112), A("TP", 0, 128, 1, 112), False, h == 1)
+        act(A("ERV"), A("P2", 256, 512), AF.Copy)
+        o = IND(A("ERW"), LBD)
+        node("s", lambda o=o: g.scalar.activation(o[0], A("ERV")[0], AF.Silu), o[1][:1], o[1][1:] + A("ERV")[1], 870)
+        owners = tt(IND(A("OWN"), LSW), A("B1"), A("LT"), OP.mult)
         if last:
             dma("g", ext(T.yown[:]), (T.OWN[0::16, 0:S], A("OWN", 0, S)[1]), "d_yo", 2500)
         else:
             tt(A("WF"), A("WN"), A("SELT", 96, 112), OP.is_gt)
-            for c in range(16):
-                mm(A("P3", 0, 1), A("ONE", 0, 128), A("WF", c, c + 1), c == 0, c == 15)
-        act(A("P3", 256, 512), A("ERW", 0, L), AF.Copy)
-        tt(A("P3", 256, 512), A("MI"), A("P3", 256, 512), OP.max)
+            mm(A("P2", 0, 16), A("ONE", 0, 128), A("WF"), True, True)
+            scan(A("RK", 0, 16), A("ONE", 0, 16), A("P2", 0, 16), OP.mult, OP.add)
+            cp(A("WI"), A("RK", 15, 16))
+        mm(A("P0", 0, 256), A("CZ", 0, 128), A("ONE"), True, False)
         for h in range(2):
-            tt(half("M2", h), half("ER%d" % t, h), half("P3", h, 256), OP.max)
+            mm(half("P0", h), A("SEL", 128 * h, 128 * h + 128, 1, 112), A("ER%d" % t, 0, 128, 1, 112), False, h == 1)
+        for h in range(2):
+            tt(half("P0", h, 256), half("MI", h), half("P0", h), OP.max)
+            tt(half("ERV", h), half("ERW", h), half("P5", h), OP.add)
+            tt(half("M2", h), half("ERV", h), half("P0", h, 256), OP.max)
             ts(half("MI", h), half("M2", h), 4095, OP.bitwise_and)
-            cp(half("PW" if last else "ML", h), half("MI", h))
+            x = cp(half("PW" if last else "ML", h), half("MI", h))
+            if not last:
+                nodes[owners]["ord"].add(x)
+            if not last and (SPLIT or h):
+                c = 128 * h if SPLIT else 0
+                n = "%d%d" % (t + 1, h)
+                swap(T.cores[(rank + 2 + t) % N], T.cores[(rank - 2 - t) % N], A("LI%d" % (t + 1), c, 128 * h + 128), A("ML", c, 128 * h + 128), "al" + n, "sl" + n)
         if last:
             dma("y", ext(T.ym[:]), A("PW"), "d_ym", 2200)
-        else:
-            swap(T.cores[(rank + 2 + t) % N], T.cores[(rank - 2 - t) % N], "LI%d" % (t + 1), A("ML"), "al%d" % (t + 1), "sl%d" % (t + 1))
 
-    after = [[] for _ in nodes]
+    link = [[[] for _ in nodes], [[] for _ in nodes]]
     for x in nodes:
         for d in x["dep"] | x["ord"]:
-            after[d].append(x["i"])
-        x["left"], x["ready"] = len(x["dep"] | x["ord"]), 0.0
+            waits = d in x["dep"]
+            link[0][d].append((x["i"], nodes[d]["ns"] + WAKE if waits else 0))
+            link[1][x["i"]].append((d, x["hold"] + nodes[d]["ns"] - nodes[d]["hold"] + WAKE if waits else 0))
+
+    def schedule(way, urgent):
+        left = [len(l) for l in link[1 - way]]
+        ready = [0.0 if way == 0 else x["ns"] - x["hold"] for x in nodes]
+        free = {q: 0.0 for q in "vstgyn"}
+        cand = {q: [x["i"] for x in nodes if x["q"] == q and not left[x["i"]]] for q in free}
+        order, ends = [], [0.0] * len(nodes)
+        while len(order) < len(nodes):
+            best = None
+            for q, l in cand.items():
+                if l:
+                    i = max(l, key=lambda y: urgent[y] - HURRY * max(0.0, ready[y] - free[q]))
+                    if ready[i] > free[q]:
+                        fit = [y for y in l if max(ready[y], free[q]) + nodes[y]["hold"] <= ready[i] + 20]
+                        i = max(fit, key=lambda y: urgent[y]) if fit else i
+                    if best is None or max(ready[i], free[q]) < best[0]:
+                        best = (max(ready[i], free[q]), i, q)
+            start, i, q = best
+            free[q] = ends[i] = start + nodes[i]["hold"]
+            cand[q].remove(i)
+            order.append(nodes[i])
+            for j, ns in link[way][i]:
+                ready[j] = max(ready[j], start + ns)
+                left[j] -= 1
+                if not left[j]:
+                    cand[nodes[j]["q"]].append(j)
+        return order, ends
+    urgent = [0.0] * len(nodes)
     for x in reversed(nodes):
-        x["way"] = max([x["ns"]] + [nodes[j]["way"] + (x["ns"] + WAKE if x["i"] in nodes[j]["dep"] else x["hold"] if x["q"] != "g" else 0)
-                                    for j in after[x["i"]]])
-    for x in nodes[:setup]:
-        x["way"] += 1e6
-    free = {q: 0.0 for q in "vstgyn"}
-    cand = {q: [] for q in free}
-    for x in nodes:
-        if not x["left"]:
-            cand[x["q"]].append(x)
-    order = []
-    while len(order) < len(nodes):
-        best = None
-        for q, l in cand.items():
-            if l:
-                x = max(l, key=lambda y: y["way"] - 8 * max(0.0, y["ready"] - free[q]))
-                gap = x["ready"] - free[q]
-                fit = [y for y in l if max(y["ready"], free[q]) + y["hold"] <= x["ready"] + 20] if gap > 0 else []
-                if fit:
-                    x = max(fit, key=lambda y: y["way"])
-                if best is None or max(x["ready"], free[q]) < max(best["ready"], free[best["q"]]):
-                    best = x
-        x, q = best, best["q"]
-        start = max(x["ready"], free[q])
-        free[q] = start + x["hold"]
-        cand[q].remove(x)
-        order.append(x)
-        for j in after[x["i"]]:
-            y = nodes[j]
-            y["ready"] = max(y["ready"], start + x["ns"] + WAKE if x["i"] in y["dep"] else start)
-            y["left"] -= 1
-            if not y["left"]:
-                cand[y["q"]].append(y)
+        urgent[x["i"]] = max([x["ns"]] + [urgent[j] + (ns or (x["hold"] if x["q"] != "g" else 0)) for j, ns in link[0][x["i"]]])
+    if START:
+        urgent = [-START * i for i in range(len(nodes))]
+    for _ in range(0 if ORDER else TURNS):
+        order, ends = schedule(0, [u + (1e6 if i < setup else 0) for i, u in enumerate(urgent)])
+        if not ORDER or max(ends) < ORDER[0]:
+            ORDER[:] = [max(ends), [x["i"] for x in order]]
+        urgent = schedule(1, ends)[1]
+    order = [nodes[i] for i in ORDER[1]]
 
     done = {n: 0 for n in SEMAPHORES}
-    know = {q: {} for q in free}
+    know = {q: {} for q in "vstgyn"}
 
     def wait(q, x):
         if know[q].get(x["sem"], 0) < x["val"]:

@@ -6,9 +6,9 @@ M64 = 1.5 * 2 ** 29
 B, F, I, U, H = "bfloat16", "float32", "int32", "uint16", "float16"
 SCRATCH = {}
 for _d, _l in ((B, "XW:4352 OWN:4352 GR:4096 GI:4096 GN:4096 S1:8192 S2:8192 MXA:4096 MXB:4096 MXC:4096 CR:256 CI:256 CB:256 ONE:256 IDB:128 IDN:128 "
-                   "IDH:128 NEG:128 IDS:256 BO:128 R0:128 R0B:128 MHALF:128 DGA:256 SM1:1024 SM2:1024 WB:32 WX:72 WG:72 WD:72 NR:128 MID:112 E0:128 "
-                   "JC:512 NC:128 CZ:384 KW:128 SEL:1024 AT:272 LM:2048 HIM:256 HIN:256 TP:128 TM:256 RP:128 B0:256 B1:256 SCM:256 SC:256 LT:256 "
-                   "EQ:3200 NF8:16 LO8:16 WF:16 NT:768 CC:48 ER0:128 ER1:128 ER2:128 FAM:512 RQ:128 XU:256"),
+                   "IDH:128 IDS:256 BO:128 R0:128 R0B:128 MHALF:128 DGA:256 SM1:1024 SM2:1024 WB:32 WX:72 WG:72 WD:72 NR:128 MID:112 E0:128 "
+                   "JC:512 NC:128 CZ:256 KW:128 SEL:768 AT:272 LM:2048 HIM:256 HIN:256 TP:128 TM:256 RP:128 B0:256 B1:256 SCM:256 SC:256 LT:256 "
+                   "EQ:3200 NF8:16 LO8:16 WF:16 NT:768 CC:48 ER0:128 ER1:128 ER2:128 FAM:512 XU:256"),
                (H, "ID16:128 LJ:512 THB:128 MSM:256 MSN:256 SL16:16"),
                (F, "IDF:128 KC:1 TB:1 COL:16 CM:256 SMF:256 SMX:256 R16:16 ALD:48 KSC:512 KSO:512 KSR:256 "
                    "EI:1024 EK:1024 RT:128 RM:256 RR:128 RK:32 KK:32 CUM:288 WN:16 DD:80 TS:80 SELT:112 LF:48 ERV:256 ERW:512 PW:256"),
@@ -21,13 +21,17 @@ for _p in PSUM:
     SCRATCH[_p] = ("psum", [128, 512], F)
 SEMAPHORES = (["q_v", "q_s", "q_t", "q_g"] + ["d_" + n for n in ("x", "m", "o", "nb", "th", "ow", "ym", "yo")]
               + [n + str(t) for n in ("ae", "se") for t in range(RO)] + ["%s%d%d" % (n, t, h) for n in ("al", "sl") for t in range(RO) for h in range(2)])
-ON_SCALAR = {"R0": 0, "R1": 4, "N0": 0, "N1": 4, "I0": 0, "I1": 0}
-WAKE, HOP, ISSUE = 90, 3000, 900
-TURNS, HURRY, EARLY, LATE = 3, 8, 2, False
+ON_SCALAR = {"R0": 4, "R1": 4, "N0": 4, "N1": 0, "I0": 0, "I1": 0}
+WAKE, HOP, ISSUE = 200, 2200, 600
+TURNS, HURRY, EARLY, LATE = 3, 20, 0, False
 MERGED, SPLIT = False, False
-ON_VECTOR = []
+GATHER = 1.35
+ON_VECTOR = [("GR", 1)]
 DIFF = ("P6", "P3")
 B1S = False
+LOOSE = True
+WHOLE = []
+MIDDLE = False
 FIRST = 1
 PRE = False
 START = 0
@@ -83,7 +87,7 @@ def rank_program(g, core, T, topo):
                         continue
                 for (i, aw, a0, a1) in acc.get(b, []):
                     if (aw or wr) and a1 > c0 and a0 < c1 and i != me["i"]:
-                        me["dep"].add(i)
+                        me["ord" if wr and LOOSE and q in "vs" and nodes[i]["sem"] == "q_" + q and sem is None else "dep"].add(i)
         for regs, wr in ((writes, True), (reads, False)):
             for (b, c0, c1) in regs:
                 l = acc.setdefault(b, [])
@@ -101,7 +105,7 @@ def rank_program(g, core, T, topo):
         if len(out[1]) > 1:
             ns = 50 + 3.2 * n
         elif full and len(full[0][1]) > 1:
-            ns = 50 + 1.3 * n
+            ns = 50 + GATHER * n
         else:
             ns = 0.83 * max(64, n * (rate or (0.5 if all(x[3] for x in full + [out]) else 1)))
         return node("v", call, out[1][:1], [r for x in ins for r in x[1]] + out[1][1:], ns)
@@ -125,10 +129,10 @@ def rank_program(g, core, T, topo):
 
     def act(out, i, func, bias=0.0, scale=1.0, after=()):
         return node("s", lambda: g.scalar.activation(out[0], i[0], func, bias=val(bias), scale=scale), out[1],
-                    i[1] + (bias[1] if isinstance(bias, tuple) else []), 120 + i[2] * (1.3 if len(i[1]) > 1 else 0.83), after=after)
+                    i[1] + (bias[1] if isinstance(bias, tuple) else []), 65 + i[2] * (GATHER if len(i[1]) > 1 else 0.83), after=after)
 
     def mm(out, l, r, start=False, stop=False):
-        return node("t", lambda: g.tensor.matmul(out[0], l[0], r[0], start, stop), out[1], l[1] + r[1], 5 + 0.42 * max(min(64, l[2]), r[2]))
+        return node("t", lambda: g.tensor.matmul(out[0], l[0], r[0], start, stop), out[1], l[1] + r[1], 0.42 * max(min(64, l[2]), r[2]))
 
     def turn(out, src, mid=True):
         if mid:
@@ -161,13 +165,13 @@ def rank_program(g, core, T, topo):
     x = dma("y", A("XW", 0, S), ext(T.x0[:]), "d_x", 6000)
     dma("s", A("MI"), ext(T.m0[:]), "d_m", 2200)
     dma("s", A("NI"), ext(T.own0[:]), "d_o", 2400)
-    dma("y", (T.THC[0::16, 0:1], A("THC")[1]), ext(T.th[:]), "d_th", 2200)
     dma("y", A("NBW"), ext(T.nb[:]), "d_nb", 12000, [x])
     cp(A("ML"), A("MI"))
     swap(T.cores[(rank + 1) % N], T.cores[(rank - 1) % N], A("LI0"), A("ML"), "al01", "sl01")
+    dma("g", (T.THC[0::16, 0:1], A("THC")[1]), ext(T.th[:]), "d_th", 5000, sent[-1:])
     fill(A("OWN"), 0.0)
     cp(A("B0"), A("NI"))
-    dma("g", (T.OWN[0::16, 0:S], A("OWN", 0, S)[1]), A("B0"), "d_ow", 3000)
+    dma("y", (T.OWN[0::16, 0:S], A("OWN", 0, S)[1]), A("B0"), "d_ow", 3000)
     fill(A("ONE"), 1.0)
     iota(A("CM"), [[0, 16], [1, 16]], 0)
     iota(A("WI"), [[0, 1]], 1)
@@ -178,8 +182,10 @@ def rank_program(g, core, T, topo):
     aff(A("BO"), A("BO"), [[16, 8], [0, 16]], OP.is_ge, 0.0, 15, -1)
     iota(A("ALD", 0, 16), [[16, 16]], 0, L)
     iota(A("ALD", 16, 48), [[0, 2], [16, 16]], 0, S)
-    for c in range(256, 3200, 368):
-        iota(A("EQ", c, c + 368), [[0, 368]], 0)
+    for c in range(15):
+        if c != 7:
+            o = 256 + 256 * c if c < 8 else 2304 + 128 * (c - 8)
+            fill(A("EQ", o, o + 16 * (c % 8 + 1)), 0.0)
     fill(A("MHALF"), -0.5)
     ts(A("SM1", 0, 256), A("CM"), 0.0, OP.not_equal)
     ts(A("SM2", 0, 256), A("CM"), 0.0, OP.is_equal, 1024.0, OP.mult)
@@ -193,21 +199,21 @@ def rank_program(g, core, T, topo):
     ts(magic, magic, M64, OP.add)
     ts(A("ALD"), A("ALD"), A("KC"), OP.add)
     ts(A("R16"), A("CM", 0, 16), A("KC"), OP.is_equal)
-    for name, w in (("IDH", 0.5), ("IDN", -1.0), ("ID16", 1.0), ("IDF", 1.0)):
+    for name, w in (("IDH", 0.5), ("ID16", 1.0)):
         ts(A(name), A("IDB"), w, OP.mult)
-    ts(A("IDS", 0, 128), A("IDB"), -64.0, OP.mult)
-    cp(A("IDS", 128, 256), A("IDB"))
+    for o, w in ((A("IDN"), -1.0), (A("IDF"), 1.0), (half("IDS", 0), -64.0), (half("IDS", 1), 1.0)):
+        act(o, A("IDB"), AF.Identity, 0.0, w)
     for c, n, w in ((0, 32, 2048.0), (32, 16, 2048.0), (48, 8, -128.0), (56, 8, 128.0), (64, 8, -128.0)):
         ts(A("WX", c, c + n), A("WB", 0, n), w, OP.mult)
     ts(A("WG"), A("WX"), -0.5, OP.mult)
     ts(A("WD"), A("WX"), 0.5, OP.mult)
-    ts(A("NC"), A("BO"), -1024.0, OP.mult)
+    act(A("NC"), A("BO"), AF.Identity, 0.0, -1024.0)
     ts(A("SMF"), A("CM"), 0.0, OP.is_equal, BIG, OP.mult)
-    ts(A("SMX"), A("SMF"), -1.0, OP.mult, 128.0, OP.add)
+    act(A("SMX"), A("SMF"), AF.Identity, 128.0, -1.0)
     ts(A("DGA"), A("CM"), A("KC"), OP.not_equal, -1024.0, OP.mult)
     ts(A("R0"), A("ONE", 0, 128), A("R16", 0, 1), OP.mult)
     ts(A("R0B"), A("BO"), A("R16", 0, 1), OP.mult)
-    ts(A("NR"), A("R0B"), -1024.0, OP.mult)
+    act(A("NR"), A("R0B"), AF.Identity, 0.0, -1024.0)
     ts(A("E0"), A("ONE", 0, 128), A("IDF", 0, 1), OP.mult)
 
     def rows(c, *parts):
@@ -232,16 +238,16 @@ def rank_program(g, core, T, topo):
     fill(A("TP"), 0.0)
     ones = A("COL", 4, 5)
     ts(ones, A("R16", 0, 1), -1.0, OP.mult, 1.0, OP.add)
-    tt(A("RM", 0, 128), cm, cm, OP.mult)
-    ts(A("CZ", 256, 384), A("RM", 0, 128), rows(5, (1, -16384.0)), OP.mult)
-    ts(A("CZ", 0, 128), A("CZ", 256, 384), rows(6, (2, 8192.0), (3, 2016.0), (4, 31.5)), OP.add)
-    fill(A("NEG"), -16384.0)
+    act(A("RT"), cm, AF.Square)
+    nodes[act(A("ERW", 0, L), A("CM"), AF.Silu, 0.0, 0.0)].update(hold=1600, ns=1600)
+    ts(A("CZ", 0, 128), A("RT"), rows(5, (1, -32768.0)), OP.mult, rows(6, (2, 16384.0), (3, 2016.0), (4, 31.5)), OP.add)
     ts(A("CZ", 128, 256), A("ONE", 0, 128), rows(7, (2, 4096.0), (3, 2016.0), (4, 31.5)), OP.mult)
-    ts(A("KW"), cm, 32768.0, OP.mult)
+    act(A("KW"), cm, AF.Identity, 0.0, 65536.0)
     ts(A("CC", 0, 16), A("E0", 0, 16), -1.0, OP.mult)
     ts(A("CC", 16, 48), A("E0", 0, 32), 2048.0, OP.mult)
     fill(A("XW", S, S + L), 0.0)
-    fill(A("CUM"), 0.0)
+    for c in (0, 144):
+        fill(A("CUM", c, c + 16), 0.0)
     cp(A("AT", 256, 264), A("WB", 0, 8))
     ts(A("AT", 264, 272), A("WB", 0, 8), 64.0, OP.mult)
     for r in range(16):
@@ -257,10 +263,9 @@ def rank_program(g, core, T, topo):
         else:
             aff(o, o, [[-step, 8], [0, 16]], OP.not_equal, weight, -row, 1)
     for h in range(2):
-        sel(4 + h, 8 * h, 1, src="KW")
-        sel(6 + h, 8 * h, 1, src="NEG")
+        sel(4 + h, 8 * h, 1, src="ONE")
         sel(h, 64 + h, 2, src="KW")
-        for row, w in ((0, 1.0), (16, 64.0), (80, -16384.0), (96, -16384.0)):
+        for row, w in ((0, 1.0), (16, 64.0), (80, -32768.0), (96, -32768.0)):
             sel(h, row + h, 2, w)
         sel(2 + h, 32 + h, 2, src="ONE")
         sel(2 + h, 48 + h, 2, 64.0)
@@ -269,8 +274,9 @@ def rank_program(g, core, T, topo):
     chain = []
 
     def gather(dst, lst, h, parts=None):
-        for c in parts or (2 * h, 2 * h + 1):
-            out, src = A(dst, 1024 * c, 1024 * c + 1024), IND(A("XW", 0, S), A(lst, 64 * c, 64 * c + 64))
+        n = 2 if (dst, h) in WHOLE else 1
+        for c in parts or range(2 * h, 2 * h + 2, n):
+            out, src = A(dst, 1024 * c, 1024 * (c + n)), IND(A("XW", 0, S), A(lst, 64 * c, 64 * (c + n)))
             if (dst, c) in ON_VECTOR:
                 cp(out, src)
             else:
@@ -334,10 +340,10 @@ def rank_program(g, core, T, topo):
         p = A("P5", 256, 384, 1, 16)
         turn(p, A("KSR", 15, 256, 16), False)
         low(A("RP", 0, 128, 1, 16), A("RR", 0, 128, 1, 16), p)
-        tt(A("RQ", 0, 128, 1, 16), A("RP", 0, 128, 1, 16), A("RP", 0, 128, 1, 16), OP.mult)
-        mm(A("P5", 0, 256), A("CZ", 256, 384), A("ONE"), True, False)
-        for i in range(4):
-            mm(half("P5", i % 2), A("SEL", 512 + 128 * i, 640 + 128 * i, 1, 16), A("RQ" if i > 1 else "RP", 0, 128, 1, 16), False, i == 3)
+        for h in range(2):
+            mm(half("P5", h), A("SEL", 512 + 128 * h, 640 + 128 * h, 1, 16), A("RP", 0, 128, 1, 16), True, True)
+        ts(A("P5", 256, 512), A("P5", 0, 256), A("KC"), OP.not_equal, 8192.0, OP.mult)
+        tt(A("PW"), A("MI"), A("P5", 256, 512), OP.add)
 
     def lists(bk, i0, i1):
         p = A(bk, 16 * i0, 16 * i1)
@@ -363,11 +369,12 @@ def rank_program(g, core, T, topo):
             tt(A("TE"), A("THC"), A("WJ"), OP.add)
         ts(A("TB"), A("TE"), 4081.0, OP.min, -2048.0, OP.add)
         ts(A("THB"), A("R0"), A("TB"), OP.mult, ones, OP.add)
-        nodes[iota(A("ERW", 0, L), [[0, L]], 0)]["ord"].update(sent[-1:])
+        if t:
+            nodes[iota(A("ERW", 0, L), [[0, L]], 0)]["ord"].update(sent[-1:])
         def own(h):
             gather("GR", "ML", h, ((0, 1, 2), (3,))[h] if PRE else None)
             centre("CR", "GR", h, 3 * h)
-            if not ON_SCALAR["R%d" % h]:
+            if not ON_SCALAR["R%d" % h] and not LATE:
                 residents(h, None)
         for h in range(FIRST):
             own(h)
@@ -398,10 +405,7 @@ def rank_program(g, core, T, topo):
                     residents(hh, DIFF)
         for h in range(FIRST, 2):
             own(h)
-            if ON_SCALAR["R%d" % h] and EARLY < 2:
-                residents(h, DIFF)
-        if EARLY < 2:
-            outermost()
+
         tt(A("DD", 64, 80), A("KK", 0, 16), A("KK", 16, 32), OP.subtract)
         act(A("B0"), IND(A("OWN", 0, S), A("LS")), AF.Identity, 1.0)
         mm(A("P4", 0, 256), A("R0B"), A("B0"), True, True)
@@ -439,6 +443,8 @@ def rank_program(g, core, T, topo):
             tt(A("WN", h, 16, 2), A("CUM", c + 31, c + 144, 16), A("CUM", c + 15, c + 128, 16), OP.is_gt)
             tt(A("DD", h, 64, 2), A("EI", 512 * h + 15, 512 * h + 512, 16), A("EK", 512 * h + 15, 512 * h + 512, 16), OP.subtract)
         neighbours(0, DIFF)
+        if MIDDLE:
+            residents(1, DIFF)
         fights(0)
         for c in range(15):
             ts(A("EQ", block(c) + 16 * c + 16, block(c) + 256), A("B1", 16 * c + 16, 256), A("SC", 16 * c + 15, 16 * c + 16), OP.is_equal)
@@ -456,11 +462,10 @@ def rank_program(g, core, T, topo):
         LBD, LSD, LSW = A("LD", 0, 16), A("LD", 16, 32), A("LD", 32, 48)
         neighbours(1, DIFF)
         fights(1)
-        if EARLY == 2:
-            for hh in range(2):
-                if ON_SCALAR["R%d" % hh]:
-                    residents(hh, DIFF)
-            outermost()
+        for hh in (1, 0):
+            if (ON_SCALAR["R%d" % hh] and (hh >= FIRST or EARLY == 2) and not (hh and MIDDLE)) or (LATE and not ON_SCALAR["R%d" % hh]):
+                residents(hh, DIFF)
+        outermost()
         for c in (64, 0, 16, 32, 48):
             tt(A("TS", c, c + 16), A("DD", c, c + 16), A("WN"), OP.mult)
         tt(A("SELT", 64, 80), A("TS", 64, 80), A("KK", 16, 32), OP.add)
@@ -499,9 +504,8 @@ def rank_program(g, core, T, topo):
         for h in range(2):
             mm(half("P0", h), A("SEL", 128 * h, 128 * h + 128, 1, 112), A("ER%d" % t, 0, 128, 1, 112), False, h == 1)
         for h in range(2):
-            tt(half("P0", h, 256), half("MI", h), half("P0", h), OP.max)
-            tt(half("ERV", h), half("ERW", h), half("P5", h), OP.add)
-            tt(half("M2", h), half("ERV", h), half("P0", h, 256), OP.max)
+            tt(half("P0", h, 256), half("PW", h), half("P0", h), OP.max)
+            tt(half("M2", h), half("ERW", h), half("P0", h, 256), OP.max)
             ts(half("MI", h), half("M2", h), 4095, OP.bitwise_and)
             x = cp(half("PW" if last else "ML", h), half("MI", h))
             if not last:
@@ -552,7 +556,7 @@ def rank_program(g, core, T, topo):
     if START:
         urgent = [-START * i for i in range(len(nodes))]
     for _ in range(0 if ORDER else TURNS):
-        order, ends = schedule(0, [u + (1e6 if i < setup else 0) for i, u in enumerate(urgent)])
+        order, ends = schedule(0, [u + (5000 if i < setup else 0) for i, u in enumerate(urgent)])
         if not ORDER or max(ends) < ORDER[0]:
             ORDER[:] = [max(ends), [x["i"] for x in order]]
         urgent = schedule(1, ends)[1]

from concourse.mybir import AluOpType as OP, ActivationFunctionType as AF

S, L, RO, WEAR = 4096, 256, 3, 8
BIG = float(2 ** 26)
M64 = 1.5 * 2 ** 29
B, F, I, U, H = "bfloat16", "float32", "int32", "uint16", "float16"
SCRATCH = {}
for _d, _l in ((B, "XW:4352 OWN:4352 GR:4096 GI:4096 GN:4096 S1:8192 S2:8192 MXA:4096 MXB:4096 MXC:4096 CR:256 CI:256 CB:256 ONE:256 IDB:128 IDN:128 "
                   "IDH:128 IDS:256 BO:128 R0:128 R0B:128 MHALF:128 DGA:256 SM1:1024 SM2:1024 WB:32 WX:72 WG:72 WD:72 NR:128 MID:112 E0:128 "
                   "JC:512 NC:128 CZ:256 KW:128 SEL:768 AT:272 LM:2048 HIM:256 HIN:256 TP:128 TM:256 RP:128 B0:256 B1:256 SCM:256 SC:256 LT:256 "
                   "EQ:3200 NF8:16 LO8:16 WF:16 NT:768 CC:48 ER0:128 ER1:128 ER2:128 FAM:512 XU:256"),
               (H, "ID16:128 LJ:512 THB:128 MSM:256 MSN:256 SL16:16"),
               (F, "IDF:128 KC:1 TB:1 COL:16 CM:256 SMF:256 SMX:256 R16:16 ALD:48 KSC:512 KSO:512 KSR:256 "
                   "EI:1024 EK:1024 RT:128 RM:256 RR:128 RK:32 KK:32 CUM:288 WN:16 DD:80 TS:80 SELT:112 LF:48 ERV:256 ERW:512 PW:256"),
               (I, "NBW:4096 MI:256 THC:1 TE:1 WI:1 WJ:1 NI:256 M2:256"),
               (U, "ML:256 LI0:256 LI1:256 LI2:256 LS:16 LB:16 NL:256 LD:48")):
    for _e in _l.split():
        SCRATCH[_e.split(":")[0]] = ("sbuf", [128, int(_e.split(":")[1])], _d)
PSUM = ["P%d" % i for i in range(8)]
for _p in PSUM:
    SCRATCH[_p] = ("psum", [128, 512], F)
SEMAPHORES = (["q_v", "q_s", "q_t", "q_g"] + ["d_" + n for n in ("x", "m", "o", "nb", "th", "ow", "ym", "yo")]
              + [n + str(t) for n in ("ae", "se") for t in range(RO)] + ["%s%d%d" % (n, t, h) for n in ("al", "sl") for t in range(RO) for h in range(2)])
ON_SCALAR = {"R0": 4, "R1": 4, "N0": 4, "N1": 0, "I0": 0, "I1": 0}
WAKE, HOP, ISSUE = 200, 2200, 600
TURNS, HURRY, EARLY, LATE = 3, 20, 0, False
MERGED, SPLIT = False, False
GATHER = 1.35
ON_VECTOR = [("GR", 1)]
DIFF = ("P6", "P3")
B1S = False
LOOSE = True
WHOLE = []
MIDDLE = False
FIRST = 1
PRE = False
START = 0
ORDER = []


def rank_program(g, core, T, topo):
    rank = T.rank_of(core)
    if rank is None:
        return
    N = len(T.cores)
    Q = {"v": g.vector, "s": g.scalar, "t": g.tensor, "g": g, "y": g.sync}
    nodes = []
    acc, bank, sent = {}, {}, []

    def A(name, c0=0, c1=None, st=1, p=None):
        t = T[name]
        c1 = t.shape[1] if c1 is None else c1
        ps = slice(None) if p is None else slice(0, p)
        return (t[ps, slice(c0, c1) if st == 1 else slice(c0, c1, st)], [(name, c0, c1)], (c1 - c0 + st - 1) // st,
                st == 1 and SCRATCH[name][2] in (B, H, U), name in PSUM)

    def half(name, h, o=0):
        return A(name, o + 128 * h, o + 128 * h + 128)

    def mem(name, h, k):
        return A(name, 2048 * h + k, 2048 * (h + 1), 16)

    def IND(win, off):
        return (win[0].indirect(off[0]), win[1] + off[1], 16 * off[2], False, False)

    def ext(t):
        return (t, [], 0, False, False)

    def val(s):
        return s[0] if isinstance(s, tuple) else s

    def node(q, call, writes, reads, ns, sem=None, n=1, hold=None, after=()):
        me = {"q": q, "call": call, "ns": ns, "hold": ns if hold is None else hold, "sem": sem or "q_" + q, "n": n,
              "dep": set(), "ord": set(after), "i": len(nodes)}
        for regs, wr in ((reads, False), (writes, True)):
            for (b, c0, c1) in regs:
                if b in PSUM:
                    e = bank.setdefault(b, [q, [], []])
                    if e[0] != q:
                        e[:] = [q, [], e[1]]
                        acc[b] = []
                    me["dep"].update(e[2])
                    if q == "t":
                        me["ord"].update(e[1][-1:])
                    e[1].append(me["i"])
                    if q == "t":
                        continue
                for (i, aw, a0, a1) in acc.get(b, []):
                    if (aw or wr) and a1 > c0 and a0 < c1 and i != me["i"]:
                        me["ord" if wr and LOOSE and q in "vs" and nodes[i]["sem"] == "q_" + q and sem is None else "dep"].add(i)
        for regs, wr in ((writes, True), (reads, False)):
            for (b, c0, c1) in regs:
                l = acc.setdefault(b, [])
                if wr:
                    l[:] = [x for x in l if not (x[2] >= c0 and x[3] <= c1)]
                l.append((me["i"], wr, c0, c1))
        me["dep"].discard(me["i"])
        me["ord"].discard(me["i"])
        nodes.append(me)
        return me["i"]

    def vec(call, out, full, cols, rate=None):
        ins = full + [c for c in cols if isinstance(c, tuple)]
        n = full[0][2] if full else out[2]
        if len(out[1]) > 1:
            ns = 50 + 3.2 * n
        elif full and len(full[0][1]) > 1:
            ns = 50 + GATHER * n
        else:
            ns = 0.83 * max(64, n * (rate or (0.5 if all(x[3] for x in full + [out]) else 1)))
        return node("v", call, out[1][:1], [r for x in ins for r in x[1]] + out[1][1:], ns)

    def cp(out, i):
        return vec(lambda: g.vector.tensor_copy(out[0], i[0]), out, [i], [])

    def tt(out, a, b, op):
        return vec(lambda: g.vector.tensor_tensor(out[0], a[0], b[0], op), out, [a, b], [], 1 if a[4] or b[4] else 2)

    def ts(out, a, s1, op0, s2=None, op1=None):
        if op1 is None:
            return vec(lambda: g.vector.tensor_scalar(out[0], a[0], val(s1), None, op0), out, [a], [s1])
        return vec(lambda: g.vector.tensor_scalar(out[0], a[0], val(s1), val(s2), op0, op1), out, [a], [s1, s2])

    def scan(out, d0, d1, op0, op1, init=0.0):
        return vec(lambda: g.vector.tensor_tensor_scan(out[0], d0[0], d1[0], init, op0, op1), out, [d0, d1], [])

    def fill(out, c):
        return vec(lambda: g.vector.memset(out[0], c), out, [], [])

    def act(out, i, func, bias=0.0, scale=1.0, after=()):
        return node("s", lambda: g.scalar.activation(out[0], i[0], func, bias=val(bias), scale=scale), out[1],
                    i[1] + (bias[1] if isinstance(bias, tuple) else []), 65 + i[2] * (GATHER if len(i[1]) > 1 else 0.83), after=after)

    def mm(out, l, r, start=False, stop=False):
        return node("t", lambda: g.tensor.matmul(out[0], l[0], r[0], start, stop), out[1], l[1] + r[1], 0.42 * max(min(64, l[2]), r[2]))

    def turn(out, src, mid=True):
        if mid:
            mm(out, A("MID", 0, src[2]), A("ONE", 0, 128), True, False)
        return node("t", lambda: g.tensor.matmul(out[0], src[0], A("IDF")[0], not mid, True), out[1], src[1] + A("IDF")[1], 225)

    def aff(out, i, pat, op, fl, base, cm):
        return node("g", lambda: g.affine_select(out[0], i[0], pat, op, fl, base, cm), out[1], i[1], 170 + 1.66 * out[2])

    def iota(out, pat, cm, base=0):
        return node("g", lambda: g.iota(out[0], pat, base, cm, allow_small_or_imprecise_dtypes=True), out[1], [], 130 + 1.66 * out[2])

    def dma(q, out, i, sem, ns, after=()):
        return node(q, lambda: Q[q].dma_start(out[0], i[0]), out[1], i[1], ns, sem, 16, ISSUE if q == "g" else 60, after)

    def lanes(src, dst):
        return topo.engines(src, dst)[:8]

    def swap(dst, src, land, i, rsem, lsem):
        rid, pid = topo.addr(dst)[:2]
        eng = lanes(core, dst)

        def call():
            g.remote_dma(land[0], i[0], T.sem[rsem], T.sem[lsem], pid, rid, sum(1 << e for e in eng))
        s = node("g", call, [], i[1], HOP, lsem, len(eng), ISSUE)
        sent.append(s)
        node("n", None, land[1], [], HOP + (2500 if rsem == "al01" else 0), rsem, len(lanes(src, core)), 0, [s])

    fill(A("THC"), 0)
    x = dma("y", A("XW", 0, S), ext(T.x0[:]), "d_x", 6000)
    dma("s", A("MI"), ext(T.m0[:]), "d_m", 2200)
    dma("s", A("NI"), ext(T.own0[:]), "d_o", 2400)
    dma("y", A("NBW"), ext(T.nb[:]), "d_nb", 12000, [x])
    cp(A("ML"), A("MI"))
    swap(T.cores[(rank + 1) % N], T.cores[(rank - 1) % N], A("LI0"), A("ML"), "al01", "sl01")
    dma("g", (T.THC[0::16, 0:1], A("THC")[1]), ext(T.th[:]), "d_th", 5000, sent[-1:])
    fill(A("OWN"), 0.0)
    cp(A("B0"), A("NI"))
    dma("y", (T.OWN[0::16, 0:S], A("OWN", 0, S)[1]), A("B0"), "d_ow", 3000)
    fill(A("ONE"), 1.0)
    iota(A("CM"), [[0, 16], [1, 16]], 0)
    iota(A("WI"), [[0, 1]], 1)
    aff(A("IDB"), A("ONE", 0, 128), [[-1, 128]], OP.is_equal, 0.0, 0, 1)
    aff(A("WB"), A("ONE", 0, 32), [[0, 4], [-16, 8]], OP.is_ge, 0.0, 0, 1)
    aff(A("WB"), A("WB"), [[0, 4], [16, 8]], OP.is_ge, 0.0, 15, -1)
    aff(A("BO"), A("ONE", 0, 128), [[-16, 8], [0, 16]], OP.is_ge, 0.0, 0, 1)
    aff(A("BO"), A("BO"), [[16, 8], [0, 16]], OP.is_ge, 0.0, 15, -1)
    iota(A("ALD", 0, 16), [[16, 16]], 0, L)
    iota(A("ALD", 16, 48), [[0, 2], [16, 16]], 0, S)
    for c in range(15):
        if c != 7:
            o = 256 + 256 * c if c < 8 else 2304 + 128 * (c - 8)
            fill(A("EQ", o, o + 16 * (c % 8 + 1)), 0.0)
    fill(A("MHALF"), -0.5)
    ts(A("SM1", 0, 256), A("CM"), 0.0, OP.not_equal)
    ts(A("SM2", 0, 256), A("CM"), 0.0, OP.is_equal, 1024.0, OP.mult)
    for c in (256, 512):
        for n in ("SM1", "SM2"):
            cp(A(n, c, 2 * c), A(n, 0, c))
    ts(A("WJ"), A("WI"), 15, OP.bitwise_and)
    cp(A("KC"), A("WJ"))
    magic = A("COL", 8, 9)
    ts(magic, A("WI"), 80.0, OP.is_ge, 1.5 * 2 ** 40 - M64, OP.mult)
    ts(magic, magic, M64, OP.add)
    ts(A("ALD"), A("ALD"), A("KC"), OP.add)
    ts(A("R16"), A("CM", 0, 16), A("KC"), OP.is_equal)
    for name, w in (("IDH", 0.5), ("ID16", 1.0)):
        ts(A(name), A("IDB"), w, OP.mult)
    for o, w in ((A("IDN"), -1.0), (A("IDF"), 1.0), (half("IDS", 0), -64.0), (half("IDS", 1), 1.0)):
        act(o, A("IDB"), AF.Identity, 0.0, w)
    for c, n, w in ((0, 32, 2048.0), (32, 16, 2048.0), (48, 8, -128.0), (56, 8, 128.0), (64, 8, -128.0)):
        ts(A("WX", c, c + n), A("WB", 0, n), w, OP.mult)
    ts(A("WG"), A("WX"), -0.5, OP.mult)
    ts(A("WD"), A("WX"), 0.5, OP.mult)
    act(A("NC"), A("BO"), AF.Identity, 0.0, -1024.0)
    ts(A("SMF"), A("CM"), 0.0, OP.is_equal, BIG, OP.mult)
    act(A("SMX"), A("SMF"), AF.Identity, 128.0, -1.0)
    ts(A("DGA"), A("CM"), A("KC"), OP.not_equal, -1024.0, OP.mult)
    ts(A("R0"), A("ONE", 0, 128), A("R16", 0, 1), OP.mult)
    ts(A("R0B"), A("BO"), A("R16", 0, 1), OP.mult)
    act(A("NR"), A("R0B"), AF.Identity, 0.0, -1024.0)
    ts(A("E0"), A("ONE", 0, 128), A("IDF", 0, 1), OP.mult)

    def rows(c, *parts):
        o = A("COL", c, c + 1)
        for i, (r, w) in enumerate(parts):
            if i == 0:
                ts(o, A("IDF", r, r + 1), w, OP.mult)
            else:
                ts(o, A("IDF", r, r + 1), w, OP.mult, o, OP.add)
        return o
    k64, k1 = rows(0, (1, 64.0)), A("IDF", 1, 2)
    lo, hi = rows(1, (3, 10304.0)), rows(2, (3, -129.0))
    fill(A("MID", 64, 112), 0.0)
    ts(A("MID", 0, 64), A("E0", 0, 64), -31.5, OP.mult)
    cm = A("CM", 0, 128)
    ts(A("JC", 0, 128), cm, k64, OP.mult, lo, OP.add)
    ts(A("JC", 128, 256), cm, k64, OP.mult, hi, OP.add)
    ts(A("JC", 256, 512), A("CM"), k1, OP.mult)
    tt(A("LJ", 0, 128), A("JC", 0, 128), A("NR"), OP.add)
    cp(A("LJ", 128, 256), A("JC", 128, 256))
    cp(A("LJ", 256, 512), A("LJ", 0, 256))
    fill(A("TP"), 0.0)
    ones = A("COL", 4, 5)
    ts(ones, A("R16", 0, 1), -1.0, OP.mult, 1.0, OP.add)
    act(A("RT"), cm, AF.Square)
    nodes[act(A("ERW", 0, L), A("CM"), AF.Silu, 0.0, 0.0)].update(hold=1600, ns=1600)
    ts(A("CZ", 0, 128), A("RT"), rows(5, (1, -32768.0)), OP.mult, rows(6, (2, 16384.0), (3, 2016.0), (4, 31.5)), OP.add)
    ts(A("CZ", 128, 256), A("ONE", 0, 128), rows(7, (2, 4096.0), (3, 2016.0), (4, 31.5)), OP.mult)
    act(A("KW"), cm, AF.Identity, 0.0, 65536.0)
    ts(A("CC", 0, 16), A("E0", 0, 16), -1.0, OP.mult)
    ts(A("CC", 16, 48), A("E0", 0, 32), 2048.0, OP.mult)
    fill(A("XW", S, S + L), 0.0)
    for c in (0, 144):
        fill(A("CUM", c, c + 16), 0.0)
    cp(A("AT", 256, 264), A("WB", 0, 8))
    ts(A("AT", 264, 272), A("WB", 0, 8), 64.0, OP.mult)
    for r in range(16):
        ts(A("AT", 16 * r, 16 * r + 16), A("AT", 256, 272), A("R16", r, r + 1), OP.mult)
        mm(A(PSUM[r // 4], 128 * (r % 4), 128 * (r % 4) + 128, 1, 16), A("AT", 16 * r, 16 * r + 16), A("IDB"), True, True)
        if r % 4 == 3:
            act(A("LM", 128 * r - 384, 128 * r + 128, 1, 16), A(PSUM[r // 4], 0, 512, 1, 16), AF.Copy)

    def sel(i, row, step, weight=None, src=None):
        o = A("SEL", 128 * i, 128 * i + 128)
        if src:
            aff(o, A(src, 0, 128), [[-step, 8], [0, 16]], OP.is_equal, 0.0, -row, 1)
        else:
            aff(o, o, [[-step, 8], [0, 16]], OP.not_equal, weight, -row, 1)
    for h in range(2):
        sel(4 + h, 8 * h, 1, src="ONE")
        sel(h, 64 + h, 2, src="KW")
        for row, w in ((0, 1.0), (16, 64.0), (80, -32768.0), (96, -32768.0)):
            sel(h, row + h, 2, w)
        sel(2 + h, 32 + h, 2, src="ONE")
        sel(2 + h, 48 + h, 2, 64.0)

    setup = len(nodes)
    chain = []

    def gather(dst, lst, h, parts=None):
        n = 2 if (dst, h) in WHOLE else 1
        for c in parts or range(2 * h, 2 * h + 2, n):
            out, src = A(dst, 1024 * c, 1024 * (c + n)), IND(A("XW", 0, S), A(lst, 64 * c, 64 * (c + n)))
            if (dst, c) in ON_VECTOR:
                cp(out, src)
            else:
                chain[:] = [act(out, src, AF.Copy, after=chain)]

    def centre(out, src, h, slot):
        for c in range(2):
            o, i = 2048 * slot + 1024 * c, A(src, 2048 * h + 1024 * c, 2048 * h + 1024 * c + 1024)
            scan(A("S1", o, o + 1024), A("SM1"), i, OP.mult, OP.max)
            scan(A("S2", o, o + 1024), A("SM2"), i, OP.add, OP.min, BIG)
        p = half("P4", slot)
        mm(p, A("IDH"), A("MHALF"), True, False)
        mm(p, A("IDH"), mem("S1", slot, 15))
        mm(p, A("IDH"), mem("S2", slot, 15), False, True)
        ts(half(out, h), p, float(2 ** 23), OP.add, -float(2 ** 23), OP.add)

    def six(lst, ms, hi_, h):
        ts(half(ms, h), half(lst, h), -2048.0, OP.add)
        ts(half(hi_, h), half(lst, h), 1 / 64, OP.mult, 129 - 31.5 / 64, OP.add)

    def sites(bk, o, ms, hi_, h):
        mm(A(bk, o, o + 128), half(ms, h), A("ID16"))
        mm(A(bk, o, o + 256), half(hi_, h), A("IDS"))

    def far(bk, o, src, h, cen, at, mx, w, n, ns, banks=None, limit=None, gn=None, stop=True):
        def key(k):
            return A(bk, o + k, o + 16 * n, 16)
        nv = 16 - 4 * ns
        if nv:
            if at is not None:
                mm(half("P7", at), A("IDB"), half(cen, h), True, True)
            if limit is not None and not ns:
                mm(A(bk, limit, limit + 128), half(cen, h), A("NC"))
            for k in range(nv):
                if ns:
                    mm(key(k), half(cen, h), A("WG", w, w + n))
                if gn != 0:
                    mm(A(bk, o + k, o + 16 * (gn or n), 16), mem(src, h, k), A("WG", w, w + (gn or n)))
        for b in range(4 - ns, 4):
            d = banks[b % 2]
            for k in range(4):
                mm(half(d, k), A("IDB"), mem(src, h, 4 * b + k), True, False)
                mm(half(d, k), A("IDN"), half(cen, h), False, True)
            act(A(mx, 2048 * h + 512 * b, 2048 * h + 512 * b + 512), A(d), AF.Abs)
        for k in range(16):
            m = half(mx, 16 * h + k)
            if k < nv:
                tt(m, mem(src, h, k), half("P7", h if at is None else at), OP.max)
            mm(key(k), m, A("WX" if k < nv else "WD", w, w + n), False, stop and k == 15)

    def low(out, r, p, m=M64):
        ts(r, p, m, OP.add, m, OP.subtract)
        tt(out, p, r, OP.subtract)

    def residents(h, banks):
        mm(half("P5", h), A("ONE", 0, 128), A("JC", 256, 384), True, False)
        far("P5", 128 * h, "GR", h, "CR", 2 + h, "MXC", 64, 8, ON_SCALAR["R%d" % h], banks)
        scan(half("KSR", h), A("SMF", 0, 128), half("P5", h), OP.add, OP.min, BIG)

    def outermost():
        p = A("P5", 256, 384, 1, 16)
        turn(p, A("KSR", 15, 256, 16), False)
        low(A("RP", 0, 128, 1, 16), A("RR", 0, 128, 1, 16), p)
        for h in range(2):
            mm(half("P5", h), A("SEL", 512 + 128 * h, 640 + 128 * h, 1, 16), A("RP", 0, 128, 1, 16), True, True)
        ts(A("P5", 256, 512), A("P5", 0, 256), A("KC"), OP.not_equal, 8192.0, OP.mult)
        tt(A("PW"), A("MI"), A("P5", 256, 512), OP.add)

    def lists(bk, i0, i1):
        p = A(bk, 16 * i0, 16 * i1)
        mm(p, A("ONE", 0, 128), A("CC", 16 * i0, 16 * i1), True, False)
        for i in range(i0, i1):
            mm(A(bk, 16 * i, 16 * i + 16), A("ID16" if i else "IDB"), A("SL16") if i else A("SC", 15, 256, 16))
        for r in range(16):
            mm(p, A("LM", 128 * r, 128 * r + 128, 1, 8), A("NT", 256 * i0 + r, 256 * i1, 16, 8), False, r == 15)
        tt(A("LF", 16 * i0, 16 * i1), p, A("ALD", 16 * i0, 16 * i1), OP.min)
        cp(A("LD", 16 * i0, 16 * i1), A("LF", 16 * i0, 16 * i1))

    def block(c):
        return 256 + 256 * c if c < 8 else 2304 + 128 * (c - 8) - 128

    for t in range(RO):
        last = t == RO - 1
        host, guest = T.cores[(rank + 1 + t) % N], T.cores[(rank - 1 - t) % N]
        LI = "LI%d" % t
        if t == 0:
            cp(A("TE"), A("THC"))
        else:
            ts(A("WJ"), A("WI"), 63, OP.bitwise_and)
            tt(A("TE"), A("THC"), A("WJ"), OP.add)
        ts(A("TB"), A("TE"), 4081.0, OP.min, -2048.0, OP.add)
        ts(A("THB"), A("R0"), A("TB"), OP.mult, ones, OP.add)
        if t:
            nodes[iota(A("ERW", 0, L), [[0, L]], 0)]["ord"].update(sent[-1:])
        def own(h):
            gather("GR", "ML", h, ((0, 1, 2), (3,))[h] if PRE else None)
            centre("CR", "GR", h, 3 * h)
            if not ON_SCALAR["R%d" % h] and not LATE:
                residents(h, None)
        for h in range(FIRST):
            own(h)
        for h in range(2):
            bk = PSUM[h]
            gather("GI", LI, h)
            centre("CI", "GI", h, 1 + h)
            six(LI, "MSM", "HIM", h)
            mm(A(bk), A("ONE", 0, 128), A("JC"), True, False)
            sites(bk, 0, "MSM", "HIM", h)
            far(bk, 0, "GI", h, "CI", h, "MXA", 32, 32, ON_SCALAR["I%d" % h], DIFF)
            if ON_SCALAR["I%d" % h] == 4:
                mm(half("P7", h), A("IDB"), half("CI", h), True, True)
            scan(A("KSC", 256 * h, 256 * h + 256), A("SMF", 0, 256), A(bk, 0, 256), OP.add, OP.min, BIG)
            p = A("P2", 0, 128, 1, 16)
            turn(p, A("KSC", 256 * h + 15, 256 * h + 256, 16))
            low(A("TM", 128 * h, 128 * h + 128, 1, 16), A("RM", 128 * h, 128 * h + 128, 1, 16), p)
            p = A("P2", 128, 136)
            for r in range(16):
                mm(p, A("LM", 128 * r, 128 * r + 128, 1, 16), A("TM", 128 * h + r, 128 * h + 128, 16, 16), r == 0, r == 15)
            ts(A("LS", 8 * h, 8 * h + 8), p, 2047.5, OP.add)
            ts(A("SL16", 8 * h, 8 * h + 8), p, -0.5, OP.add)
            cp(half("NL", h), IND(A("NBW"), A("LS", 8 * h, 8 * h + 8)))
            scan(A("KSO", 256 * h, 256 * h + 256), A("SMF", 0, 256), A(bk, 256, 512), OP.add, OP.min, BIG)
            low(A("KK", h, 32, 2), A("RK", 16 * h, 16 * h + 16), A("KSO", 256 * h + 15, 256 * h + 256, 16))
            for hh in range(FIRST):
                if h == EARLY and ON_SCALAR["R%d" % hh]:
                    residents(hh, DIFF)
        for h in range(FIRST, 2):
            own(h)

        tt(A("DD", 64, 80), A("KK", 0, 16), A("KK", 16, 32), OP.subtract)
        act(A("B0"), IND(A("OWN", 0, S), A("LS")), AF.Identity, 1.0)
        mm(A("P4", 0, 256), A("R0B"), A("B0"), True, True)
        tt(A("SCM"), A("P4", 0, 256), A("DGA"), OP.add)
        scan(A("SC"), A("SM1", 0, 256), A("SCM"), OP.mult, OP.max)
        ts(A("LB"), A("SC", 15, 256, 16), -1.0, OP.add)
        tt(A("EQ", 0, 256), A("SC"), A("P4", 0, 256), OP.is_equal)
        if B1S:
            act(A("B1"), A("P4", 0, 256), AF.Copy)
        else:
            cp(A("B1"), A("P4", 0, 256))
        act(A("CB"), IND(A("CR"), A("LB")), AF.Copy)
        ts(A("LT"), A("B1"), 256.0, OP.is_lt)

        def neighbours(h, banks):
            gather("GN", "NL", h)
            six("NL", "MSN", "HIN", h)
            ns = ON_SCALAR["N%d" % h]
            bk = PSUM[h]
            mm(A(bk), A("THB"), A("LJ"), True, False)
            sites(bk, 0, "MSN", "HIN", h)
            sites(bk, 256, "MSN", "HIN", h)
            far(bk, 0, "GN", h, "CI", None, "MXA", 0, 16, 0, None, 0, 16 if ns else 32, False)
            far(bk, 256, "GN", h, "CB", 2 + h, "MXB", 0, 16, ns, banks, 256, None if ns else 0)

        def fights(h):
            bi = br = PSUM[h]
            c = 144 * h
            for bk, o in ((bi, 0), (br, 256)):
                act(half("FAM", h, o), A(bk, o, o + 128), AF.Sign, 2.0 ** 21 - 0.5, -1.0)
            for bk, o, out in ((bi, 0, "EI"), (br, 256, "EK")):
                scan(A(out, 512 * h + o, 512 * h + o + 256), A("SMF"), A(bk, o, o + 256), OP.add, OP.min, BIG)
                scan(A(out, 512 * h + 256 - o, 512 * h + 512 - o), A("SMX"), A(bk, o, o + 256), OP.add, OP.max)
            scan(A("CUM", c + 16, c + 144), half("FAM", h), half("FAM", h, 256), OP.add, OP.subtract)
            tt(A("WN", h, 16, 2), A("CUM", c + 31, c + 144, 16), A("CUM", c + 15, c + 128, 16), OP.is_gt)
            tt(A("DD", h, 64, 2), A("EI", 512 * h + 15, 512 * h + 512, 16), A("EK", 512 * h + 15, 512 * h + 512, 16), OP.subtract)
        neighbours(0, DIFF)
        if MIDDLE:
            residents(1, DIFF)
        fights(0)
        for c in range(15):
            ts(A("EQ", block(c) + 16 * c + 16, block(c) + 256), A("B1", 16 * c + 16, 256), A("SC", 16 * c + 15, 16 * c + 16), OP.is_equal)
        for h in range(2):
            src = [0] + [block(c) for c in range(7 + 8 * h)]
            for o in src:
                mm(A("P4", 256 + h, 272, 2), half("EQ", h, o), A("WB", 0, 8), o == 0, o == src[-1])
        ts(A("SELT", 96, 112), A("P4", 256, 272), 1.5, OP.is_gt)
        ts(A("NF8"), A("P4", 256, 272), 1.5, OP.is_gt, 8192.0, OP.mult)
        for i in range(4):
            mm(A("P4", 128 * i, 128 * i + 128, 1, 8), A("NF8", i % 2, 16, 2), A("IDB"), True, True)
        act(A("NT", 0, 512, 1, 8), A("P4", 0, 512, 1, 8), AF.Copy)
        if not MERGED:
            lists("P4", 0, 2)
        LBD, LSD, LSW = A("LD", 0, 16), A("LD", 16, 32), A("LD", 32, 48)
        neighbours(1, DIFF)
        fights(1)
        for hh in (1, 0):
            if (ON_SCALAR["R%d" % hh] and (hh >= FIRST or EARLY == 2) and not (hh and MIDDLE)) or (LATE and not ON_SCALAR["R%d" % hh]):
                residents(hh, DIFF)
        outermost()
        for c in (64, 0, 16, 32, 48):
            tt(A("TS", c, c + 16), A("DD", c, c + 16), A("WN"), OP.mult)
        tt(A("SELT", 64, 80), A("TS", 64, 80), A("KK", 16, 32), OP.add)
        tt(A("SELT", 80, 96), A("SELT", 64, 80), A("SELT", 64, 80), OP.mult)
        for h in range(2):
            tt(A("SELT", h, 64, 2), A("TS", h, 64, 2), A("EK", 512 * h + 15, 512 * h + 512, 16), OP.add)
        p = A("P4", 0, 128, 1, 112)
        turn(p, A("SELT"))
        low(A("TP", 0, 128, 1, 112), A("RT", 0, 128, 1, 112), p, A("COL", 8, 9, 1, 112))
        swap(guest, host, A("ER%d" % t), A("TP"), "ae%d" % t, "se%d" % t)
        ts(A("LO8"), A("WN"), -8192.0, OP.mult, 8192.0, OP.add)
        for h in range(2):
            o = A("P1", 128 * h, 128 * h + 128, 1, 8)
            mm(o, A("NF8", h, 16, 2), A("IDB"), True, False)
            mm(o, A("LO8", h, 16, 2), A("IDB"), False, True)
        act(A("NT", 512, 768, 1, 8), A("P1", 0, 256, 1, 8), AF.Copy)
        lists("P1", 0 if MERGED else 2, 3)
        if not last:
            act(A("XU"), IND(A("XW"), LSD), AF.Relu, -float(WEAR))
            cp(IND(A("XW"), LSD), A("XU"))
        mm(A("P2", 256, 512), A("CZ", 128, 256), A("ONE"), True, False)
        for h in range(2):
            mm(half("P2", h, 256), A("SEL", 256 + 128 * h, 384 + 128 * h, 1, 112), A("TP", 0, 128, 1, 112), False, h == 1)
        act(A("ERV"), A("P2", 256, 512), AF.Copy)
        o = IND(A("ERW"), LBD)
        node("s", lambda o=o: g.scalar.activation(o[0], A("ERV")[0], AF.Silu), o[1][:1], o[1][1:] + A("ERV")[1], 870)
        owners = tt(IND(A("OWN"), LSW), A("B1"), A("LT"), OP.mult)
        if last:
            dma("g", ext(T.yown[:]), (T.OWN[0::16, 0:S], A("OWN", 0, S)[1]), "d_yo", 2500)
        else:
            tt(A("WF"), A("WN"), A("SELT", 96, 112), OP.is_gt)
            mm(A("P2", 0, 16), A("ONE", 0, 128), A("WF"), True, True)
            scan(A("RK", 0, 16), A("ONE", 0, 16), A("P2", 0, 16), OP.mult, OP.add)
            cp(A("WI"), A("RK", 15, 16))
        mm(A("P0", 0, 256), A("CZ", 0, 128), A("ONE"), True, False)
        for h in range(2):
            mm(half("P0", h), A("SEL", 128 * h, 128 * h + 128, 1, 112), A("ER%d" % t, 0, 128, 1, 112), False, h == 1)
        for h in range(2):
            tt(half("P0", h, 256), half("PW", h), half("P0", h), OP.max)
            tt(half("M2", h), half("ERW", h), half("P0", h, 256), OP.max)
            ts(half("MI", h), half("M2", h), 4095, OP.bitwise_and)
            x = cp(half("PW" if last else "ML", h), half("MI", h))
            if not last:
                nodes[owners]["ord"].add(x)
            if not last and (SPLIT or h):
                c = 128 * h if SPLIT else 0
                n = "%d%d" % (t + 1, h)
                swap(T.cores[(rank + 2 + t) % N], T.cores[(rank - 2 - t) % N], A("LI%d" % (t + 1), c, 128 * h + 128), A("ML", c, 128 * h + 128), "al" + n, "sl" + n)
        if last:
            dma("y", ext(T.ym[:]), A("PW"), "d_ym", 2200)

    link = [[[] for _ in nodes], [[] for _ in nodes]]
    for x in nodes:
        for d in x["dep"] | x["ord"]:
            waits = d in x["dep"]
            link[0][d].append((x["i"], nodes[d]["ns"] + WAKE if waits else 0))
            link[1][x["i"]].append((d, x["hold"] + nodes[d]["ns"] - nodes[d]["hold"] + WAKE if waits else 0))

    def schedule(way, urgent):
        left = [len(l) for l in link[1 - way]]
        ready = [0.0 if way == 0 else x["ns"] - x["hold"] for x in nodes]
        free = {q: 0.0 for q in "vstgyn"}
        cand = {q: [x["i"] for x in nodes if x["q"] == q and not left[x["i"]]] for q in free}
        order, ends = [], [0.0] * len(nodes)
        while len(order) < len(nodes):
            best = None
            for q, l in cand.items():
                if l:
                    i = max(l, key=lambda y: urgent[y] - HURRY * max(0.0, ready[y] - free[q]))
                    if ready[i] > free[q]:
                        fit = [y for y in l if max(ready[y], free[q]) + nodes[y]["hold"] <= ready[i] + 20]
                        i = max(fit, key=lambda y: urgent[y]) if fit else i
                    if best is None or max(ready[i], free[q]) < best[0]:
                        best = (max(ready[i], free[q]), i, q)
            start, i, q = best
            free[q] = ends[i] = start + nodes[i]["hold"]
            cand[q].remove(i)
            order.append(nodes[i])
            for j, ns in link[way][i]:
                ready[j] = max(ready[j], start + ns)
                left[j] -= 1
                if not left[j]:
                    cand[nodes[j]["q"]].append(j)
        return order, ends
    urgent = [0.0] * len(nodes)
    for x in reversed(nodes):
        urgent[x["i"]] = max([x["ns"]] + [urgent[j] + (ns or (x["hold"] if x["q"] != "g" else 0)) for j, ns in link[0][x["i"]]])
    if START:
        urgent = [-START * i for i in range(len(nodes))]
    for _ in range(0 if ORDER else TURNS):
        order, ends = schedule(0, [u + (5000 if i < setup else 0) for i, u in enumerate(urgent)])
        if not ORDER or max(ends) < ORDER[0]:
            ORDER[:] = [max(ends), [x["i"] for x in order]]
        urgent = schedule(1, ends)[1]
    order = [nodes[i] for i in ORDER[1]]

    done = {n: 0 for n in SEMAPHORES}
    know = {q: {} for q in "vstgyn"}

    def wait(q, x):
        if know[q].get(x["sem"], 0) < x["val"]:
            Q[q].wait_ge(T.sem[x["sem"]], x["val"])
            for k, v in list(x["knew"].items()) + [(x["sem"], x["val"])]:
                know[q][k] = max(know[q].get(k, 0), v)
    for at, x in enumerate(order):
        q = x["q"]
        for d in sorted((nodes[d] for d in x["dep"]), key=lambda y: -y["at"]):
            wait(q, d)
        done[x["sem"]] += x["n"]
        x["at"], x["val"], x["knew"] = at, done[x["sem"]], dict(know[q])
        if q != "n":
            ins = x["call"]()
            if ins is not None:
                ins.then_inc(T.sem[x["sem"]], x["n"])
    for s in SEMAPHORES:
        if done[s]:
            wait("g", {"sem": s, "val": done[s], "knew": {}})
